import numpy as np, ml_dtypes
CORES = [35,38,43,46]
N = 4
BF = ml_dtypes.bfloat16
W, L, RO, SH = 4096, 256, 8, (1,)
KK = np.arange(16, dtype=np.int32).reshape(1, 1, 16, 1)
REC = np.array([0.3, 0.0, 1.0, 0.5, 1.0, 0.3, 1.0, 1.0]).reshape(1, 8, 1, 1)
def spans(rng, kind):
    p = np.argsort(rng.random((N, 8, 16, L)), axis=2).astype(np.float64); x = rng.random((N, 8, 16, L)); t = rng.random((N, 8, 16, L))
    s = np.exp2(-rng.integers(0, 6, (N, 8, 1, L)).astype(np.float64))
    c = np.where((kind == 1) | (kind == 3), p, x)
    dur = np.where(kind == 1, 0.5, np.where(kind == 2, 1.0 + t, np.where(kind == 3, 31.0 - 2.0 * p, t * s)))
    pos = np.argsort(np.argsort(np.concatenate([c, c + dur], axis=2), axis=2, kind="stable"), axis=2)
    return pos[:, :, :16], pos[:, :, 16:]
def kinds(rng):
    return rng.choice(np.array([0, 0, 0, 0, 1, 2, 3]), (N, 8, 1, L))
def parts(rng):
    xt = np.floor(rng.random((N, 8, 16, W)) * rng.choice(np.array([12, 24, 40, 64]), (N, 8, 1, W))).astype(np.int64)
    vt = rng.integers(0, 64, (N, 8, 16, W))
    z0 = np.floor(rng.random((N, 8, 16, L)) * rng.choice(np.array([16, 32, 64]), (N, 8, 1, L))).astype(np.int64)
    nm = rng.integers(0, 4096, (N, 8, 16, L)); wt = rng.integers(0, 4096, (N, 8, 16))
    th = rng.integers(150, 330, (N, 8, 1)) + rng.integers(-60, 61, (N, 8, 16))
    th[np.arange(N), rng.integers(0, 8, N)] = rng.integers(0, 30, (N, 16))
    return xt, vt, z0, nm, wt, th
def aim(c):
    return (c - 37 * KK) & 4095
def few(a):
    return np.ascontiguousarray(np.reshape(a, (N, 128, -1))).astype(np.float32).astype(BF)
def big(a):
    return np.ascontiguousarray(np.reshape(a, (N, 128, -1))).astype(np.int32)
def pack(xt, vt, z0, nm, ca, rt, wt, th):
    return {"xt": few(xt), "vt": few(vt), "z0": few(z0), "nm": big(nm), "ca": few(ca), "rt": few(rt), "wt": big(wt), "th": big(th)}
def setup_inputs(rng):
    xt, vt, z0, nm, wt, th = parts(rng); ca, rt = spans(rng, kinds(rng))
    return pack(xt, vt, z0, nm, ca, rt, wt, th)
def uneven(rng, bits, *shape):
    return np.minimum(np.floor(np.exp2(bits * rng.random(shape))), 2 ** bits).astype(np.int64) - 1
def sized(rng, n):
    a = np.minimum(np.floor(np.exp2(6.0 * rng.random((N, 8, 1, n))) * rng.random((N, 8, 16, n))), 63).astype(np.int64)
    return np.where(rng.random((N, 8, 1, n)) < 0.5, a, 63 - a)
def setup_inputs_spread(rng):
    ca, rt = spans(rng, kinds(rng))
    return pack(sized(rng, W), sized(rng, W), sized(rng, L), uneven(rng, 12, N, 8, 16, L), ca, rt, uneven(rng, 12, N, 8, 16), np.minimum(uneven(rng, 10, N, 8, 16), 1007))
def tips(rng, n):
    return np.where(rng.random((N, 8, 1, n)) < REC, 63 * rng.integers(0, 2, (N, 8, 1, n)), 63 * rng.integers(0, 2, (N, 8, 16, n)))
def setup_inputs_ends(rng):
    xt, vt, z0 = tips(rng, W), tips(rng, W), tips(rng, L)
    nm = 4095 * rng.integers(0, 2, (N, 8, 16, L)); wt = 4095 * rng.integers(0, 2, (N, 8, 16)); th = 1007 * rng.integers(0, 2, (N, 8, 16))
    th[:, :, 0] = 0; th[:, :, 15] = 1007
    us = np.arange(W); hit = np.flatnonzero((((us * us) >> 5) + 37 * us + 613) & (W - 1) == W - 1)
    one = 65 if len(hit) == 0 else (-65 * int(hit[rng.integers(0, len(hit))])) & 4095
    wt[:, 0] = 4095; wt[:, 6:] = 0; wt[:, 7, 15] = 65; wt[:, 6, 15] = one
    last = np.array([0, 1, 6, L - 2, L - 1])
    z0[:, 0][..., last] = 63; z0[:, 7][..., last] = 63; nm[:, 7][..., last] = 4095
    ca, rt = spans(rng, rng.choice(np.array([1, 2, 3]), (N, 8, 1, L)))
    return pack(xt, vt, z0, nm, ca, rt, wt, th)
def setup_inputs_corners(rng):
    xt, vt, z0, nm, wt, th = parts(rng); H = W // 2
    hi = rng.integers(0, 64, (N, 4, 16, H)) * (rng.random((N, 4, 1, H)) < 0.5); hi[:, :, :8] = 63; hi[:, :, 8] = 0
    lo = np.where(rng.random((N, 4, 1, H)) < 0.5, 63, rng.integers(0, 64, (N, 4, 16, H))); lo[:, :, :9] = 0
    xt[:, :4, :, :H] = hi; xt[:, :4, :, H:] = lo; z0[:, :4] = rng.integers(1, 63, (N, 4, 16, L)); wt[:, :4] = 0; th[:, :4] = 0
    kind = kinds(rng); kind[:, :4] = rng.choice(np.array([1, 2, 2, 3]), (N, 4, 1, L)); kind[:, 4] = 1; kind[:, 5] = 2; kind[:, 6] = 3
    ca, rt = spans(rng, kind)
    many = rng.choice(np.array([0, 1, RO // 2, RO - 2, RO - 1, 16]), (N, 8, 1, L)); many[:, 1] = rng.integers(0, 2, (N, 1, L)); many[:, 2] = RO // 2; many[:, 3] = 16
    many[:, 0, :, L - 1] = RO - 2
    order = np.argsort(np.argsort(ca, axis=2), axis=2)
    c = np.where(order < many, rng.integers(0, H - 32, (N, 8, 16, L)), rng.integers(H, W - 32, (N, 8, 16, L)))
    nm[:, :4] = aim(c)[:, :4]
    wt[:, 4] = 4095 * rng.integers(0, 2, (N, 16)); th[:, 4] = 0; th[:, 7] = np.where(rng.random((N, 16)) < 0.25, 1007, 0)
    return pack(xt, vt, z0, nm, ca, rt, wt, th)
def setup_inputs_crowd(rng):
    xt, vt, z0, nm, wt, th = parts(rng); Q = W // 4
    xt[..., :Q] = rng.integers(40, 64, (N, 8, 16, Q)); xt[..., Q:2 * Q] = rng.integers(24, 33, (N, 8, 16, Q)); xt[..., 2 * Q:] = 0
    z0 = rng.integers(1, 8, (N, 8, 16, L)); wt[:, 0::2] = 0; wt[:, 1::2] = W // 2
    xt[:, 1::2] = (xt[:, 1::2] >> 1) << 1; z0[:, 1::2] = np.maximum((z0[:, 1::2] >> 1) << 1, 2)
    vt[..., 613] = 0; th = rng.integers(0, 300, (N, 8, 16))
    ca, rt = spans(rng, kinds(rng)); first = ca == np.min(ca, axis=2, keepdims=True)
    low = rng.integers(2 * Q, W - 32, (N, 8, 16, L)); mid = rng.integers(Q, 2 * Q - 32, (N, 8, 16, L))
    c = np.where(first, rng.integers(0, Q - 32, (N, 8, 16, L)), np.where(rng.random((N, 8, 1, L)) < 0.5, mid, low))
    out = np.zeros((N, 8, 1, L), bool); out[1, 7, 0, L - 1] = True
    for q in range(2, N - 1):
        for g in range(1, 8, 2): out[q, g, 0, rng.integers(0, L)] = True
    nm = aim(np.where(out, low, c))
    e = N - 1; cols = np.arange(W)
    xt[e] = rng.integers(0, 64, (8, 16, W)); xt[e, :, 8:] = xt[e, :, 8:] >> 2; vt[e, :, 8:] = vt[e, :, 8:] >> 2
    z0[e, :, :8] = 0; z0[e, :, 8:] = rng.integers(50, 64, (8, 8, L)); th[e] = rng.integers(0, 100, (8, 16))
    wt[e, 0::2] = rng.integers(0, 4096, (4, 16)); nm[e, 0::2] = rng.integers(0, 4096, (4, 16, L))
    wt[e, 1::2] = 0; wt[e, 1::2, 0] = 1; wt[e, 1::2, 1] = 64
    xt[e, 1::2, 0] = cols & 63; xt[e, 1::2, 1] = cols >> 6; xt[e, 1::2, 2] = np.where(cols < 600, 0, rng.integers(1, 64, (4, W)))
    us = np.arange(600, W); us = us[np.unique(((us * us >> 5) + 37 * us) & (W - 1), return_index=True)[1]]
    for g in range(1, 8, 2): nm[e, g] = np.where(first[e, g], aim(np.resize(rng.permutation(us), L))[0, 0], 0)
    return pack(xt, vt, z0, nm, ca, rt, wt, th)
def setup_inputs_twins(rng):
    xt, vt, z0, nm, wt, th = parts(rng); B = W // 128
    b = np.floor(rng.random((1, 8, 16, B)) * rng.choice(np.array([12, 24, 40, 64]), (1, 8, 1, B))).astype(np.int64)
    xt = np.repeat(np.repeat(b, 128, axis=3), N, axis=0)
    a = rng.integers(0, 40, (1, 8, 16, L // 2)); z0 = np.repeat(np.concatenate([a, a], axis=3), N, axis=0)
    a = rng.integers(0, 4096, (1, 8, 16, L // 2)); nm = np.repeat(np.concatenate([a, a], axis=3), N, axis=0)
    wt = np.repeat(wt[:1], N, axis=0); th = rng.integers(0, 4, (N, 8, 16)); ca, rt = spans(rng, kinds(rng))
    return pack(xt, vt, z0, nm, ca, rt, wt, th)
def check_inputs(d):
    bad = []
    for k, lo, hi in (("xt", 0, 63), ("vt", 0, 63), ("z0", 0, 63), ("nm", 0, 4095), ("ca", 0, 30), ("rt", 1, 31), ("wt", 0, 4095), ("th", 0, 1007)):
        a = np.asarray(d[k]).astype(np.float64)
        if not np.all((a >= lo) & (a <= hi)): bad.append("range of " + k)
        elif not np.all(a == np.floor(a)): bad.append("whole numbers in " + k)
    c = np.asarray(d["ca"]).astype(np.float64).reshape(N, 8, 16, L); r = np.asarray(d["rt"]).astype(np.float64).reshape(N, 8, 16, L)
    if not np.all(c < r): bad.append("ca under rt")
    e = np.sort(np.concatenate([c, r], axis=2), axis=2)
    if not np.all(e[:, :, 1:] > e[:, :, :-1]): bad.append("positions of a lane distinct")
    return bad
def ints(a):
    return np.asarray(a).astype(np.float32).astype(np.int32)
def pick(t, ix):
    return np.stack([np.stack([np.take(t[q, g], ix[q, g], axis=1) for g in range(8)]) for q in range(N)])
def mark(x, w):
    return np.sum(x * w, axis=2, dtype=np.int32) & (W - 1)
def place(u, d):
    return ((u * u >> 5) + 37 * u + 613 * d) & (W - 1)
def reference(xt, vt, z0, nm, ca, rt, wt, th):
    X = ints(xt).reshape(N, 8, 16, W); V = ints(vt).reshape(N, 8, 16, W); z = ints(z0).reshape(N, 8, 16, L)
    n = nm.astype(np.int32).reshape(N, 8, 16, L); c = ints(ca).reshape(N, 8, 16, L); r = ints(rt).reshape(N, 8, 16, L)
    w = wt.astype(np.int32).reshape(N, 8, 16, 1); t = th.astype(np.int32).reshape(N, 8, 16, 1)
    lev = np.zeros((N, 8, 16, L), np.int32); dep = np.zeros((N, 8, L), np.int32); ptr = np.full((N, 8, L), -1, np.int32)
    stk = np.zeros((N, 8, 16, RO, L), np.int32); A = np.zeros((N, 1, 1, 1), np.int32); height = np.arange(RO).reshape(1, 1, 1, RO, 1)
    for step in range(RO):
        kap = np.min(np.where(lev > 0, 32, r), axis=2, keepdims=True)
        can = (lev == 0) & (c > ptr[:, :, None]) & (c < kap)
        uz = mark(z, w); zz = z[:, :, :, None]
        y = pick(X, ((n * uz[:, :, None] >> 5) + n + 37 * KK + A) & (W - 1))
        zk = np.abs(zz - y); rows = np.sum(y >= zz, axis=2, dtype=np.int32)
        v = pick(V, place(mark(zk, w[..., None]), dep[:, :, None] + 1))
        far = np.sum(np.abs(v - zk), axis=2, dtype=np.int32)
        key = np.where(can & (rows >= 8) & (far > t), c, 32)
        k = np.argmin(key, axis=2); push = np.min(key, axis=2) < 32; pop = ~push & (dep > 0)
        at = place(uz, dep); wins = {}
        for q in range(N):
            for g in range(8):
                i = np.flatnonzero(pop[q, g]); p, f = np.unique(at[q, g, i], return_index=True)
                wins[q, g] = (p, z[q, g][:, i[f]])
        for d in (0,) + SH:
            for q in range(N):
                for g in range(8):
                    V[(q + d) % N, g][:, wins[q, g][0]] = wins[q, g][1]
        old = np.take_along_axis(stk, np.maximum(dep - 1, 0)[:, :, None, None, :], axis=3)[:, :, :, 0]
        new = np.take_along_axis(zk, k[:, :, None, None, :], axis=3)[:, :, :, 0]
        stk = np.where(push[:, :, None, None, :] & (dep[:, :, None, None, :] == height), zz, stk)
        P, O, D = push[:, :, None], pop[:, :, None], dep[:, :, None]
        top = O & (lev == D)
        ptr = np.where(pop, np.sum(np.where(top, c, 0), axis=2, dtype=np.int32), -1)
        lev = np.where(P & (KK == k[:, :, None]), D + 1, np.where(top, 0, lev))
        z = np.where(P, new, np.where(O, old, 63 - z))
        dep = dep + push.astype(np.int32) - pop.astype(np.int32)
        A = (np.sum(pop, axis=(1, 2)) & 31).reshape(N, 1, 1, 1)
    return {"yv": V.reshape(N, 128, W).astype(np.float32).astype(BF), "yz": z.reshape(N, 128, L).astype(np.float32).astype(BF),
            "yl": lev.reshape(N, 128, L).astype(np.float32).astype(BF), "yp": ptr.astype(np.float32)}

@@ -1,0 +1,589 @@
+from concourse.mybir import AluOpType as Op, AxisListType, ActivationFunctionType as Act
+
+STEPS = 8
+NE = 9
+FL, ZS = 4096, 4352
+LAT, CYC, GAT, WIN = 0.1, 0.00083, 1.56, 0.02
+BIAS = {"x": -3.6, "gx": -3, "ln": -1.4, "sc": -0.9, "pk": -16.5, "bb": -0.1, "row": -12.0, "mv": -0.8, "ab": 4.2, "far": 7.8,
+        "vi": 1.6, "dd": 1.9, "vg": -2.2, "sh": -3.4}
+_B = {
+    "bfloat16": "XT 4128 VT 4352 ZW 6656 D 4096 BB 4096 EE 4096 AB 4096 CMP 4096 ZIN 2048 CAI 256 RTI 256 CAT 256 RTT 256 CAC 256 CAB 256 "
+                "RTB 256 CM 256 G1 256 HIT 256 LEV0 256 LEV1 256 HD 144 RED 2048 BSEL 2048 TRI 2048 ONE 2048 ZER 256 BLK 128 IDN 128 NEG 128 "
+                "I64 128 N64 128 I1K 128 I32 128 PAR 128 NPAR 128 SM 512 UPQ 256 OFFD 256 LEV 256 YLB 256 LB 2048 Z4 1024",
+    "float16": "PR 256 NMF 256 NMT 256 THM 256 WRED 2048 D19 128 LH 64",
+    "uint16": "WIN 128 WO 128 XO 256 HO 256 ZO 32",
+    "int32": "NMI 256 WTI 1 THI 1 NB 256 NK 256 K37 256 T2 256 T3 256 V1 256 UM 256 V3 256 V4 256 V5 256 LI 4096",
+    "float32": "KC 256 TH 256 PK 256 KEY 64 RM 256 KS 256 CS 256 HC 144 DC 144 TS 144 RS9 144 RSA 256 RSM 256 IO3 256 IO4 256 IO5 144 "
+               "LVT 256 YL 256 YP 256 LF 2048",
+}
+SCRATCH = {}
+for _t in _B:
+    _w = _B[_t].split()
+    for _i in range(0, len(_w), 2):
+        SCRATCH[_w[_i]] = ("sbuf", [128, int(_w[_i + 1])], _t)
+for _i in range(8):
+    SCRATCH["pb%d" % _i] = ("psum", [128, 512], "float32")
+LOADS = ["lnm", "lwt", "lca", "lx", "lxw", "lz", "lrt", "lth", "lv"]
+OUTS = ["ov", "oz", "ol", "op"]
+SEMAPHORES = ["sv", "ss", "st", "sg", "loc"] + LOADS + OUTS + ["az%d" % s for s in range(1, STEPS)] + ["aw%d" % s for s in range(1, STEPS)]
+QSEM = {"vector": "sv", "scalar": "ss", "tensor": "st", "gpsimd": "sg"}
+SIZE = {"bfloat16": 2, "float16": 2, "uint16": 2, "float32": 4, "int32": 4}
+
+
+def rank_program(g, core, T, topo):
+    rank = T.rank_of(core)
+    if rank is None:
+        return
+    n = len(T.cores)
+    nxt, prv = T.cores[(rank + 1) % n], T.cores[(rank - 1) % n]
+    ops = []
+    tag = ["init"]
+    slots, used = {}, {"LF": 0, "LI": 0, "LB": 0, "LH": 0}
+
+    def v(name, c0=0, c1=None, st=1):
+        return (name, c0, SCRATCH[name][1][1] if c1 is None else c1, st)
+
+    def ap(x):
+        return T[x[0]][:, x[1]:x[2]] if x[3] == 1 else T[x[0]][:, x[1]:x[2]:x[3]]
+
+    def width(x):
+        return (x[2] - x[1] + x[3] - 1) // x[3]
+
+    def psum(x):
+        return SCRATCH[x[0]][0] == "psum"
+
+    def size(x):
+        return SIZE[SCRATCH[x[0]][2]]
+
+    def sub(x, a, b):
+        return (x[0], x[1] + a, x[1] + b, 1)
+
+    def h16(x):
+        return sub(x, 0, 16)
+
+    def lane(name, buf, w=32):
+        if name not in slots:
+            slots[name] = v(buf, used[buf], used[buf] + w)
+            used[buf] += w
+        return slots[name]
+
+    def add(q, fn, rd, wr, cost, done=None, pre=()):
+        ops.append({"q": q, "fn": fn, "rd": list(rd), "wr": list(wr), "cost": cost, "done": done, "pre": list(pre), "tag": tag[0]})
+
+    def vcost(cyc):
+        return max(64, cyc) * CYC
+
+    def half(a, b):
+        return 0.5 if size(a) == 2 and size(b) == 2 else 1
+
+    def tt(out, a, b, op):
+        add("vector", lambda: [g.vector.tensor_tensor(ap(out), ap(a), ap(b), op)], [a, b], [out],
+            vcost(width(out) * (1 if psum(a) or psum(b) else 2)))
+
+    def ts(out, a, s1, op0, s2=None, op1=None):
+        def val(s):
+            return ap(s) if isinstance(s, tuple) else s
+
+        def fn():
+            if op1 is None:
+                return [g.vector.tensor_scalar(ap(out), ap(a), val(s1), None, op0)]
+            return [g.vector.tensor_scalar(ap(out), ap(a), val(s1), val(s2), op0, op1)]
+        add("vector", fn, [a] + [s for s in (s1, s2) if isinstance(s, tuple)], [out], vcost(width(out) * half(out, a)))
+
+    def cp(out, a):
+        add("vector", lambda: [g.vector.tensor_copy(ap(out), ap(a))], [a], [out], vcost(width(out) * half(out, a)))
+
+    def fill(out, c):
+        add("vector", lambda: [g.vector.memset(ap(out), c)], [], [out], vcost(width(out) * half(out, out)))
+
+    def scan(out, d0, d1, op0, op1):
+        add("vector", lambda: [g.vector.tensor_tensor_scan(ap(out), ap(d0), ap(d1), 0.0, op0, op1)], [d0, d1], [out], vcost(width(out)))
+
+    def turn(out, a):
+        add("vector", lambda: [g.vector.transpose(ap(out), ap(a))], [a], [out], vcost(width(out)))
+
+    def act(out, a, func, scale=1.0, bias=0.0):
+        add("scalar", lambda: [g.scalar.activation(ap(out), ap(a), func, bias=bias, scale=scale)], [a], [out], max(64, width(out)) * CYC)
+
+    def mms(lst):
+        rd, wr, c = [], [], 0
+        for o, l, r, a, b in lst:
+            rd += [l, r]
+            wr.append(o)
+            c += max(64, width(r))
+        add("tensor", lambda: [g.tensor.matmul(ap(o), ap(l), ap(r), a, b) for o, l, r, a, b in lst], rd, wr, c * CYC)
+
+    def iota(out, pattern, base, cm):
+        if SCRATCH[out[0]][2] == "int32":
+            fn = lambda: [g.iota(ap(out), pattern, base, cm)]
+        else:
+            fn = lambda: [g.iota(ap(out), pattern, base, cm, allow_small_or_imprecise_dtypes=True)]
+        add("gpsimd", fn, [], [out], 0.13 + 2 * width(out) * CYC)
+
+    def asel(out, a, pattern, cmp, base, cm):
+        add("gpsimd", lambda: [g.affine_select(ap(out), ap(a), pattern, cmp, 0.0, base, cm)], [a], [out], 0.17 + 2 * width(out) * CYC)
+
+    def dma(q, out, src, rd, wr, sem, cost):
+        eng = g.sync if q == "sync" else g.scalar
+        add(q, lambda: [eng.dma_start(out, src)], rd, wr, cost, done=(sem, 16))
+
+    dma("scalar", T.NMI[:], T.nm[:], [], [v("NMI")], "lnm", 2.5)
+    dma("scalar", T.ZW[:, ZS:ZS + 256], T.z0[:], [], [v("ZW", ZS, ZS + 256)], "lz", 2.5)
+    dma("sync", T.WTI[:], T.wt[:], [], [v("WTI")], "lwt", 2.5)
+    dma("scalar", T.THI[:], T.th[:], [], [v("THI")], "lth", 2.5)
+    dma("sync", T.CAI[:], T.ca[:], [], [v("CAI")], "lca", 2.5)
+    dma("scalar", T.RTI[:], T.rt[:], [], [v("RTI")], "lrt", 2.5)
+    dma("sync", T.XT[:, 0:4096], T.xt[:], [], [v("XT", 0, 4096)], "lx", 8.0)
+    dma("scalar", T.XT[:, 4096:4128], T.xt[:, 0:32], [], [v("XT", 4096, 4128)], "lxw", 3.0)
+    dma("sync", T.VT[:, 0:4096], T.vt[:], [], [v("VT", 0, 4096)], "lv", 12.0)
+
+    one = v("ONE", 0, 128)
+    fill(v("ONE"), 1.0)
+    fill(v("ZER"), 0.0)
+    fill(v("RED"), 0.0)
+    gv, ga, gb, gB = lane("gv", "LF", 8), lane("ga", "LF", 8), lane("gb", "LF", 8), lane("gB", "LF", 8)
+    pI, lI = lane("pI", "LI", 16), lane("lI", "LI", 16)
+    iota(gv, [[-16, 8]], 0, 1)
+    iota(pI, [[0, 16]], 0, 1)
+    iota(lI, [[16, 16]], 0, 0)
+    asel(v("IDN"), one, [[-1, 128]], Op.is_equal, 0, 1)
+    asel(v("UPQ", 0, 128), one, [[-1, 128]], Op.is_equal, -16, 1)
+    asel(v("UPQ", 128, 256), one, [[-1, 128]], Op.is_equal, 16, 1)
+    iota(v("PAR"), [[0, 4], [1, 2], [0, 16]], 0, 0)
+    iota(v("K37"), [[37, 16], [0, 16]], 0, 0)
+    iota(v("IO3"), [[0, 16], [1, 16]], 0, 0)
+    iota(v("IO4"), [[1, 16], [0, 16]], 0, 0)
+    asel(v("BLK"), one, [[-16, 8], [0, 16]], Op.is_ge, 0, 1)
+    asel(v("BLK"), v("BLK"), [[16, 8], [0, 16]], Op.is_ge, 15, -1)
+    iota(v("KC"), [[4096, 16], [0, 16]], 32 * 131072, 0)
+    iota(v("IO5"), [[0, 16], [1, NE]], 0, 0)
+    ts(v("NPAR"), v("PAR"), -1.0, Op.mult, 1.0, Op.add)
+
+    def smx(gp, lhp):
+        return v("SM", 128 * (2 * gp + lhp), 128 * (2 * gp + lhp) + 128)
+    for gp in range(2):
+        for lhp in range(2):
+            src = v("IDN") if gp == lhp else v("UPQ", 0, 128) if lhp == 1 else v("UPQ", 128, 256)
+            tt(smx(gp, lhp), src, v("PAR") if gp else v("NPAR"), Op.mult)
+    ts(ga, gv, 0.0, Op.is_ge)
+    ts(gb, gv, 15.0, Op.is_le)
+    tt(gB, ga, gb, Op.mult)
+    for lp in range(16):
+        cp(v("RED", lp * 128 + lp, lp * 128 + 128, 16), gB)
+    wh, wf = lane("wh", "LF", 1), lane("wf", "LF", 1)
+    ts(wh, v("WTI"), 2048.0, Op.is_ge, -4096.0, Op.mult)
+    tt(wf, wh, v("WTI"), Op.add)
+    ts(v("WRED"), v("RED"), wf, Op.mult)
+    for nm, c in (("NEG", -1.0), ("I64", 64.0), ("N64", -64.0), ("I1K", 1024.0), ("I32", 32.0), ("D19", 19616.0)):
+        ts(v(nm), v("IDN"), c, Op.mult)
+
+    def mat(name, lp):
+        return v(name, lp * 128, lp * 128 + 128)
+    u0, uI, u4 = v("pb1", 256, 272), lane("uI", "LI", 64), lane("u_0", "LI", 64)
+    mms([(u0, mat("WRED", lp), v("ZW", ZS + lp, ZS + 256, 16), lp == 0, lp == 15) for lp in range(16)])
+    for q in range(4):
+        cp(sub(uI, 16 * q, 16 * q + 16), u0)
+    ts(u4, uI, 4095, Op.bitwise_and)
+
+    def conv_k(bank, c0, src):
+        mms([(v(bank, c0 + k * 16 + lhp, c0 + k * 16 + 16, 2), smx(gp, lhp), v(src, gp * 16 + k, 256, 32), gp == 0, gp == 1)
+             for k in range(16) for lhp in range(2) for gp in range(2)])
+    ts(v("NMF"), v("NMI"), -2048.0, Op.add)
+    turn(v("NMT"), v("NMF"))
+    conv_k("pb6", 0, "NMT")
+    ts(v("NB"), v("pb6", 0, 256), 2048.0, Op.add)
+    tt(v("T3"), v("NB"), v("K37"), Op.add)
+    ts(v("T2"), v("T3"), 4095, Op.bitwise_and)
+    ts(v("NK"), v("T2"), 32.0, Op.mult, -131072.0, Op.add)
+    turn(v("CAT"), v("CAI"))
+    turn(v("RTT"), v("RTI"))
+    conv_k("pb0", 256, "CAT")
+    mms([(v("pb0", (2 * b + lhp) * 16, (2 * b + lhp) * 16 + 16), smx(gp, lhp), v("RTT", 32 * b + 16 * gp, 32 * b + 16 * gp + 16), gp == 0, gp == 1)
+         for b in range(8) for lhp in range(2) for gp in range(2)])
+    RTP, CAN = v("pb0", 0, 256), v("pb0", 256, 512)
+    CB = v("pb7", 0, 256)
+    ts(v("CAC"), CAN, -1.0, Op.mult, 32.0, Op.add)
+    ts(v("KS"), CAN, -131072.0, Op.mult)
+    tt(CB, v("KS"), v("KC"), Op.add)
+    cp(v("RTB"), RTP)
+    cp(v("CAB"), CAN)
+    fill(v("LEV0"), 0.0)
+    pm, lc, dmp = lane("pm", "LI", 16), lane("lc", "LI", 16), lane("dmp", "LF", 16)
+    pf, thf = lane("pf", "LF", 1), lane("thf", "LF", 1)
+    ts(pm, pI, 15, Op.bitwise_and)
+    tt(lc, pm, lI, Op.add)
+    ts(dmp, lc, 4096.0, Op.add)
+    cp(pf, sub(pm, 0, 1))
+    cp(thf, v("THI"))
+    ts(v("THM"), v("IO4"), pf, Op.is_equal, thf, Op.mult)
+    mms([(v("pb4", 256, 512), v("BLK"), v("THM"), True, True)])
+    ts(v("TH"), v("pb4", 256, 512), 1024.0, Op.add)
+    ts(v("OFFD"), v("IO3"), pf, Op.not_equal, -1000.0, Op.mult)
+    ts(v("RSM"), v("IO3"), 0.0, Op.is_gt)
+    ts(v("RSA"), v("RSM"), -1001.0, Op.mult, 1000.0, Op.add)
+    ts(v("RS9"), v("IO5"), 0.0, Op.is_gt)
+    wq, si, si2, s63 = lane("wq", "LH", 2), lane("si", "LI", 1), lane("si2", "LI", 1), lane("s63", "LF", 1)
+    cp(sub(wq, 0, 1), wf)
+    mms([(v("pb1", 280, 281), v("BLK"), sub(wq, 0, 1), True, True)])
+    ts(si, v("pb1", 280, 281), 63.0, Op.mult)
+    ts(si2, si, 4095, Op.bitwise_and)
+    cp(s63, si2)
+    asel(v("BSEL"), v("ONE"), [[-1, 16], [-16, 8], [0, 16]], Op.is_equal, 0, 1)
+    asel(v("TRI"), v("ONE"), [[0, 16], [-16, 8], [0, 16]], Op.is_ge, 0, 1)
+    asel(v("TRI"), v("TRI"), [[1, 16], [16, 8], [0, 16]], Op.is_ge, -1, -1)
+    fill(lane("d_0", "LB"), 0.0)
+    fill(lane("ptr_0", "LB"), 0.0)
+    fill(v("HD"), -1.0)
+    fill(v("HD", 0, 144, NE), 0.0)
+    fill(v("HC"), 0.0)
+    A = None
+
+    for s in range(STEPS):
+        par, nxp, last = "_%d" % (s % 2), "_%d" % ((s + 1) % 2), s == STEPS - 1
+
+        def L(name, buf, w=32, par=par):
+            return lane(name + par, buf, w)
+        u, d = L("u", "LI", 64), L("d", "LB")
+        z = v("ZW", ZS + 256 * s, ZS + 256 * s + 256)
+        if s:
+            en = topo.engines(core, nxt)[:8]
+            rid, pid = topo.addr(nxt)[:2]
+
+            def send(dst, src, sem, mask=sum(1 << e for e in en), rid=rid, pid=pid):
+                def fn():
+                    g.remote_dma(out_ap=ap(dst), in_ap=ap(src), remote_sem=T.sem[sem], local_sem=T.sem.loc, pid=pid, routing_id=rid, dma_engine_mask=mask)
+                    return []
+                add("gpsimd", fn, [src], [], 1.0, done=("none", 0))
+            zin, win, wo = v("ZIN", 256 * s, 256 * s + 256), v("WIN", 16 * s, 16 * s + 16), v("WO", 16 * s, 16 * s + 16)
+            send(zin, z, "az%d" % s)
+        tag[0] = "x"
+        for q in range(4):
+            c0, c1 = 64 * q, 64 * q + 64
+            t1, t2, t3, xo = v("pb7", 256 + c0, 256 + c1), v("T2", c0, c1), v("T3", c0, c1), v("XO", c0, c1)
+            tt(t1, v("NB", c0, c1), u, Op.mult)
+            tt(t2, t1, v("NK", c0, c1), Op.add)
+            ts(t3, t2, 5, Op.arith_shift_right, 4095, Op.bitwise_and)
+            if A is None:
+                cp(xo, t3)
+            else:
+                ts(xo, t3, A, Op.add)
+        tag[0] = "sh"
+        d1, d2 = L("d1", "LB", 64), L("d2", "LB")
+        act(sub(d1, 0, 32), d, Act.Identity, bias=1.0)
+        act(sub(d1, 32, 64), d, Act.Identity, bias=1.0)
+        act(d2, d, Act.Identity, scale=2.0, bias=1.0)
+        DR, dr = v("pb2", 0, 256), v("pb2", 256, 400)
+        mms([(sub(DR, 64 * i, 64 * i + 64), v("D19"), d1, True, True) for i in range(4)])
+        fa, fb = L("fa", "LI", 16), L("fb", "LI", 16)
+        ts(fa, h16(u), -1.0, Op.mult, s63, Op.add)
+        ts(fb, fa, 4095, Op.bitwise_and)
+        cp(v("HC", 0, 144, NE), fb)
+        mms([(v("pb2", 256 + e, 400, NE), v("IDN"), h16(d), True, True) for e in range(s + 1 if s else NE)])
+        tt(dr, v("HD"), dr, Op.is_equal)
+        tt(v("DC"), dr, v("HC"), Op.mult)
+        scan(v("TS"), v("RS9"), v("DC"), Op.mult, Op.max)
+        top, ta, tb, tc, tca, pt = L("top", "LI"), L("ta", "LI"), L("tb", "LI"), L("tc", "LI"), L("tca", "LI"), L("pt", "LB")
+        cp(sub(top, 0, 16), v("TS", NE - 1, 144, NE))
+        cp(sub(top, 16, 32), v("TS", NE - 1, 144, NE))
+        ts(ta, top, 4095, Op.bitwise_and)
+        ts(tb, top, 6, Op.arith_shift_right, 0xF000, Op.bitwise_and)
+        tt(tc, ta, tb, Op.add)
+        ts(tca, top, 12, Op.arith_shift_right, 63, Op.bitwise_and)
+        ts(pt, tca, -1.0, Op.mult, 33.0, Op.add)
+        scan(v("KS"), v("RSA"), RTP, Op.max, Op.min)
+        act(v("CM"), CAN, Act.Sign, bias=0.5)
+        kk, kth, kp, dp, alt = L("kk", "LF"), L("kth", "LF"), L("kp", "LF"), L("dp", "LF"), L("alt", "LF")
+        for i in range(2):
+            act(sub(kk, 16 * i, 16 * i + 16), v("KS", 15, 256, 16), Act.Identity, scale=-131072.0, bias=32.0 * 131072 + 65536)
+        act(kth, kk, Act.Identity, bias=65536.0)
+        act(dp, d, Act.Sign)
+        tt(kp, kth, dp, Op.mult)
+        tt(alt, tc, kk, Op.add)
+        act(v("ZW", FL, FL + 256), z, Act.Identity, scale=-1.0, bias=63.0)
+        tag[0] = "pl"
+        if s:
+            pa, pb, pc, pd, pe = L("pa", "LI", 16), L("pb", "LI", 16), L("pc", "LF", 16), L("pd", "LI", 16), L("pe", "LI", 16)
+            ps, ad = L("ps", "LH", 16), L("ad", "LF", 16)
+            ts(pa, h16(u), 1184.0, Op.add)
+            tt(pb, pa, h16(u), Op.mult)
+            act(pc, h16(d), Act.Copy, scale=19616.0)
+            tt(pd, pb, pc, Op.add)
+            ts(pe, pd, 5, Op.arith_shift_right, 4095, Op.bitwise_and)
+            ts(ps, pe, -2048.0, Op.add)
+            tt(ad, pe, dmp, Op.subtract)
+            mms([(v("pb6", lp, 256, 16), mat("BSEL", lp), ps, True, True) for lp in range(16)])
+            cp(v("PR"), v("pb6", 0, 256))
+        for q in range(4):
+            a, b, c0, c1 = 1024 * q, 1024 * q + 1024, 64 * q, 64 * q + 64
+            tag[0] = "gx"
+            if q:
+                def gx4(a=a, b=b, c0=c0, c1=c1):
+                    return [g.vector.tensor_tensor(T.D[:, a:b], T.XT[:, 0:4128].indirect(T.XO[:, c0:c1]), T.Z4[:], Op.subtract)]
+                add("vector", gx4, [v("XT"), v("XO", c0, c1), v("Z4")], [v("D", a, b)], 0.05 + GAT * 1024 * CYC)
+            else:
+                act(v("Z4", 0, 256), z, Act.Copy)
+                act(v("Z4", 256, 512), z, Act.Copy)
+                act(v("Z4", 512, 1024), v("Z4", 0, 512), Act.Copy)
+                for k in range(4):
+                    def gx(k=k, z=z):
+                        return [g.vector.tensor_tensor(T.D[:, 256 * k:256 * k + 256], T.XT[:, 0:4128].indirect(T.XO[:, 16 * k:16 * k + 16]), ap(z), Op.subtract)]
+                    add("vector", gx, [v("XT"), v("XO", 16 * k, 16 * k + 16), z], [v("D", 256 * k, 256 * k + 256)], 0.05 + GAT * 256 * CYC)
+            tag[0] = "ab"
+            act(v("ZW", a, b), v("D", a, b), Act.Abs)
+            tag[0] = "bb"
+            act(v("BB", a, b), v("D", a, b), Act.Sign, bias=0.5)
+            tag[0] = "vi"
+            up, V2 = v("pb1", c0, c1), v("pb7", 256 + c0, 256 + c1)
+            mms([(up, mat("WRED", lp), v("ZW", a + lp, b, 16), lp == 0, lp == 15) for lp in range(16)])
+            V1, UM, V3, V4, V5 = [v(x, c0, c1) for x in ("V1", "UM", "V3", "V4", "V5")]
+            cp(V1, up)
+            ts(UM, V1, 4095, Op.bitwise_and)
+            ts(V2, UM, 1184.0, Op.add)
+            tt(V3, UM, V2, Op.mult)
+            tt(V4, V3, v("pb2", c0, c1), Op.add)
+            ts(V5, V4, 5, Op.arith_shift_right, 4095, Op.bitwise_and)
+            cp(v("HO", c0, c1), V5)
+            tag[0] = "row"
+            if q == 0:
+                mms([(v("pb3", 0, 256), v("ZER", 0, 128), v("ZER"), True, False)])
+            mms([(v("pb3", c0, c1), mat("RED", lp), v("BB", a + lp, b, 16), False, False) for lp in range(16)])
+            if q == 3:
+                mms([(v("pb3", 0, 256), v("I32"), v("CM"), False, True)])
+                act(v("G1"), v("pb3", 0, 256), Act.Sign, bias=-31.5)
+            tag[0] = "pk"
+            tt(v("PK", c0, c1), UM, sub(CB, c0, c1), Op.add)
+        for q in range(4):
+            a, b, c0, c1 = 1024 * q, 1024 * q + 1024, 64 * q, 64 * q + 64
+            tag[0] = "vg"
+
+            def gvt(a=a, b=b, c0=c0, c1=c1):
+                return [g.vector.tensor_tensor(T.EE[:, a:b], T.VT[:, 0:4096].indirect(T.HO[:, c0:c1]), T.ZW[:, a:b], Op.subtract)]
+            add("vector", gvt, [v("VT", 0, 4096), v("HO", c0, c1), v("ZW", a, b)], [v("EE", a, b)], 0.05 + GAT * 1024 * CYC)
+            act(v("AB", a, b), v("EE", a, b), Act.Abs)
+            tag[0] = "far"
+            fp, ff = v("pb4", c0, c1), v("pb7", 256 + c0, 256 + c1)
+            ky = ff if q else v("KEY")
+            mms([(fp, v("I1K"), v("G1", c0, c1), True, False)] +
+                [(fp, mat("RED", lp), v("AB", a + lp, b, 16), False, lp == 15) for lp in range(16)])
+            tt(ff, fp, v("TH", c0, c1), Op.is_gt)
+            tt(ky, ff, v("PK", c0, c1), Op.mult)
+            if q == 0:
+                tt(sub(ky, 0, 32), sub(ky, 0, 32), alt, Op.max)
+                rm = ky
+            else:
+                tt(v("RM", c0, c1), rm, ky, Op.max)
+                rm = v("RM", c0, c1)
+        M1, Wd = L("M1", "LF", 64), L("W", "LI", 64)
+        tt(sub(M1, 0, 32), sub(rm, 0, 32), sub(rm, 32, 64), Op.max)
+        tt(sub(M1, 32, 64), sub(rm, 0, 32), sub(rm, 32, 64), Op.max)
+        tt(sub(Wd, 0, 48), sub(M1, 0, 48), sub(M1, 16, 64), Op.max)
+        tt(sub(Wd, 48, 64), sub(M1, 48, 64), sub(M1, 0, 16), Op.max)
+        W32 = sub(Wd, 0, 32)
+        tag[0] = "mv"
+        if not last:
+            ts(lane("u" + nxp, "LI", 64), Wd, 4095, Op.bitwise_and)
+        za, zb, zo = L("za", "LI", 16), L("zb", "LI", 16), v("ZO", 16 * (s % 2), 16 * (s % 2) + 16)
+        ts(za, h16(Wd), 4, Op.arith_shift_right, 0x1F00, Op.bitwise_and)
+        tt(zb, za, lc, Op.add)
+        cp(zo, zb)
+        zn, zw = v("ZW", ZS + 256 * (s + 1), ZS + 256 * (s + 2)), v("ZW", 0, ZS + 256 * (s + 1))
+
+        def gz(zn=zn, zw=zw, zo=zo):
+            return [g.scalar.activation(ap(zn), ap(zw).indirect(ap(zo)), Act.Copy)]
+        add("scalar", gz, [zw, zo], [zn], 0.065 + GAT * 256 * CYC)
+        if last:
+            dma("scalar", T.yz[:], ap(zn), [zn], [], "oz", 2.5)
+        pop, m = L("pop", "LB"), L("m", "LB")
+        tt(pop, W32, kp, Op.is_lt)
+        if s and not last:
+            cn, ct, am, A = v("pb2", 400, 416), L("ct", "LF", 1), L("am", "LI", 1), L("A", "LF", 1)
+            mms([(cn, one, h16(pop), True, True)])
+            add("vector", lambda ct=ct, cn=cn: [g.vector.tensor_reduce(ap(ct), ap(cn), AxisListType.X, Op.add)], [cn], [ct], 64 * CYC)
+            ts(am, ct, 1.0 / 32, Op.mult, -0.484375, Op.add)
+            ts(A, am, -32.0, Op.mult, ct, Op.add)
+        tag[0] = "ln"
+        tt(m, W32, kth, Op.is_ge)
+        hi, y1, y2, tau, y3, dl = L("hi", "LI"), L("y1", "LF"), L("y2", "LF"), L("tau", "LB"), L("y3", "LB"), L("dl", "LB")
+        tau4, dl4, pn, pn4 = L("tau4", "LB", 64), L("dl4", "LB", 64), lane("ptr" + nxp, "LB"), L("pn4", "LB", 64)
+        ts(hi, W32, 17, Op.arith_shift_right)
+        tt(y1, hi, tca, Op.subtract)
+        tt(y2, y1, m, Op.mult)
+        tt(tau, y2, tca, Op.add)
+        tt(y3, m, d2, Op.mult)
+        tt(dl, y3, d, Op.subtract)
+        for i in range(2):
+            act(sub(tau4, 32 * i, 32 * i + 32), tau, Act.Copy)
+            act(sub(dl4, 32 * i, 32 * i + 32), dl, Act.Copy)
+        mms([(v("pb5", 64 * i, 64 * i + 64), v("IDN"), tau4, True, True) for i in range(4)] +
+            [(v("pb5", 256 + 64 * i, 320 + 64 * i), v("IDN"), dl4, True, True) for i in range(4)])
+        lv = v("LEV%d" % ((s + 1) % 2))
+        tt(v("HIT"), v("CAC"), v("pb5", 0, 256), Op.is_equal)
+        tt(v("pb5", 0, 256), v("HIT"), v("pb5", 256, 512), Op.mult)
+        tt(lv, v("LEV%d" % (s % 2)), v("pb5", 0, 256), Op.add)
+        tt(pn, pop, pt, Op.mult)
+        if not last:
+            act(sub(pn4, 0, 32), pn, Act.Copy)
+            act(sub(pn4, 32, 64), pn, Act.Copy)
+            mms([(RTP, v("IDN"), v("RTB"), True, False)] + [(v("pb0", k, 256, 16), v("I64"), sub(lv, 16 * k, 16 * k + 16), False, k == 15) for k in range(16)])
+            mms([(CAN, v("IDN"), v("CAB"), True, False), (CAN, v("N64"), lv, False, False)] +
+                [(v("pb0", 256 + 64 * i, 320 + 64 * i), v("NEG"), pn4, False, i == 3) for i in range(4)])
+            dx, ca_, cb_ = L("dx", "LB"), L("ca_", "LI", 16), L("cb_", "LI", 16)
+            tt(dx, d, m, Op.add)
+            tt(lane("d" + nxp, "LB"), dx, pop, Op.subtract)
+            tt(v("HD", s + 1, 144, NE), h16(m), h16(d1), Op.mult)
+            ts(ca_, h16(hi), 4096.0, Op.mult, float((s + 1) * 262144), Op.add)
+            tt(cb_, ca_, h16(u), Op.add)
+            tt(v("HC", s + 1, 144, NE), cb_, h16(m), Op.mult)
+        tag[0] = "dd"
+        if s:
+            sx, sc = L("sx", "LF", 16), L("sc", "LF", 16)
+            act(sx, h16(pop), Act.Identity, scale=-9999.0, bias=9999.0)
+            tt(sc, sx, ps, Op.add)
+            for lh in range(16):
+                ts(v("CMP", 272 * lh, 256 * lh + 256), v("PR", 16 * lh, 256), sub(sc, lh, lh + 1), Op.is_equal)
+            mms([(v("pb6", 0, 256), v("IDN"), v("OFFD"), True, False)] +
+                [(v("pb6", 16 * lh + 16, 256), v("BLK"), v("CMP", 272 * lh + 16, 256 * lh + 256), False, False) for lh in range(15)] +
+                [(v("pb6", lp, 256, 16), mat("TRI", lp), v("CMP", lp, 4096, 272), False, lp == 15) for lp in range(16)])
+            scan(v("CS"), v("RSM"), v("pb6", 0, 256), Op.mult, Op.max)
+            nc, wn, wa, wb = L("nc", "LF", 16), L("wn", "LF", 16), L("wa", "LF", 16), L("wb", "LF", 16)
+            ts(nc, v("CS", 15, 256, 16), 0.5, Op.is_lt)
+            tt(wn, nc, h16(pop), Op.mult)
+            tt(wa, wn, ad, Op.mult)
+            tt(wb, wa, dmp, Op.add)
+            cp(wo, wb)
+            send(win, wo, "aw%d" % s)
+            tag[0] = "sc"
+
+            def scat(lst, src):
+                add("vector", lambda: [g.vector.tensor_copy(T.VT[:, 0:4352].indirect(ap(lst)), ap(src))], [lst, src], [v("VT")], 0.05 + 3.8 * 256 * CYC)
+            snd = len(ops) - 1
+            scat(wo, z)
+            ne = len(topo.engines(prv, core)[:8])
+            add("net", None, [], [win, zin], 3.0, [("az%d" % s, ne), ("aw%d" % s, ne)], [snd])
+            scat(win, zin)
+    tag[0] = "out"
+    dma("sync", T.yv[:], T.VT[:, 0:4096], [v("VT")], [], "ov", 8.0)
+    pz = h16(lane("ptr_0", "LB"))
+    add("tensor", lambda: [g.tensor.matmul(T.pb1[0:8, lp:256:16], T.BSEL[:, lp * 128:lp * 128 + 128:16], ap(pz), True, True) for lp in range(16)],
+        [v("BSEL"), pz], [v("pb1", 0, 256)], 1.0)
+    add("vector", lambda: [g.vector.tensor_scalar(T.YP[0:8, :], T.pb1[0:8, 0:256], -1.0, None, Op.add)], [v("pb1", 0, 256)], [v("YP")], 0.22)
+    dma("sync", T.yp[:], T.YP[0:8, :], [v("YP")], [], "op", 2.5)
+    mms([(v("pb0", k, 256, 16), v("IDN"), sub(lv, 16 * k, 16 * k + 16), True, True) for k in range(16)])
+    cp(v("LEV"), RTP)
+    mms([(v("pb3", 32 * b + 16 * gp, 32 * b + 16 * gp + 16), smx(lhp, gp), v("LEV", (2 * b + lhp) * 16, (2 * b + lhp) * 16 + 16), lhp == 0, lhp == 1)
+         for b in range(8) for gp in range(2) for lhp in range(2)])
+    cp(v("LVT"), v("pb3", 0, 256))
+    turn(v("YL"), v("LVT"))
+    cp(v("YLB"), v("YL"))
+    dma("scalar", T.yl[:], T.YLB[:], [v("YLB")], [], "ol", 2.5)
+    queues = {"vector": g.vector, "scalar": g.scalar, "tensor": g.tensor, "gpsimd": g, "sync": g.sync}
+    schedule(g, T, ops, queues)
+    g.wait_ge(T.sem.loc, 2 * (STEPS - 1) * len(topo.engines(core, nxt)[:8]))
+
+
+def schedule(g, T, ops, queues):
+    N = len(ops)
+    preds = [dict() for _ in range(N)]
+    hist = {}
+    for i, o in enumerate(ops):
+        for p in o["pre"]:
+            preds[i][p] = o["q"] != "net"
+        for kind, regs in (("r", o["rd"]), ("w", o["wr"])):
+            for (name, c0, c1, st) in regs:
+                ps = SCRATCH[name][0] == "psum"
+                for (j, k2, b0, b1) in hist.get(name, ()):
+                    if j == i:
+                        continue
+                    same = ops[j]["q"] == o["q"] and not ops[j]["done"]
+                    if b0 < c1 and c0 < b1 and (kind == "w" or k2 == "w"):
+                        need = (not same) or k2 == "w"
+                        if same and o["q"] == "tensor" and ps:
+                            need = False
+                        preds[i][j] = preds[i].get(j, False) or need
+                    elif ps and not same:
+                        preds[i][j] = True
+        for kind, regs in (("r", o["rd"]), ("w", o["wr"])):
+            for (name, c0, c1, st) in regs:
+                h = hist.setdefault(name, [])
+                if kind == "w" and st == 1:
+                    keep = SCRATCH[name][0] == "psum"
+                    h[:] = [x for x in h if not (c0 <= x[2] and x[3] <= c1 and x[0] != i) or (keep and x[0] > i - 600)]
+                h.append((i, kind, c0, c1))
+    succ = [[] for _ in range(N)]
+    for i in range(N):
+        for j in preds[i]:
+            succ[j].append(i)
+    prio = [0.0] * N
+    for i in range(N - 1, -1, -1):
+        prio[i] = ops[i]["cost"] + max([prio[x] + LAT for x in succ[i]] + [0.0])
+    own = [prio[i] + BIAS.get(ops[i]["tag"], 0.0) for i in range(N)]
+    left = [len(p) for p in preds]
+    est, end = [0.0] * N, [0.0] * N
+    free, ready, order, seq = {}, {}, {}, []
+    for i in range(N):
+        if not left[i]:
+            ready.setdefault(ops[i]["q"], []).append(i)
+    for _ in range(N):
+        best = None
+        for q, lst in ready.items():
+            if not lst:
+                continue
+            f = free.get(q, 0.0)
+            t0 = min(max(f, est[i]) for i in lst)
+            i = max((x for x in lst if max(f, est[x]) <= t0 + WIN), key=lambda x: own[x])
+            t = max(f, est[i])
+            if best is None or t < best[0]:
+                best = (t, q, i)
+        t, q, i = best
+        ready[q].remove(i)
+        end[i] = t + ops[i]["cost"]
+        free[q] = t if q == "net" else t + 0.1 if ops[i]["done"] and ops[i]["done"][1] else end[i]
+        order.setdefault(q, []).append(i)
+        seq.append(i)
+        for x in succ[i]:
+            est[x] = max(est[x], t if ops[x]["q"] == q and not preds[x][i] else end[i] + LAT)
+            left[x] -= 1
+            if not left[x]:
+                ready.setdefault(ops[x]["q"], []).append(x)
+    count = {q: 0 for q in QSEM}
+    known, fin = {}, [None] * N
+    for i in seq:
+        o = ops[i]
+        q = o["q"]
+        if q == "net":
+            fin[i] = (list(o["done"]), {})
+            continue
+        kq = known.setdefault(q, {})
+        pj = [j for j, c in preds[i].items() if c]
+        need = {}
+        for j in pj:
+            for sem, val in fin[j][0]:
+                if sem != "none" and kq.get(sem, 0) < val:
+                    need[sem] = max(need.get(sem, 0), val)
+        for j in pj:
+            for sem, val in fin[j][1].items():
+                if sem in need and need[sem] <= val and sem not in [x[0] for x in fin[j][0]]:
+                    del need[sem]
+        for sem, val in sorted(need.items()):
+            queues[q].wait_ge(T.sem[sem], val)
+            kq[sem] = max(kq.get(sem, 0), val)
+        for j in pj:
+            for sem, val in list(fin[j][1].items()) + fin[j][0]:
+                kq[sem] = max(kq.get(sem, 0), val)
+        ins = o["fn"]()
+        if o["done"]:
+            sem, val = o["done"]
+            for x in ins:
+                x.then_inc(T.sem[sem], val)
+            fin[i] = ([(sem, val)], dict(kq))
+        else:
+            for x in ins:
+                x.then_inc(T.sem[QSEM[q]], 1)
+            count[q] += len(ins)
+            fin[i] = ([(QSEM[q], count[q])], dict(kq))
+    for q in QSEM:
+        if count[q]:
+            g.wait_ge(T.sem[QSEM[q]], count[q])
+    for sem in LOADS + OUTS:
+        g.wait_ge(T.sem[sem], 16)
+    return max(end), order, end

@@ -1,26 +1,31 @@
+import math
 from concourse.mybir import AluOpType as Op, AxisListType, ActivationFunctionType as Act
 
 STEPS = 8
-NE = 9
 FL, ZS = 4096, 4352
-LAT, CYC, GAT, WIN = 0.1, 0.00083, 1.56, 0.02
-BIAS = {"x": -3.6, "gx": -3, "ln": -1.4, "sc": -0.9, "pk": -16.5, "bb": -0.1, "row": -12.0, "mv": -0.8, "ab": 4.2, "far": 7.8,
-        "vi": 1.6, "dd": 1.9, "vg": -2.2, "sh": -3.4}
+LAT, CYC, GAT, SCA, WIN = 0.1, 0.001, 1.56, 3.8, 0.02
+PLAN = {"X": "VSVS", "SIGN": "VSVS", "V": "SVVV", "TAIL": (512, 512), "SMALL": "S"}
+ORDER, ROUNDS, HEAT, SEED = {}, 1500, 0.3, 1
+WHEN = dict(x0=0, x1=0.1, x2=2, x3=0.2, gx0=1, gx1=1, gx3=1.1, ab0=2, ab1=3, bb1=3.1, gx2=2.5, ab2=6, ab3=6.1, bb3=6.2, vi0=4, vi1=7, bb0=8.5, bb2=11,
+            row0=9, row1=11.5, pk0=13, pk1=13, vg0=8, vg1=8, vg2=9.5, vg3=10, far0=12, far1=15, sh=12.5, pl=12.6, mv=19, u=19.1, z=19.05, ln=26.5,
+            dd=21.5, sc=24.5, out=40)
 _B = {
-    "bfloat16": "XT 4128 VT 4352 ZW 6656 D 4096 BB 4096 EE 4096 AB 4096 CMP 4096 ZIN 2048 CAI 256 RTI 256 CAT 256 RTT 256 CAC 256 CAB 256 "
-                "RTB 256 CM 256 G1 256 HIT 256 LEV0 256 LEV1 256 HD 144 RED 2048 BSEL 2048 TRI 2048 ONE 2048 ZER 256 BLK 128 IDN 128 NEG 128 "
-                "I64 128 N64 128 I1K 128 I32 128 PAR 128 NPAR 128 SM 512 UPQ 256 OFFD 256 LEV 256 YLB 256 LB 2048 Z4 1024",
-    "float16": "PR 256 NMF 256 NMT 256 THM 256 WRED 2048 D19 128 LH 64",
+    "bfloat16": "XT 4128 VT 4352 ZW 6656 D 4096 BB 4096 EE 4096 AB 4096 ZIN 2048 CAI 256 RTI 256 CAC 256 "
+                "G1 256 FF 256 HIT 256 LEV0 256 LEV1 256 BSEL 2048 TRI 128 ONE 2048 BLK 128 IDN 128 NEG 128 "
+                "I64 128 N64 128 I2K 128 I4K 128 NBG 128 HLF 128 PRM 144 P4K 144 PBG 144 PAR 128 NPAR 128 SM 512 UPQ 256 OFFD 256 YLB 256 LB 1024 L4 256",
+    "float16": "PR 256 NMF 256 NMT 256 SEL 256 THB 128 THC 256 WG 16 FR 256 LH 64",
     "uint16": "WIN 128 WO 128 XO 256 HO 256 ZO 32",
-    "int32": "NMI 256 WTI 1 THI 1 NB 256 NK 256 K37 256 T2 256 T3 256 V1 256 UM 256 V3 256 V4 256 V5 256 LI 4096",
-    "float32": "KC 256 TH 256 PK 256 KEY 64 RM 256 KS 256 CS 256 HC 144 DC 144 TS 144 RS9 144 RSA 256 RSM 256 IO3 256 IO4 256 IO5 144 "
-               "LVT 256 YL 256 YP 256 LF 2048",
+    "int32": "NMI 256 WTI 1 THI 1 K37 256 T1 256 T2 256 T3 256 QQ 256 V4 256 V5 256 WK 144 LI 1024",
+    "float32": "KC 256 KS 256 CS 256 DC 128 TS 128 RS4 64 RS8 128 AL0 144 AL1 144 W0 144 RSA 256 RSM 256 IO3 256 IO4 256 LVT 256 YL 256 YP 256 LF 1024",
 }
 SCRATCH = {}
 for _t in _B:
     _w = _B[_t].split()
     for _i in range(0, len(_w), 2):
         SCRATCH[_w[_i]] = ("sbuf", [128, int(_w[_i + 1])], _t)
+for _n, _a, _b, _t in (("CMP", 16, 256, "bfloat16"), ("CAT", 8, 32, "bfloat16"), ("RTT", 8, 32, "bfloat16"), ("LV3", 16, 16, "bfloat16"), ("HD", 16, 8, "bfloat16"),
+                       ("HC", 16, 8, "float32"), ("CM", 32, 9, "bfloat16"), ("CB", 32, 9, "float16"), ("CAB", 16, 16, "bfloat16"), ("RTB", 16, 16, "bfloat16")):
+    SCRATCH[_n] = ("sbuf", [128, _a, _b], _t)
 for _i in range(8):
     SCRATCH["pb%d" % _i] = ("psum", [128, 512], "float32")
 LOADS = ["lnm", "lwt", "lca", "lx", "lxw", "lz", "lrt", "lth", "lv"]
@@ -37,17 +42,29 @@ def rank_program(g, core, T, topo):
     n = len(T.cores)
     nxt, prv = T.cores[(rank + 1) % n], T.cores[(rank - 1) % n]
     ops = []
-    tag = ["init"]
+    tag = ["init", 0]
     slots, used = {}, {"LF": 0, "LI": 0, "LB": 0, "LH": 0}
 
-    def v(name, c0=0, c1=None, st=1):
-        return (name, c0, SCRATCH[name][1][1] if c1 is None else c1, st)
+    def v(name, c0=0, c1=None, st=1, p=128):
+        sh = SCRATCH[name][1]
+        if len(sh) == 3:
+            return (name, c0, sh[2] if c1 is None else c1, st, (0, sh[1], 1), p)
+        return (name, c0, sh[1] if c1 is None else c1, st, None, p)
+
+    def w(name, a0, a1, c0, c1, sa=1):
+        return (name, c0, c1, 1, (a0, a1, sa), 128)
 
     def ap(x):
-        return T[x[0]][:, x[1]:x[2]] if x[3] == 1 else T[x[0]][:, x[1]:x[2]:x[3]]
+        if x[4] is None:
+            return T[x[0]][0:x[5], x[1]:x[2]:x[3]]
+        if x[2] - x[1] == 1:
+            return T[x[0]][0:x[5], x[4][0]:x[4][1]:x[4][2], x[1]]
+        if x[4][1] - x[4][0] == 1:
+            return T[x[0]][0:x[5], x[4][0], x[1]:x[2]]
+        return T[x[0]][0:x[5], x[4][0]:x[4][1]:x[4][2], x[1]:x[2]]
 
     def width(x):
-        return (x[2] - x[1] + x[3] - 1) // x[3]
+        return (x[2] - x[1] + x[3] - 1) // x[3] * (1 if x[4] is None else (x[4][1] - x[4][0] + x[4][2] - 1) // x[4][2])
 
     def psum(x):
         return SCRATCH[x[0]][0] == "psum"
@@ -56,19 +73,19 @@ def rank_program(g, core, T, topo):
         return SIZE[SCRATCH[x[0]][2]]
 
     def sub(x, a, b):
-        return (x[0], x[1] + a, x[1] + b, 1)
+        return (x[0], x[1] + a, x[1] + b, 1, x[4], x[5])
 
-    def h16(x):
-        return sub(x, 0, 16)
-
-    def lane(name, buf, w=32):
+    def lane(name, buf, wd=16):
         if name not in slots:
-            slots[name] = v(buf, used[buf], used[buf] + w)
-            used[buf] += w
+            slots[name] = v(buf, used[buf], used[buf] + wd)
+            used[buf] += max(wd, 8)
         return slots[name]
 
     def add(q, fn, rd, wr, cost, done=None, pre=()):
-        ops.append({"q": q, "fn": fn, "rd": list(rd), "wr": list(wr), "cost": cost, "done": done, "pre": list(pre), "tag": tag[0]})
+        ops.append({"q": q, "fn": fn, "rd": list(rd), "wr": list(wr), "cost": cost, "done": done, "pre": list(pre), "tag": tag[0], "step": tag[1]})
+
+    def part(name, i):
+        tag[0] = name + str(i)
 
     def vcost(cyc):
         return max(64, cyc) * CYC
@@ -76,14 +93,14 @@ def rank_program(g, core, T, topo):
     def half(a, b):
         return 0.5 if size(a) == 2 and size(b) == 2 else 1
 
+    def val(s):
+        return ap(s) if isinstance(s, tuple) else s
+
     def tt(out, a, b, op):
         add("vector", lambda: [g.vector.tensor_tensor(ap(out), ap(a), ap(b), op)], [a, b], [out],
             vcost(width(out) * (1 if psum(a) or psum(b) else 2)))
 
     def ts(out, a, s1, op0, s2=None, op1=None):
-        def val(s):
-            return ap(s) if isinstance(s, tuple) else s
-
         def fn():
             if op1 is None:
                 return [g.vector.tensor_scalar(ap(out), ap(a), val(s1), None, op0)]
@@ -103,14 +120,21 @@ def rank_program(g, core, T, topo):
         add("vector", lambda: [g.vector.transpose(ap(out), ap(a))], [a], [out], vcost(width(out)))
 
     def act(out, a, func, scale=1.0, bias=0.0):
-        add("scalar", lambda: [g.scalar.activation(ap(out), ap(a), func, bias=bias, scale=scale)], [a], [out], max(64, width(out)) * CYC)
+        add("scalar", lambda: [g.scalar.activation(ap(out), ap(a), func, bias=val(bias), scale=scale)],
+            [a] + ([bias] if isinstance(bias, tuple) else []), [out], max(64, width(out)) * CYC)
+
+    def lin(out, a, scale=1.0, bias=0.0, eng=None):
+        if (eng or PLAN["SMALL"]) == "S":
+            act(out, a, Act.Identity, scale, bias)
+        else:
+            ts(out, a, scale, Op.mult, bias, Op.add)
 
     def mms(lst):
         rd, wr, c = [], [], 0
         for o, l, r, a, b in lst:
             rd += [l, r]
             wr.append(o)
-            c += max(64, width(r))
+            c += max(min(64, width(l)), width(r))
         add("tensor", lambda: [g.tensor.matmul(ap(o), ap(l), ap(r), a, b) for o, l, r, a, b in lst], rd, wr, c * CYC)
 
     def iota(out, pattern, base, cm):
@@ -127,36 +151,42 @@ def rank_program(g, core, T, topo):
         eng = g.sync if q == "sync" else g.scalar
         add(q, lambda: [eng.dma_start(out, src)], rd, wr, cost, done=(sem, 16))
 
+    def gather(eng, out, win, lst, minus=None):
+        if eng == "V":
+            add("vector", lambda: [g.vector.tensor_tensor(ap(out), ap(win).indirect(ap(lst)), ap(minus), Op.subtract)], [win, lst, minus], [out],
+                0.05 + GAT * width(out) * CYC)
+        else:
+            add("scalar", lambda: [g.scalar.activation(ap(out), ap(win).indirect(ap(lst)), Act.Copy)], [win, lst], [out], 0.065 + GAT * width(out) * CYC)
+
     dma("scalar", T.NMI[:], T.nm[:], [], [v("NMI")], "lnm", 2.5)
     dma("scalar", T.ZW[:, ZS:ZS + 256], T.z0[:], [], [v("ZW", ZS, ZS + 256)], "lz", 2.5)
     dma("sync", T.WTI[:], T.wt[:], [], [v("WTI")], "lwt", 2.5)
-    dma("scalar", T.THI[:], T.th[:], [], [v("THI")], "lth", 2.5)
-    dma("sync", T.CAI[:], T.ca[:], [], [v("CAI")], "lca", 2.5)
-    dma("scalar", T.RTI[:], T.rt[:], [], [v("RTI")], "lrt", 2.5)
     dma("sync", T.XT[:, 0:4096], T.xt[:], [], [v("XT", 0, 4096)], "lx", 8.0)
     dma("scalar", T.XT[:, 4096:4128], T.xt[:, 0:32], [], [v("XT", 4096, 4128)], "lxw", 3.0)
+    dma("sync", T.CAI[:], T.ca[:], [], [v("CAI")], "lca", 2.5)
+    dma("scalar", T.RTI[:], T.rt[:], [], [v("RTI")], "lrt", 2.5)
+    dma("scalar", T.THI[:], T.th[:], [], [v("THI")], "lth", 2.5)
     dma("sync", T.VT[:, 0:4096], T.vt[:], [], [v("VT", 0, 4096)], "lv", 12.0)
 
-    one = v("ONE", 0, 128)
+    one, grp = v("ONE", 0, 128), v("BLK", 0, 128, 16)
     fill(v("ONE"), 1.0)
-    fill(v("ZER"), 0.0)
-    fill(v("RED"), 0.0)
-    gv, ga, gb, gB = lane("gv", "LF", 8), lane("ga", "LF", 8), lane("gb", "LF", 8), lane("gB", "LF", 8)
-    pI, lI = lane("pI", "LI", 16), lane("lI", "LI", 16)
-    iota(gv, [[-16, 8]], 0, 1)
-    iota(pI, [[0, 16]], 0, 1)
-    iota(lI, [[16, 16]], 0, 0)
+    fill(v("HLF"), -1.0 / 256)
+    pI, lI = lane("pI", "LI"), lane("lI", "LI")
     asel(v("IDN"), one, [[-1, 128]], Op.is_equal, 0, 1)
+    asel(v("BLK"), one, [[-16, 8], [0, 16]], Op.is_ge, 0, 1)
+    asel(v("BLK"), v("BLK"), [[16, 8], [0, 16]], Op.is_ge, 15, -1)
     asel(v("UPQ", 0, 128), one, [[-1, 128]], Op.is_equal, -16, 1)
     asel(v("UPQ", 128, 256), one, [[-1, 128]], Op.is_equal, 16, 1)
     iota(v("PAR"), [[0, 4], [1, 2], [0, 16]], 0, 0)
     iota(v("K37"), [[37, 16], [0, 16]], 0, 0)
+    iota(pI, [[0, 16]], 0, 1)
+    iota(lI, [[16, 16]], 0, 0)
     iota(v("IO3"), [[0, 16], [1, 16]], 0, 0)
     iota(v("IO4"), [[1, 16], [0, 16]], 0, 0)
-    asel(v("BLK"), one, [[-16, 8], [0, 16]], Op.is_ge, 0, 1)
-    asel(v("BLK"), v("BLK"), [[16, 8], [0, 16]], Op.is_ge, 15, -1)
-    iota(v("KC"), [[4096, 16], [0, 16]], 32 * 131072, 0)
-    iota(v("IO5"), [[0, 16], [1, NE]], 0, 0)
+    iota(v("KC"), [[0, 16], [2, 16]], 1985, 0)
+    asel(v("PRM"), v("ONE", 0, 144), [[-1, 16], [-16, 9]], Op.is_equal, 16, 1)
+    asel(v("TRI"), v("BLK"), [[1, 128]], Op.is_ge, -1, -1)
+    asel(v("BSEL"), v("ONE"), [[-1, 16], [-16, 8], [0, 16]], Op.is_equal, 0, 1)
     ts(v("NPAR"), v("PAR"), -1.0, Op.mult, 1.0, Op.add)
 
     def smx(gp, lhp):
@@ -165,86 +195,109 @@ def rank_program(g, core, T, topo):
         for lhp in range(2):
             src = v("IDN") if gp == lhp else v("UPQ", 0, 128) if lhp == 1 else v("UPQ", 128, 256)
             tt(smx(gp, lhp), src, v("PAR") if gp else v("NPAR"), Op.mult)
-    ts(ga, gv, 0.0, Op.is_ge)
-    ts(gb, gv, 15.0, Op.is_le)
-    tt(gB, ga, gb, Op.mult)
-    for lp in range(16):
-        cp(v("RED", lp * 128 + lp, lp * 128 + 128, 16), gB)
-    wh, wf = lane("wh", "LF", 1), lane("wf", "LF", 1)
+    wh, wf, wg = lane("wh", "LF", 1), lane("wf", "LF", 1), v("WG", 0, 8)
     ts(wh, v("WTI"), 2048.0, Op.is_ge, -4096.0, Op.mult)
     tt(wf, wh, v("WTI"), Op.add)
-    ts(v("WRED"), v("RED"), wf, Op.mult)
-    for nm, c in (("NEG", -1.0), ("I64", 64.0), ("N64", -64.0), ("I1K", 1024.0), ("I32", 32.0), ("D19", 19616.0)):
+    ts(wg, grp, wf, Op.mult, 1.0 / 4096, Op.mult)
+    for nm, c in (("I4K", 4096.0), ("NEG", -1.0), ("I64", 64.0), ("N64", -64.0), ("I2K", 2048.0), ("NBG", -8388608.0)):
         ts(v(nm), v("IDN"), c, Op.mult)
+    ts(v("P4K"), v("PRM"), 4096.0, Op.mult)
+    ts(v("PBG"), v("PRM"), -8388608.0, Op.mult)
 
-    def mat(name, lp):
-        return v(name, lp * 128, lp * 128 + 128)
-    u0, uI, u4 = v("pb1", 256, 272), lane("uI", "LI", 64), lane("u_0", "LI", 64)
-    mms([(u0, mat("WRED", lp), v("ZW", ZS + lp, ZS + 256, 16), lp == 0, lp == 15) for lp in range(16)])
-    for q in range(4):
-        cp(sub(uI, 16 * q, 16 * q + 16), u0)
-    ts(u4, uI, 4095, Op.bitwise_and)
+    def residue(out, q, src):
+        ts(q, src, 1.0 / 8192, Op.add)
+        tt(out, src, q, Op.subtract)
+    u4 = lane("u_0", "LI", 64)
+    mms([(v("pb1", 0, 128, p=16), v("ONE", 0, 16), v("HLF"), True, False)] +
+        [(v("pb1", lp, 128, 16, p=16), v("ZW", ZS + lp, ZS + 256, 16), wg, False, lp == 15) for lp in range(16)])
+    residue(v("FR", 0, 128, p=16), v("QQ", 0, 128, p=16), v("pb1", 0, 128, p=16))
+    mms([(v("pb1", 256 + 16 * i, 272 + 16 * i), v("FR", 0, 128, p=16), v("I4K", 0, 16, p=16), True, True) for i in range(4)])
+    ts(u4, v("pb1", 256, 320), 2048.0, Op.add)
 
-    def conv_k(bank, c0, src):
-        mms([(v(bank, c0 + k * 16 + lhp, c0 + k * 16 + 16, 2), smx(gp, lhp), v(src, gp * 16 + k, 256, 32), gp == 0, gp == 1)
-             for k in range(16) for lhp in range(2) for gp in range(2)])
+    NB, NK = v("pb7", 0, 256), v("pb7", 256, 512)
     ts(v("NMF"), v("NMI"), -2048.0, Op.add)
     turn(v("NMT"), v("NMF"))
-    conv_k("pb6", 0, "NMT")
-    ts(v("NB"), v("pb6", 0, 256), 2048.0, Op.add)
-    tt(v("T3"), v("NB"), v("K37"), Op.add)
-    ts(v("T2"), v("T3"), 4095, Op.bitwise_and)
-    ts(v("NK"), v("T2"), 32.0, Op.mult, -131072.0, Op.add)
-    turn(v("CAT"), v("CAI"))
-    turn(v("RTT"), v("RTI"))
-    conv_k("pb0", 256, "CAT")
-    mms([(v("pb0", (2 * b + lhp) * 16, (2 * b + lhp) * 16 + 16), smx(gp, lhp), v("RTT", 32 * b + 16 * gp, 32 * b + 16 * gp + 16), gp == 0, gp == 1)
+    mms([(v("pb2", 2 * b + lhp, 256, 16), smx(gp, lhp), v("NMT", 32 * b + 16 * gp, 32 * b + 16 * gp + 16), gp == 0, gp == 1)
          for b in range(8) for lhp in range(2) for gp in range(2)])
+    ts(NB, v("pb2", 0, 256), 2048.0, Op.add)
+    tt(v("T3"), NB, v("K37"), Op.add)
+    ts(v("T2"), v("T3"), 4095, Op.bitwise_and)
+    ts(NK, v("T2"), 32.0, Op.mult, -131072.0, Op.add)
     RTP, CAN = v("pb0", 0, 256), v("pb0", 256, 512)
-    CB = v("pb7", 0, 256)
-    ts(v("CAC"), CAN, -1.0, Op.mult, 32.0, Op.add)
-    ts(v("KS"), CAN, -131072.0, Op.mult)
-    tt(CB, v("KS"), v("KC"), Op.add)
-    cp(v("RTB"), RTP)
-    cp(v("CAB"), CAN)
+    for src, tr, bk, to in (("RTI", "RTT", "pb5", "RTB"), ("CAI", "CAT", "pb6", "CAB")):
+        turn(v(tr), v(src))
+        mms([(v(bk, 128 * lhp, 128 * lhp + 128), smx(gp, lhp), v(tr, 16 * gp, 16 * gp + 16), gp == 0, gp == 1) for lhp in range(2) for gp in range(2)])
+        for lhp in range(2):
+            act(w(to, lhp, 16, 0, 16, 2), v(bk, 128 * lhp, 128 * lhp + 128), Act.Copy)
+    mms([(RTP, v("IDN"), v("RTB"), True, True), (CAN, v("IDN"), v("CAB"), True, True)])
+    ts(v("CAC"), v("CAB"), -1.0, Op.mult, 31.0, Op.add)
+    ts(v("KS"), v("CAB"), -64.0, Op.mult)
+    fill(v("CB", 0, 1), 4096.0)
+    fill(v("CM", 0, 1), 0.0)
+    tt(v("CB", 1, 9), v("KS"), v("KC"), Op.add)
+    for h in range(2):
+        fill(v("AL%d" % h), 8388608.0)
+        fill(v("AL%d" % h, 1, 144, 9), 0.0)
     fill(v("LEV0"), 0.0)
-    pm, lc, dmp = lane("pm", "LI", 16), lane("lc", "LI", 16), lane("dmp", "LF", 16)
+    pm, lc, dmp = lane("pm", "LI"), lane("lc", "LI"), lane("dmp", "LF")
     pf, thf = lane("pf", "LF", 1), lane("thf", "LF", 1)
     ts(pm, pI, 15, Op.bitwise_and)
     tt(lc, pm, lI, Op.add)
     ts(dmp, lc, 4096.0, Op.add)
     cp(pf, sub(pm, 0, 1))
     cp(thf, v("THI"))
-    ts(v("THM"), v("IO4"), pf, Op.is_equal, thf, Op.mult)
-    mms([(v("pb4", 256, 512), v("BLK"), v("THM"), True, True)])
-    ts(v("TH"), v("pb4", 256, 512), 1024.0, Op.add)
+    ts(v("SEL"), v("IO4"), pf, Op.is_equal)
+    ts(v("THB"), v("BLK"), thf, Op.mult)
+    mms([(v("pb4", 128 * h, 128 * h + 128), v("SEL", 128 * h, 128 * h + 128), v("THB"), True, True) for h in range(2)])
+    ts(v("THC"), v("pb4", 0, 256), -1.0, Op.mult)
     ts(v("OFFD"), v("IO3"), pf, Op.not_equal, -1000.0, Op.mult)
     ts(v("RSM"), v("IO3"), 0.0, Op.is_gt)
     ts(v("RSA"), v("RSM"), -1001.0, Op.mult, 1000.0, Op.add)
-    ts(v("RS9"), v("IO5"), 0.0, Op.is_gt)
+    for ne in (4, 8):
+        fill(v("RS%d" % ne), 1.0)
+        fill(v("RS%d" % ne, 0, 16 * ne, ne), 0.0)
     wq, si, si2, s63 = lane("wq", "LH", 2), lane("si", "LI", 1), lane("si2", "LI", 1), lane("s63", "LF", 1)
     cp(sub(wq, 0, 1), wf)
-    mms([(v("pb1", 280, 281), v("BLK"), sub(wq, 0, 1), True, True)])
-    ts(si, v("pb1", 280, 281), 63.0, Op.mult)
+    mms([(v("pb3", 0, 1), v("BLK"), sub(wq, 0, 1), True, True)])
+    ts(si, v("pb3", 0, 1), 63.0, Op.mult)
     ts(si2, si, 4095, Op.bitwise_and)
     cp(s63, si2)
-    asel(v("BSEL"), v("ONE"), [[-1, 16], [-16, 8], [0, 16]], Op.is_equal, 0, 1)
-    asel(v("TRI"), v("ONE"), [[0, 16], [-16, 8], [0, 16]], Op.is_ge, 0, 1)
-    asel(v("TRI"), v("TRI"), [[1, 16], [16, 8], [0, 16]], Op.is_ge, -1, -1)
-    fill(lane("d_0", "LB"), 0.0)
-    fill(lane("ptr_0", "LB"), 0.0)
-    fill(v("HD"), -1.0)
-    fill(v("HD", 0, 144, NE), 0.0)
+    L3 = lane("L3", "LB", 64)
+    tau, dl, pn, f = [sub(L3, 16 * i, 16 * i + 16) for i in range(4)]
+    tau4, dl4, pn4, f4 = [v("L4", 64 * i, 64 * i + 64) for i in range(4)]
+    fill(f, 0.5)
+    fill(f4, 0.5)
+    fill(v("HD"), 0.0)
+    fill(v("HD", 0, 1), 0.5)
     fill(v("HC"), 0.0)
     A = None
+    flip = [0]
+
+    def minus(src, a, b, other):
+        flip[0] ^= 1
+        bank = "pb3" if flip[0] else "pb2"
+        lst = [(v(bank, 0, b - a), v("IDN"), v(src, a, b), True, False)]
+        c = 0
+        for i, o in enumerate(other):
+            lst.append((v(bank, c, c + width(o)), v("NEG"), o, False, i == len(other) - 1))
+            c += width(o)
+        mms(lst)
+        return v(bank, 0, b - a)
+
+    def sums(out, src, h, rhs, first=None):
+        lst = [(out, first[0], first[1], True, False)] if first else []
+        mms(lst + [((out[0], out[1] + lp, out[2], 16, None, 128), v(src, 2048 * h + lp, 2048 * h + 2048, 16), rhs, not first, not first or lp == 15)
+                   for lp in range(16)])
 
     for s in range(STEPS):
         par, nxp, last = "_%d" % (s % 2), "_%d" % ((s + 1) % 2), s == STEPS - 1
 
-        def L(name, buf, w=32, par=par):
-            return lane(name + par, buf, w)
-        u, d = L("u", "LI", 64), L("d", "LB")
+        def L(name, buf, wd=16):
+            return lane(name, buf, wd)
+        u = lane("u" + par, "LI", 64)
+        u1 = sub(u, 0, 16)
         z = v("ZW", ZS + 256 * s, ZS + 256 * s + 256)
+        tag[:] = ["x0", s]
         if s:
             en = topo.engines(core, nxt)[:8]
             rid, pid = topo.addr(nxt)[:2]
@@ -256,206 +309,208 @@ def rank_program(g, core, T, topo):
                 add("gpsimd", fn, [src], [], 1.0, done=("none", 0))
             zin, win, wo = v("ZIN", 256 * s, 256 * s + 256), v("WIN", 16 * s, 16 * s + 16), v("WO", 16 * s, 16 * s + 16)
             send(zin, z, "az%d" % s)
-        tag[0] = "x"
         for q in range(4):
+            part("x", q)
             c0, c1 = 64 * q, 64 * q + 64
-            t1, t2, t3, xo = v("pb7", 256 + c0, 256 + c1), v("T2", c0, c1), v("T3", c0, c1), v("XO", c0, c1)
-            tt(t1, v("NB", c0, c1), u, Op.mult)
-            tt(t2, t1, v("NK", c0, c1), Op.add)
+            t1, t2, t3, xo = v("T1", c0, c1), v("T2", c0, c1), v("T3", c0, c1), v("XO", c0, c1)
+            tt(t1, sub(NB, c0, c1), u, Op.mult)
+            tt(t2, sub(NK, c0, c1), t1, Op.add)
             ts(t3, t2, 5, Op.arith_shift_right, 4095, Op.bitwise_and)
-            if A is None:
-                cp(xo, t3)
-            else:
-                ts(xo, t3, A, Op.add)
+            lin(xo, t3, 1.0, 0.0 if A is None else A, eng=PLAN["X"][q] if PLAN["SMALL"] == "S" else "V")
         tag[0] = "sh"
-        d1, d2 = L("d1", "LB", 64), L("d2", "LB")
-        act(sub(d1, 0, 32), d, Act.Identity, bias=1.0)
-        act(sub(d1, 32, 64), d, Act.Identity, bias=1.0)
-        act(d2, d, Act.Identity, scale=2.0, bias=1.0)
-        DR, dr = v("pb2", 0, 256), v("pb2", 256, 400)
-        mms([(sub(DR, 64 * i, 64 * i + 64), v("D19"), d1, True, True) for i in range(4)])
-        fa, fb = L("fa", "LI", 16), L("fb", "LI", 16)
-        ts(fa, h16(u), -1.0, Op.mult, s63, Op.add)
+        dd, d2, d3, dp, dt = L("dd", "LB"), L("d2", "LB"), L("d3", "LB"), L("dp", "LF"), L("dt", "LF", 64)
+        act(dd, f, Act.Identity, bias=-0.5)
+        act(d2, f, Act.Identity, scale=2.0)
+        act(d3, f, Act.Identity, bias=1.0)
+        act(dp, f, Act.Sign, bias=-0.5)
+        for a, b, src in ((0, 16, f), (16, 32, f)):
+            act(sub(dt, a, b), src, Act.Identity, scale=19616.0, bias=9808.0 + 42752)
+        act(sub(dt, 32, 64), sub(dt, 0, 32), Act.Copy)
+        fa, fb = L("fa", "LI"), L("fb", "LI")
+        lin(fa, u1, -1.0, s63)
         ts(fb, fa, 4095, Op.bitwise_and)
-        cp(v("HC", 0, 144, NE), fb)
-        mms([(v("pb2", 256 + e, 400, NE), v("IDN"), h16(d), True, True) for e in range(s + 1 if s else NE)])
-        tt(dr, v("HD"), dr, Op.is_equal)
-        tt(v("DC"), dr, v("HC"), Op.mult)
-        scan(v("TS"), v("RS9"), v("DC"), Op.mult, Op.max)
-        top, ta, tb, tc, tca, pt = L("top", "LI"), L("ta", "LI"), L("tb", "LI"), L("tc", "LI"), L("tca", "LI"), L("pt", "LB")
-        cp(sub(top, 0, 16), v("TS", NE - 1, 144, NE))
-        cp(sub(top, 16, 32), v("TS", NE - 1, 144, NE))
-        ts(ta, top, 4095, Op.bitwise_and)
-        ts(tb, top, 6, Op.arith_shift_right, 0xF000, Op.bitwise_and)
-        tt(tc, ta, tb, Op.add)
-        ts(tca, top, 12, Op.arith_shift_right, 63, Op.bitwise_and)
-        ts(pt, tca, -1.0, Op.mult, 33.0, Op.add)
+        tc, tf, tca, pt = L("tc", "LI"), L("tf", "LF"), L("tca", "LF"), L("pt", "LB")
+        if s:
+            ne = 4 if s < 4 else 8
+            lin(v("HC", 0, 1), fb)
+            dr = v("pb6", 256, 256 + 16 * ne)
+            mms([(v("pb6", 256 + e, 256 + 16 * ne, ne // 4), v("IDN"), f4, True, True) for e in range(ne // 4)])
+            tt(dr, v("HD", 0, ne), dr, Op.is_equal)
+            tt(v("DC", 0, 16 * ne), dr, v("HC", 0, ne), Op.mult)
+            scan(v("TS", 0, 16 * ne), v("RS%d" % ne), v("DC", 0, 16 * ne), Op.mult, Op.max)
+            top = v("TS", ne - 1, 16 * ne, ne)
+            cp(tc, top)
+            tt(tf, top, tc, Op.subtract)
+            act(tca, tf, Act.Identity, scale=64.0)
+            act(pt, tf, Act.Identity, scale=-64.0, bias=32.0)
+        else:
+            tc = fb
+            fill(tca, 0.0)
+            fill(pt, 0.0)
         scan(v("KS"), v("RSA"), RTP, Op.max, Op.min)
-        act(v("CM"), CAN, Act.Sign, bias=0.5)
-        kk, kth, kp, dp, alt = L("kk", "LF"), L("kth", "LF"), L("kp", "LF"), L("dp", "LF"), L("alt", "LF")
-        for i in range(2):
-            act(sub(kk, 16 * i, 16 * i + 16), v("KS", 15, 256, 16), Act.Identity, scale=-131072.0, bias=32.0 * 131072 + 65536)
-        act(kth, kk, Act.Identity, bias=65536.0)
-        act(dp, d, Act.Sign)
+        act(v("CM", 1, 9), CAN, Act.Relu, scale=-1.0)
+        kk, kth, kp = L("kk", "LF"), L("kth", "LF"), L("kp", "LF")
+        act(kk, v("KS", 15, 256, 16), Act.Identity, scale=-131072.0, bias=31.0 * 131072 + 65536)
+        act(kth, v("KS", 15, 256, 16), Act.Identity, scale=-131072.0, bias=32.0 * 131072)
         tt(kp, kth, dp, Op.mult)
+        alt = L("alt", "LF")
         tt(alt, tc, kk, Op.add)
         act(v("ZW", FL, FL + 256), z, Act.Identity, scale=-1.0, bias=63.0)
         tag[0] = "pl"
         if s:
-            pa, pb, pc, pd, pe = L("pa", "LI", 16), L("pb", "LI", 16), L("pc", "LF", 16), L("pd", "LI", 16), L("pe", "LI", 16)
-            ps, ad = L("ps", "LH", 16), L("ad", "LF", 16)
-            ts(pa, h16(u), 1184.0, Op.add)
-            tt(pb, pa, h16(u), Op.mult)
-            act(pc, h16(d), Act.Copy, scale=19616.0)
+            pb, pc, pd, pe = L("pb", "LF"), L("pc", "LF"), L("pd", "LI"), L("pe", "LI")
+            ps, ad = L("ps", "LH"), L("ad", "LF")
+            if PLAN["SMALL"] == "S":
+                act(pb, u1, Act.Square, bias=592.0)
+            else:
+                ts(pc, u1, 592.0, Op.add)
+                tt(pb, pc, pc, Op.mult)
+            act(pc, f, Act.Identity, scale=19616.0, bias=42752.0 - 9808)
             tt(pd, pb, pc, Op.add)
             ts(pe, pd, 5, Op.arith_shift_right, 4095, Op.bitwise_and)
-            ts(ps, pe, -2048.0, Op.add)
+            lin(ps, pe, 1.0, -2048.0)
             tt(ad, pe, dmp, Op.subtract)
-            mms([(v("pb6", lp, 256, 16), mat("BSEL", lp), ps, True, True) for lp in range(16)])
-            cp(v("PR"), v("pb6", 0, 256))
-        for q in range(4):
-            a, b, c0, c1 = 1024 * q, 1024 * q + 1024, 64 * q, 64 * q + 64
-            tag[0] = "gx"
-            if q:
-                def gx4(a=a, b=b, c0=c0, c1=c1):
-                    return [g.vector.tensor_tensor(T.D[:, a:b], T.XT[:, 0:4128].indirect(T.XO[:, c0:c1]), T.Z4[:], Op.subtract)]
-                add("vector", gx4, [v("XT"), v("XO", c0, c1), v("Z4")], [v("D", a, b)], 0.05 + GAT * 1024 * CYC)
-            else:
-                act(v("Z4", 0, 256), z, Act.Copy)
-                act(v("Z4", 256, 512), z, Act.Copy)
-                act(v("Z4", 512, 1024), v("Z4", 0, 512), Act.Copy)
-                for k in range(4):
-                    def gx(k=k, z=z):
-                        return [g.vector.tensor_tensor(T.D[:, 256 * k:256 * k + 256], T.XT[:, 0:4128].indirect(T.XO[:, 16 * k:16 * k + 16]), ap(z), Op.subtract)]
-                    add("vector", gx, [v("XT"), v("XO", 16 * k, 16 * k + 16), z], [v("D", 256 * k, 256 * k + 256)], 0.05 + GAT * 256 * CYC)
-            tag[0] = "ab"
-            act(v("ZW", a, b), v("D", a, b), Act.Abs)
-            tag[0] = "bb"
-            act(v("BB", a, b), v("D", a, b), Act.Sign, bias=0.5)
-            tag[0] = "vi"
-            up, V2 = v("pb1", c0, c1), v("pb7", 256 + c0, 256 + c1)
-            mms([(up, mat("WRED", lp), v("ZW", a + lp, b, 16), lp == 0, lp == 15) for lp in range(16)])
-            V1, UM, V3, V4, V5 = [v(x, c0, c1) for x in ("V1", "UM", "V3", "V4", "V5")]
-            cp(V1, up)
-            ts(UM, V1, 4095, Op.bitwise_and)
-            ts(V2, UM, 1184.0, Op.add)
-            tt(V3, UM, V2, Op.mult)
-            tt(V4, V3, v("pb2", c0, c1), Op.add)
-            ts(V5, V4, 5, Op.arith_shift_right, 4095, Op.bitwise_and)
-            cp(v("HO", c0, c1), V5)
-            tag[0] = "row"
-            if q == 0:
-                mms([(v("pb3", 0, 256), v("ZER", 0, 128), v("ZER"), True, False)])
-            mms([(v("pb3", c0, c1), mat("RED", lp), v("BB", a + lp, b, 16), False, False) for lp in range(16)])
-            if q == 3:
-                mms([(v("pb3", 0, 256), v("I32"), v("CM"), False, True)])
-                act(v("G1"), v("pb3", 0, 256), Act.Sign, bias=-31.5)
-            tag[0] = "pk"
-            tt(v("PK", c0, c1), UM, sub(CB, c0, c1), Op.add)
-        for q in range(4):
-            a, b, c0, c1 = 1024 * q, 1024 * q + 1024, 64 * q, 64 * q + 64
-            tag[0] = "vg"
-
-            def gvt(a=a, b=b, c0=c0, c1=c1):
-                return [g.vector.tensor_tensor(T.EE[:, a:b], T.VT[:, 0:4096].indirect(T.HO[:, c0:c1]), T.ZW[:, a:b], Op.subtract)]
-            add("vector", gvt, [v("VT", 0, 4096), v("HO", c0, c1), v("ZW", a, b)], [v("EE", a, b)], 0.05 + GAT * 1024 * CYC)
-            act(v("AB", a, b), v("EE", a, b), Act.Abs)
-            tag[0] = "far"
-            fp, ff = v("pb4", c0, c1), v("pb7", 256 + c0, 256 + c1)
-            ky = ff if q else v("KEY")
-            mms([(fp, v("I1K"), v("G1", c0, c1), True, False)] +
-                [(fp, mat("RED", lp), v("AB", a + lp, b, 16), False, lp == 15) for lp in range(16)])
-            tt(ff, fp, v("TH", c0, c1), Op.is_gt)
-            tt(ky, ff, v("PK", c0, c1), Op.mult)
-            if q == 0:
-                tt(sub(ky, 0, 32), sub(ky, 0, 32), alt, Op.max)
-                rm = ky
-            else:
-                tt(v("RM", c0, c1), rm, ky, Op.max)
-                rm = v("RM", c0, c1)
-        M1, Wd = L("M1", "LF", 64), L("W", "LI", 64)
-        tt(sub(M1, 0, 32), sub(rm, 0, 32), sub(rm, 32, 64), Op.max)
-        tt(sub(M1, 32, 64), sub(rm, 0, 32), sub(rm, 32, 64), Op.max)
-        tt(sub(Wd, 0, 48), sub(M1, 0, 48), sub(M1, 16, 64), Op.max)
-        tt(sub(Wd, 48, 64), sub(M1, 48, 64), sub(M1, 0, 16), Op.max)
-        W32 = sub(Wd, 0, 32)
+            mms([(v("pb6", lp, 256, 16), v("BSEL", 128 * lp, 128 * lp + 128), ps, True, True) for lp in range(16)])
+            lin(v("PR"), v("pb6", 0, 256))
+        keys = []
+        for h in range(2):
+            for q in (2 * h, 2 * h + 1):
+                a, b = 1024 * q, 1024 * q + 1024
+                part("gx", q)
+                if PLAN["X"][q] == "V":
+                    for k in range(4 * q, 4 * q + 4):
+                        gather("V", v("D", 256 * k, 256 * k + 256), v("XT"), v("XO", 16 * k, 16 * k + 16), z)
+                    parts = [(a, a + 512, v("D", a, a + 512)), (a + 512, b, v("D", a + 512, b))]
+                else:
+                    gather("S", v("D", a, b), v("XT"), v("XO", 64 * q, 64 * q + 64))
+                    parts = [(a, a + 512, None), (a + 512, b, None)]
+                for a1, b1, d in parts:
+                    d = d or minus("D", a1, b1, [z, z])
+                    part("ab", q)
+                    act(v("ZW", a1, b1), d, Act.Abs)
+                    part("bb", q)
+                    if PLAN["SIGN"][q] == "S":
+                        act(v("BB", a1, b1), d, Act.Sign, bias=0.5)
+                    else:
+                        ts(v("BB", a1, b1), d, 0.0, Op.is_ge, -0.5, Op.add)
+            c0, c1 = 128 * h, 128 * h + 128
+            part("vi", h)
+            bk = ("pb1", "pb4")[h]
+            uc, ub, rw, fr = v(bk, 0, 128), v(bk, 128, 256), v(bk, 256, 384), v("FR", c0, c1)
+            sums(uc, "ZW", h, wg, (one, v("HLF")))
+            residue(fr, v("QQ", c0, c1), uc)
+            mms([(ub, fr, v("I4K"), True, True)])
+            act(ub, ub, Act.Square, bias=2640.0)
+            for c in (0, 64):
+                tt(v("V4", c0 + c, c0 + c + 64), sub(ub, c, c + 64), dt, Op.add)
+            ts(v("V5", c0, c1), v("V4", c0, c1), 5, Op.arith_shift_right, 4095, Op.bitwise_and)
+            lin(v("HO", c0, c1), v("V5", c0, c1))
+            part("row", h)
+            sums(rw, "BB", h, grp)
+            act(v("G1", c0, c1), rw, Act.Relu, scale=-1.0)
+            part("pk", h)
+            key = v(("pb1", "pb5")[h], 0, 144)
+            keys.append([(key, v("I2K"), w("CB", h, 32, 0, 9, 2), True, False), (key, v("NBG"), w("CM", h, 32, 0, 9, 2), False, False),
+                         (key, fr, v("P4K"), False, False), (key, v("G1", c0, c1), v("PBG"), False, False)])
+        mms(keys[1])
+        for h in range(2):
+            for q in (2 * h, 2 * h + 1):
+                a = 1024 * q
+                part("vg", q)
+                if PLAN["V"][q] == "S":
+                    gather("S", v("EE", a, a + 1024), v("VT", 0, 4096), v("HO", 64 * q, 64 * q + 64))
+                for wd in (PLAN["TAIL"] if q == 3 else (1024,)) if PLAN["V"][q] == "V" else (512, 512):
+                    b = a + wd
+                    if PLAN["V"][q] == "V":
+                        e = v("EE", a, b)
+                        gather("V", e, v("VT", 0, 4096), v("HO", a // 16, b // 16), v("ZW", a, b))
+                    else:
+                        e = minus("EE", a, b, [v("ZW", a, b)])
+                    act(v("AB", a, b), e, Act.Abs)
+                    a = b
+            part("far", h)
+            c0, c1 = 128 * h, 128 * h + 128
+            fc = v(("pb1", "pb4")[h], 384, 512)
+            sums(fc, "AB", h, grp, (v("IDN"), v("THC", c0, c1)))
+            act(v("FF", c0, c1), fc, Act.Relu, scale=-1.0, bias=1.0)
+            key = keys[h][0][0]
+            mms(([] if h else keys[0]) + [(key, v("FF", c0, c1), v("PBG"), False, True)])
+            scan(v(("W0", "WK")[h]), v("AL%d" % h), key, Op.min, Op.max)
+            if not h:
+                tt(v("AL1", 1, 144, 9), v("W0", 8, 144, 9), alt, Op.max)
+        W = v("WK", 8, 144, 9)
         tag[0] = "mv"
-        if not last:
-            ts(lane("u" + nxp, "LI", 64), Wd, 4095, Op.bitwise_and)
-        za, zb, zo = L("za", "LI", 16), L("zb", "LI", 16), v("ZO", 16 * (s % 2), 16 * (s % 2) + 16)
-        ts(za, h16(Wd), 4, Op.arith_shift_right, 0x1F00, Op.bitwise_and)
-        tt(zb, za, lc, Op.add)
-        cp(zo, zb)
-        zn, zw = v("ZW", ZS + 256 * (s + 1), ZS + 256 * (s + 2)), v("ZW", 0, ZS + 256 * (s + 1))
-
-        def gz(zn=zn, zw=zw, zo=zo):
-            return [g.scalar.activation(ap(zn), ap(zw).indirect(ap(zo)), Act.Copy)]
-        add("scalar", gz, [zw, zo], [zn], 0.065 + GAT * 256 * CYC)
-        if last:
-            dma("scalar", T.yz[:], ap(zn), [zn], [], "oz", 2.5)
         pop, m = L("pop", "LB"), L("m", "LB")
-        tt(pop, W32, kp, Op.is_lt)
+        tt(pop, W, kp, Op.is_lt)
         if s and not last:
-            cn, ct, am, A = v("pb2", 400, 416), L("ct", "LF", 1), L("am", "LI", 1), L("A", "LF", 1)
-            mms([(cn, one, h16(pop), True, True)])
+            cn, ct, am, A = v("pb1", 0, 16), L("ct", "LF", 1), L("am", "LI", 1), L("A", "LF", 1)
+            mms([(cn, one, pop, True, True)])
             add("vector", lambda ct=ct, cn=cn: [g.vector.tensor_reduce(ap(ct), ap(cn), AxisListType.X, Op.add)], [cn], [ct], 64 * CYC)
             ts(am, ct, 1.0 / 32, Op.mult, -0.484375, Op.add)
             ts(A, am, -32.0, Op.mult, ct, Op.add)
+        tag[0] = "u"
+        if not last:
+            for i in range(4):
+                ts(sub(lane("u" + nxp, "LI", 64), 16 * i, 16 * i + 16), W, 4095, Op.bitwise_and)
+        tag[0] = "z"
+        za, zb, zo = L("za", "LI"), L("zb", "LI"), v("ZO", 16 * (s % 2), 16 * (s % 2) + 16)
+        ts(za, W, 4, Op.arith_shift_right, 0x1F00, Op.bitwise_and)
+        tt(zb, za, lc, Op.add)
+        lin(zo, zb)
+        zn = v("ZW", ZS + 256 * (s + 1), ZS + 256 * (s + 2))
+        gather("S", zn, v("ZW", 0, ZS + 256 * (s + 1)), zo)
+        if last:
+            dma("scalar", T.yz[:], ap(zn), [zn], [], "oz", 2.5)
         tag[0] = "ln"
-        tt(m, W32, kth, Op.is_ge)
-        hi, y1, y2, tau, y3, dl = L("hi", "LI"), L("y1", "LF"), L("y2", "LF"), L("tau", "LB"), L("y3", "LB"), L("dl", "LB")
-        tau4, dl4, pn, pn4 = L("tau4", "LB", 64), L("dl4", "LB", 64), lane("ptr" + nxp, "LB"), L("pn4", "LB", 64)
-        ts(hi, W32, 17, Op.arith_shift_right)
+        hi, y1, y2, y3 = L("hi", "LI"), L("y1", "LF"), L("y2", "LF"), L("y3", "LB")
+        tt(m, W, kth, Op.is_ge)
+        ts(hi, W, 17, Op.arith_shift_right)
         tt(y1, hi, tca, Op.subtract)
         tt(y2, y1, m, Op.mult)
         tt(tau, y2, tca, Op.add)
         tt(y3, m, d2, Op.mult)
-        tt(dl, y3, d, Op.subtract)
-        for i in range(2):
-            act(sub(tau4, 32 * i, 32 * i + 32), tau, Act.Copy)
-            act(sub(dl4, 32 * i, 32 * i + 32), dl, Act.Copy)
-        mms([(v("pb5", 64 * i, 64 * i + 64), v("IDN"), tau4, True, True) for i in range(4)] +
-            [(v("pb5", 256 + 64 * i, 320 + 64 * i), v("IDN"), dl4, True, True) for i in range(4)])
-        lv = v("LEV%d" % ((s + 1) % 2))
-        tt(v("HIT"), v("CAC"), v("pb5", 0, 256), Op.is_equal)
-        tt(v("pb5", 0, 256), v("HIT"), v("pb5", 256, 512), Op.mult)
-        tt(lv, v("LEV%d" % (s % 2)), v("pb5", 0, 256), Op.add)
+        tt(dl, y3, dd, Op.subtract)
         tt(pn, pop, pt, Op.mult)
+        act(f, dl, Act.Abs, bias=0.5)
+        for i in range(4):
+            act(v("L4", i, 256, 4), L3, Act.Copy)
+        tp, dlp = v("pb5", 256, 512), v("pb5", 0, 256)
+        mms([(v("pb5", 256 + i, 512, 4), v("IDN"), tau4, True, True) for i in range(4)] + [(v("pb5", i, 256, 4), v("IDN"), dl4, True, True) for i in range(4)])
+        lv = v("LEV%d" % ((s + 1) % 2))
+        tt(v("HIT"), v("CAC"), tp, Op.is_equal)
+        tt(dlp, v("HIT"), dlp, Op.mult)
+        tt(lv, v("LEV%d" % (s % 2)), dlp, Op.add)
         if not last:
-            act(sub(pn4, 0, 32), pn, Act.Copy)
-            act(sub(pn4, 32, 64), pn, Act.Copy)
-            mms([(RTP, v("IDN"), v("RTB"), True, False)] + [(v("pb0", k, 256, 16), v("I64"), sub(lv, 16 * k, 16 * k + 16), False, k == 15) for k in range(16)])
-            mms([(CAN, v("IDN"), v("CAB"), True, False), (CAN, v("N64"), lv, False, False)] +
-                [(v("pb0", 256 + 64 * i, 320 + 64 * i), v("NEG"), pn4, False, i == 3) for i in range(4)])
-            dx, ca_, cb_ = L("dx", "LB"), L("ca_", "LI", 16), L("cb_", "LI", 16)
-            tt(dx, d, m, Op.add)
-            tt(lane("d" + nxp, "LB"), dx, pop, Op.subtract)
-            tt(v("HD", s + 1, 144, NE), h16(m), h16(d1), Op.mult)
-            ts(ca_, h16(hi), 4096.0, Op.mult, float((s + 1) * 262144), Op.add)
-            tt(cb_, ca_, h16(u), Op.add)
-            tt(v("HC", s + 1, 144, NE), cb_, h16(m), Op.mult)
+            mms([(RTP, v("IDN"), v("RTB"), True, False), (RTP, v("I64"), lv, False, True),
+                 (CAN, v("IDN"), v("CAB"), True, False), (CAN, v("N64"), lv, False, False)] +
+                [(v("pb0", 256 + i, 512, 4), v("NEG"), pn4, False, i == 3) for i in range(4)])
+            ca_ = L("ca_", "LF")
+            tt(v("HD", s + 1, s + 2), m, d3, Op.mult)
+            lin(ca_, hi, 1.0 / 64, (s + 1) * 4096.0)
+            tt(v("HC", s + 1, s + 2), ca_, u1, Op.add)
         tag[0] = "dd"
         if s:
-            sx, sc = L("sx", "LF", 16), L("sc", "LF", 16)
-            act(sx, h16(pop), Act.Identity, scale=-9999.0, bias=9999.0)
+            sx, sc = L("sx", "LF"), L("sc", "LF")
+            act(sx, pop, Act.Identity, scale=-9999.0, bias=9999.0)
             tt(sc, sx, ps, Op.add)
             for lh in range(16):
-                ts(v("CMP", 272 * lh, 256 * lh + 256), v("PR", 16 * lh, 256), sub(sc, lh, lh + 1), Op.is_equal)
-            mms([(v("pb6", 0, 256), v("IDN"), v("OFFD"), True, False)] +
-                [(v("pb6", 16 * lh + 16, 256), v("BLK"), v("CMP", 272 * lh + 16, 256 * lh + 256), False, False) for lh in range(15)] +
-                [(v("pb6", lp, 256, 16), mat("TRI", lp), v("CMP", lp, 4096, 272), False, lp == 15) for lp in range(16)])
-            scan(v("CS"), v("RSM"), v("pb6", 0, 256), Op.mult, Op.max)
-            nc, wn, wa, wb = L("nc", "LF", 16), L("wn", "LF", 16), L("wa", "LF", 16), L("wb", "LF", 16)
-            ts(nc, v("CS", 15, 256, 16), 0.5, Op.is_lt)
-            tt(wn, nc, h16(pop), Op.mult)
+                ts(w("CMP", lh, lh + 1, 0, 256 - 16 * lh), v("PR", 16 * lh, 256), sub(sc, lh, lh + 1), Op.is_equal)
+            cnt = v("pb6", 0, 256)
+            mms([(cnt, v("IDN"), v("OFFD"), True, False)])
+            for lh in range(15):
+                mms([(v("pb6", 16 * lh + 16, 256), v("BLK"), w("CMP", lh, lh + 1, 16, 256 - 16 * lh), False, False)])
+            mms([(cnt, v("TRI"), v("CMP", 0, 16), False, True)])
+            scan(v("CS"), v("RSM"), cnt, Op.mult, Op.max)
+            wn, wa, wb = L("wn", "LF"), L("wa", "LF"), L("wb", "LF")
+            tt(wn, v("CS", 15, 256, 16), pop, Op.is_lt)
             tt(wa, wn, ad, Op.mult)
             tt(wb, wa, dmp, Op.add)
-            cp(wo, wb)
+            lin(wo, wb, eng="V")
             send(win, wo, "aw%d" % s)
             tag[0] = "sc"
 
             def scat(lst, src):
-                add("vector", lambda: [g.vector.tensor_copy(T.VT[:, 0:4352].indirect(ap(lst)), ap(src))], [lst, src], [v("VT")], 0.05 + 3.8 * 256 * CYC)
+                add("vector", lambda: [g.vector.tensor_copy(T.VT[:, 0:4352].indirect(ap(lst)), ap(src))], [lst, src], [v("VT")], 0.05 + SCA * 256 * CYC)
             snd = len(ops) - 1
             scat(wo, z)
             ne = len(topo.engines(prv, core)[:8])
@@ -463,18 +518,15 @@ def rank_program(g, core, T, topo):
             scat(win, zin)
     tag[0] = "out"
     dma("sync", T.yv[:], T.VT[:, 0:4096], [v("VT")], [], "ov", 8.0)
-    pz = h16(lane("ptr_0", "LB"))
-    add("tensor", lambda: [g.tensor.matmul(T.pb1[0:8, lp:256:16], T.BSEL[:, lp * 128:lp * 128 + 128:16], ap(pz), True, True) for lp in range(16)],
-        [v("BSEL"), pz], [v("pb1", 0, 256)], 1.0)
+    add("tensor", lambda: [g.tensor.matmul(T.pb1[0:8, lp:256:16], T.BSEL[:, lp * 128:lp * 128 + 128:16], ap(pn), True, True) for lp in range(16)],
+        [v("BSEL"), pn], [v("pb1", 0, 256)], 1.0)
     add("vector", lambda: [g.vector.tensor_scalar(T.YP[0:8, :], T.pb1[0:8, 0:256], -1.0, None, Op.add)], [v("pb1", 0, 256)], [v("YP")], 0.22)
     dma("sync", T.yp[:], T.YP[0:8, :], [v("YP")], [], "op", 2.5)
-    mms([(v("pb0", k, 256, 16), v("IDN"), sub(lv, 16 * k, 16 * k + 16), True, True) for k in range(16)])
-    cp(v("LEV"), RTP)
-    mms([(v("pb3", 32 * b + 16 * gp, 32 * b + 16 * gp + 16), smx(lhp, gp), v("LEV", (2 * b + lhp) * 16, (2 * b + lhp) * 16 + 16), lhp == 0, lhp == 1)
-         for b in range(8) for gp in range(2) for lhp in range(2)])
-    cp(v("LVT"), v("pb3", 0, 256))
-    turn(v("YL"), v("LVT"))
-    cp(v("YLB"), v("YL"))
+    cp(v("LV3"), lv)
+    mms([(v("pb0", 128 * gp, 128 * gp + 128), smx(lhp, gp), w("LV3", lhp, 16, 0, 16, 2), lhp == 0, lhp == 1) for gp in range(2) for lhp in range(2)])
+    for gp in range(2):
+        act(v("CAT", 16 * gp, 16 * gp + 16), v("pb0", 128 * gp, 128 * gp + 128), Act.Copy)
+    turn(v("YLB"), v("CAT"))
     dma("scalar", T.yl[:], T.YLB[:], [v("YLB")], [], "ol", 2.5)
     queues = {"vector": g.vector, "scalar": g.scalar, "tensor": g.tensor, "gpsimd": g, "sync": g.sync}
     schedule(g, T, ops, queues)
@@ -484,67 +536,123 @@ def rank_program(g, core, T, topo):
 def schedule(g, T, ops, queues):
     N = len(ops)
     preds = [dict() for _ in range(N)]
-    hist = {}
+    hist, bank = {}, {}
     for i, o in enumerate(ops):
         for p in o["pre"]:
             preds[i][p] = o["q"] != "net"
+        o["banks"] = sorted(set(x[0][:3] for x in o["rd"] + o["wr"] if SCRATCH[x[0]][0] == "psum"))
         for kind, regs in (("r", o["rd"]), ("w", o["wr"])):
-            for (name, c0, c1, st) in regs:
-                ps = SCRATCH[name][0] == "psum"
-                for (j, k2, b0, b1) in hist.get(name, ()):
-                    if j == i:
-                        continue
-                    same = ops[j]["q"] == o["q"] and not ops[j]["done"]
-                    if b0 < c1 and c0 < b1 and (kind == "w" or k2 == "w"):
-                        need = (not same) or k2 == "w"
-                        if same and o["q"] == "tensor" and ps:
-                            need = False
+            for x in regs:
+                a0, a1 = x[4][:2] if x[4] else (0, 1)
+                for (j, k2, b0, b1, e0, e1, st) in hist.get(x[0], ()):
+                    if j != i and (st != x[3] or (b0 - x[1]) % st == 0) and b0 < x[2] and x[1] < b1 and e0 < a1 and a0 < e1 and (kind == "w" or k2 == "w"):
+                        same = ops[j]["q"] == o["q"] and not ops[j]["done"]
+                        need = not same or (k2 == "w" and not (o["q"] == "tensor" and SCRATCH[x[0]][0] == "psum"))
                         preds[i][j] = preds[i].get(j, False) or need
-                    elif ps and not same:
-                        preds[i][j] = True
+        if o["q"] == "tensor":
+            for b in set(o["banks"]) & {"pb5", "pb6"}:
+                if b in bank:
+                    preds[i].setdefault(bank[b], False)
+                bank[b] = i
         for kind, regs in (("r", o["rd"]), ("w", o["wr"])):
-            for (name, c0, c1, st) in regs:
-                h = hist.setdefault(name, [])
-                if kind == "w" and st == 1:
-                    keep = SCRATCH[name][0] == "psum"
-                    h[:] = [x for x in h if not (c0 <= x[2] and x[3] <= c1 and x[0] != i) or (keep and x[0] > i - 600)]
-                h.append((i, kind, c0, c1))
-    succ = [[] for _ in range(N)]
+            for x in regs:
+                a0, a1, sa = x[4] or (0, 1, 1)
+                h = hist.setdefault(x[0], [])
+                if kind == "w" and x[3] == 1 and sa == 1 and x[5] == 128:
+                    h[:] = [y for y in h if not (x[1] <= y[2] and y[3] <= x[2] and a0 <= y[4] and y[5] <= a1 and y[0] != i)]
+                h.append((i, kind, x[1], x[2], a0, a1, x[3]))
+    occ = [0.0 if o["q"] == "net" else 0.1 if o["done"] and o["done"][1] else o["cost"] for o in ops]
+    fw = [[(j, ops[j]["cost"] + LAT if c or ops[j]["q"] != ops[i]["q"] else occ[j]) for j, c in preds[i].items()] for i in range(N)]
+    bw = [[] for _ in range(N)]
     for i in range(N):
-        for j in preds[i]:
-            succ[j].append(i)
-    prio = [0.0] * N
-    for i in range(N - 1, -1, -1):
-        prio[i] = ops[i]["cost"] + max([prio[x] + LAT for x in succ[i]] + [0.0])
-    own = [prio[i] + BIAS.get(ops[i]["tag"], 0.0) for i in range(N)]
-    left = [len(p) for p in preds]
-    est, end = [0.0] * N, [0.0] * N
-    free, ready, order, seq = {}, {}, {}, []
-    for i in range(N):
-        if not left[i]:
-            ready.setdefault(ops[i]["q"], []).append(i)
-    for _ in range(N):
-        best = None
-        for q, lst in ready.items():
-            if not lst:
+        for j, dly in fw[i]:
+            bw[j].append((i, dly + occ[i] - occ[j]))
+
+    lines = [[(o["q"], 0.0)] + [(b + e, LAT) for b in o["banks"] for e in ("vector", "scalar", "tensor") if e != o["q"]] for o in ops]
+    holds = [[o["q"]] + [b + o["q"] for b in o["banks"]] for o in ops]
+
+    def after(lst, t):
+        a, b = 0, len(lst)
+        while a < b:
+            c = (a + b) // 2
+            a, b = (c + 1, b) if lst[c][1] <= t else (a, c)
+        return a
+
+    def place(edges, key):
+        at, busy, done = [0.0] * N, {}, [False] * N
+        stack = sorted(range(N), key=key, reverse=True)
+        while stack:
+            i = stack[-1]
+            late = [j for j, _ in edges[i] if not done[j]]
+            if late:
+                stack += sorted(late, key=key, reverse=True)
                 continue
-            f = free.get(q, 0.0)
-            t0 = min(max(f, est[i]) for i in lst)
-            i = max((x for x in lst if max(f, est[x]) <= t0 + WIN), key=lambda x: own[x])
-            t = max(f, est[i])
-            if best is None or t < best[0]:
-                best = (t, q, i)
-        t, q, i = best
-        ready[q].remove(i)
-        end[i] = t + ops[i]["cost"]
-        free[q] = t if q == "net" else t + 0.1 if ops[i]["done"] and ops[i]["done"][1] else end[i]
-        order.setdefault(q, []).append(i)
-        seq.append(i)
-        for x in succ[i]:
-            est[x] = max(est[x], t if ops[x]["q"] == q and not preds[x][i] else end[i] + LAT)
-            left[x] -= 1
-            if not left[x]:
-                ready.setdefault(ops[x]["q"], []).append(x)
+            stack.pop()
+            if done[i]:
+                continue
+            t, d = max([at[j] + dly for j, dly in edges[i]] + [0.0]), occ[i]
+            moved = d > 0
+            while moved:
+                moved = False
+                for r, pad in lines[i]:
+                    lst = busy.get(r)
+                    if lst and lst[-1][1] + pad > t:
+                        c = after(lst, t - pad + 1e-9)
+                        while c < len(lst) and lst[c][0] < t + d + pad - 1e-9:
+                            t, moved, c = lst[c][1] + pad, len(lines[i]) > 1, c + 1
+            for r in holds[i]:
+                lst = busy.setdefault(r, [])
+                if not lst or lst[-1][1] <= t + 1e-9:
+                    lst.append((t, t + d))
+                else:
+                    lst.insert(after(lst, t + 1e-9), (t, t + d))
+            at[i], done[i] = t, True
+        return at
+
+    def arrange():
+        prio = [0.0] * N
+        for i in range(N - 1, -1, -1):
+            prio[i] = max([prio[x] + dly + occ[i] - occ[x] for x, dly in bw[i]] + [ops[i]["cost"]])
+        top = max(prio) - 12
+        key = [20.0 * o["step"] + WHEN[o["tag"]] if o["tag"] in WHEN else top - prio[i] for i, o in enumerate(ops)]
+        twins, nth = {}, {}
+        for i, o in enumerate(ops):
+            k = (o["step"], o["tag"])
+            nth[k] = nth.get(k, 0) + 1
+            twins.setdefault((o["tag"], nth[k]), []).append(i)
+        names, seed, cur, best = list(twins), [SEED], None, None
+
+        def rnd():
+            seed[0] = (seed[0] * 1103515245 + 12345) % 2147483648
+            return seed[0] / 2147483648.0
+        for n in range(ROUNDS + 1):
+            at = place(fw, lambda i: (key[i], i))
+            span = max(at[i] + ops[i]["cost"] for i in range(N))
+            if cur is None or span <= cur[0] - HEAT * (1.001 - n / ROUNDS) * math.log(rnd() + 1e-9):
+                cur = (span, at)
+                best = cur if best is None or span < best[0] else best
+            key = list(cur[1])
+            if rnd() < 0.15:
+                back = place(bw, lambda i: (-key[i] - occ[i], -i))
+                key = [-back[i] - occ[i] for i in range(N)]
+                continue
+            for _ in range(1 << int(4 * rnd())):
+                name, k = names[int(rnd() * len(names))]
+                shift = (rnd() + rnd() - 1) * (0.7, 2.5, 7.0)[int(3 * rnd())]
+                for j in range((1, 1, 2, 4)[int(4 * rnd())]):
+                    for i in twins.get((name, k + j), ()):
+                        key[i] += shift
+        return best + (max(prio),)
+    if N not in ORDER:
+        ORDER[N] = arrange()
+    at = ORDER[N][1]
+    seq, users = sorted(range(N), key=lambda i: (at[i], i)), {}
+    for i in seq:
+        for b in ops[i]["banks"]:
+            for q, j in users.setdefault(b, {}).items():
+                if q != ops[i]["q"]:
+                    preds[i][j] = True
+            users[b][ops[i]["q"]] = i
     count = {q: 0 for q in QSEM}
     known, fin = {}, [None] * N
     for i in seq:
@@ -586,4 +694,3 @@ def schedule(g, T, ops, queues):
             g.wait_ge(T.sem[QSEM[q]], count[q])
     for sem in LOADS + OUTS:
         g.wait_ge(T.sem[sem], 16)
-    return max(end), order, end

@@ -3,20 +3,22 @@ from concourse.mybir import AluOpType as Op, AxisListType, ActivationFunctionTyp
 
 STEPS = 8
 FL, ZS = 4096, 4352
-LAT, CYC, GAT, SCA, WIN = 0.1, 0.001, 1.56, 3.8, 0.02
-PLAN = {"X": "VSVS", "SIGN": "VSVS", "V": "SVVV", "TAIL": (512, 512), "SMALL": "S"}
-ORDER, ROUNDS, HEAT, SEED = {}, 1500, 0.3, 1
+LAT, CYC, GAT, GAV, SCA = 0.17, 0.00087, 1.56, 1.85, 3.8
+PLAN = {"X": "VVSSVVSS", "SIGN": "VVSSVSSS", "V": "SSVVVVVV", "SMALL": "S", "Q": "S", "A": "V", "U": "V", "WO": "V", "HO": "S", "XO": "VVSS", "L4": "G", "FAR": ((0, 8), (0, 6, 8))}
+FIRST = {"X": "VVSSVVVV", "SIGN": "VVSSVVVV"}
+MORE = 2
+ORDER, ROUNDS, POLISH, HEAT, SEED = {}, 9000, 60, 0.3, 4
 WHEN = dict(x0=0, x1=0.1, x2=2, x3=0.2, gx0=1, gx1=1, gx3=1.1, ab0=2, ab1=3, bb1=3.1, gx2=2.5, ab2=6, ab3=6.1, bb3=6.2, vi0=4, vi1=7, bb0=8.5, bb2=11,
-            row0=9, row1=11.5, pk0=13, pk1=13, vg0=8, vg1=8, vg2=9.5, vg3=10, far0=12, far1=15, sh=12.5, pl=12.6, mv=19, u=19.1, z=19.05, ln=26.5,
-            dd=21.5, sc=24.5, out=40)
+            row0=9, row1=11.5, pk0=13, pk1=13, vg0=8, vg1=8, vg2=9.5, vg3=10, far0=12, far1=15, sh=3, pl=16.5, mv=19, u=19.1, z=19.05, ln=23,
+            dd=20.5, sc=23, out=40, nz=0, st=16, kk=16, cm=12.5, lv=28, hs=34)
 _B = {
-    "bfloat16": "XT 4128 VT 4352 ZW 6656 D 4096 BB 4096 EE 4096 AB 4096 ZIN 2048 CAI 256 RTI 256 CAC 256 "
-                "G1 256 FF 256 HIT 256 LEV0 256 LEV1 256 BSEL 2048 TRI 128 ONE 2048 BLK 128 IDN 128 NEG 128 "
+    "bfloat16": "XT 4128 VT 4352 ZW 6656 D 4096 BB 4096 EE 4096 AB 4096 ZIN 2048 Z4 1024 CAI 256 RTI 256 CAC 256 "
+                "G1 256 FF 256 HIT 256 CR 256 BSEL 2048 TRI 128 ONE 2048 BLK 128 IDN 128 NEG 128 "
                 "I64 128 N64 128 I2K 128 I4K 128 NBG 128 HLF 128 PRM 144 P4K 144 PBG 144 PAR 128 NPAR 128 SM 512 UPQ 256 OFFD 256 YLB 256 LB 1024 L4 256",
-    "float16": "PR 256 NMF 256 NMT 256 SEL 256 THB 128 THC 256 WG 16 FR 256 LH 64",
+    "float16": "PR 256 NMF 256 NMT 256 SEL 256 THB 128 THC 256 WG 16 FR 256 CK 288 LH 64 RL0 256 RL1 256 KH 256 RSA 256",
     "uint16": "WIN 128 WO 128 XO 256 HO 256 ZO 32",
-    "int32": "NMI 256 WTI 1 THI 1 K37 256 T1 256 T2 256 T3 256 QQ 256 V4 256 V5 256 WK 144 LI 1024",
-    "float32": "KC 256 KS 256 CS 256 DC 128 TS 128 RS4 64 RS8 128 AL0 144 AL1 144 W0 144 RSA 256 RSM 256 IO3 256 IO4 256 LVT 256 YL 256 YP 256 LF 1024",
+    "int32": "NMI 256 WTI 1 THI 1 K37 256 T1 256 T2 256 T3 256 QQ 256 V4 256 V5 256 WK 288 LI 1024",
+    "float32": "KC 256 KS 256 CS 256 DC 128 TS 128 RS4 64 RS8 128 AL 288 RSM 256 IO3 256 IO4 256 LVT 256 YL 256 YP 256 LF 1024",
 }
 SCRATCH = {}
 for _t in _B:
@@ -31,6 +33,8 @@ for _i in range(8):
 LOADS = ["lnm", "lwt", "lca", "lx", "lxw", "lz", "lrt", "lth", "lv"]
 OUTS = ["ov", "oz", "ol", "op"]
 SEMAPHORES = ["sv", "ss", "st", "sg", "loc"] + LOADS + OUTS + ["az%d" % s for s in range(1, STEPS)] + ["aw%d" % s for s in range(1, STEPS)]
+SEMAPHORES += [p + "%d_%d" % (s, q) for s in range(STEPS) for q in range(4) for p in "xn"]
+DMA, NET = 3.0, 2.8
 QSEM = {"vector": "sv", "scalar": "ss", "tensor": "st", "gpsimd": "sg"}
 SIZE = {"bfloat16": 2, "float16": 2, "uint16": 2, "float32": 4, "int32": 4}
 
@@ -39,6 +43,22 @@ def rank_program(g, core, T, topo):
     rank = T.rank_of(core)
     if rank is None:
         return
+    ops = operations(g, core, T, topo, STEPS)
+    preds = dependences(ops)
+    if not ORDER:
+        short = operations(g, core, T, topo, 4)
+        at = arrange(short, dependences(short), None, ROUNDS, MORE)[1]
+        when = {(o["step"], o["tag"], o["nth"]): t for o, t in zip(short, at)}
+        period = when[2, "u", 1] - when[1, "u", 1]
+        like = [0, 1] + [2] * (STEPS - 3) + [3]
+        key = [when[like[o["step"]], o["tag"], o["nth"]] + period * (o["step"] - like[o["step"]]) for o in ops]
+        ORDER[0] = arrange(ops, preds, key, POLISH)
+    emit(g, T, ops, preds, ORDER[0][1])
+    g.wait_ge(T.sem.loc, 2 * (STEPS - 1) * len(topo.engines(core, T.cores[(rank + 1) % len(T.cores)])[:8]))
+
+
+def operations(g, core, T, topo, steps):
+    rank = T.rank_of(core)
     n = len(T.cores)
     nxt, prv = T.cores[(rank + 1) % n], T.cores[(rank - 1) % n]
     ops = []
@@ -55,6 +75,8 @@ def rank_program(g, core, T, topo):
         return (name, c0, c1, 1, (a0, a1, sa), 128)
 
     def ap(x):
+        if isinstance(x[5], tuple):
+            return T[x[0]][x[5][0]:x[5][1], x[1]:x[2]:x[3]]
         if x[4] is None:
             return T[x[0]][0:x[5], x[1]:x[2]:x[3]]
         if x[2] - x[1] == 1:
@@ -114,7 +136,8 @@ def rank_program(g, core, T, topo):
         add("vector", lambda: [g.vector.memset(ap(out), c)], [], [out], vcost(width(out) * half(out, out)))
 
     def scan(out, d0, d1, op0, op1):
-        add("vector", lambda: [g.vector.tensor_tensor_scan(ap(out), ap(d0), ap(d1), 0.0, op0, op1)], [d0, d1], [out], vcost(width(out)))
+        add("vector", lambda: [g.vector.tensor_tensor_scan(ap(out), ap(d0), ap(d1), 0.0, op0, op1)], [d0, d1], [out],
+            vcost(width(out) * max(half(out, d0), half(out, d1))))
 
     def turn(out, a):
         add("vector", lambda: [g.vector.transpose(ap(out), ap(a))], [a], [out], vcost(width(out)))
@@ -124,7 +147,9 @@ def rank_program(g, core, T, topo):
             [a] + ([bias] if isinstance(bias, tuple) else []), [out], max(64, width(out)) * CYC)
 
     def lin(out, a, scale=1.0, bias=0.0, eng=None):
-        if (eng or PLAN["SMALL"]) == "S":
+        if eng == "G":
+            asel(out, a, [[0, width(out)]], Op.is_ge, 0, 0)
+        elif (eng or PLAN["SMALL"]) == "S":
             act(out, a, Act.Identity, scale, bias)
         else:
             ts(out, a, scale, Op.mult, bias, Op.add)
@@ -151,25 +176,27 @@ def rank_program(g, core, T, topo):
         eng = g.sync if q == "sync" else g.scalar
         add(q, lambda: [eng.dma_start(out, src)], rd, wr, cost, done=(sem, 16))
 
-    def gather(eng, out, win, lst, minus=None):
+    def gather(eng, out, win, lst, minus=None, scale=1.0):
         if eng == "V":
             add("vector", lambda: [g.vector.tensor_tensor(ap(out), ap(win).indirect(ap(lst)), ap(minus), Op.subtract)], [win, lst, minus], [out],
-                0.05 + GAT * width(out) * CYC)
+                0.05 + GAV * width(out) * CYC)
         else:
-            add("scalar", lambda: [g.scalar.activation(ap(out), ap(win).indirect(ap(lst)), Act.Copy)], [win, lst], [out], 0.065 + GAT * width(out) * CYC)
+            add("scalar", lambda: [g.scalar.activation(ap(out), ap(win).indirect(ap(lst)), Act.Copy, scale=scale)], [win, lst], [out], 0.065 + GAT * width(out) * CYC)
 
     dma("scalar", T.NMI[:], T.nm[:], [], [v("NMI")], "lnm", 2.5)
     dma("scalar", T.ZW[:, ZS:ZS + 256], T.z0[:], [], [v("ZW", ZS, ZS + 256)], "lz", 2.5)
     dma("sync", T.WTI[:], T.wt[:], [], [v("WTI")], "lwt", 2.5)
-    dma("sync", T.XT[:, 0:4096], T.xt[:], [], [v("XT", 0, 4096)], "lx", 8.0)
-    dma("scalar", T.XT[:, 4096:4128], T.xt[:, 0:32], [], [v("XT", 4096, 4128)], "lxw", 3.0)
     dma("sync", T.CAI[:], T.ca[:], [], [v("CAI")], "lca", 2.5)
+    dma("sync", T.XT[:, 0:4096], T.xt[:], [], [v("XT", 0, 4096)], "lx", 6.0)
+    ops[-1]["pre"] = [len(ops) - 3, len(ops) - 2]
+    dma("scalar", T.XT[:, 4096:4128], T.xt[:, 0:32], [], [v("XT", 4096, 4128)], "lxw", 3.0)
     dma("scalar", T.RTI[:], T.rt[:], [], [v("RTI")], "lrt", 2.5)
     dma("scalar", T.THI[:], T.th[:], [], [v("THI")], "lth", 2.5)
-    dma("sync", T.VT[:, 0:4096], T.vt[:], [], [v("VT", 0, 4096)], "lv", 12.0)
+    dma("sync", T.VT[:, 0:4096], T.vt[:], [v("XT", 0, 16)], [v("VT", 0, 4096)], "lv", 6.0)
 
     one, grp = v("ONE", 0, 128), v("BLK", 0, 128, 16)
-    fill(v("ONE"), 1.0)
+    fill(v("ONE", 0, 144), 1.0)
+    fill(v("ONE", 144, 2048), 1.0)
     fill(v("HLF"), -1.0 / 256)
     pI, lI = lane("pI", "LI"), lane("lI", "LI")
     asel(v("IDN"), one, [[-1, 128]], Op.is_equal, 0, 1)
@@ -178,7 +205,7 @@ def rank_program(g, core, T, topo):
     asel(v("UPQ", 0, 128), one, [[-1, 128]], Op.is_equal, -16, 1)
     asel(v("UPQ", 128, 256), one, [[-1, 128]], Op.is_equal, 16, 1)
     iota(v("PAR"), [[0, 4], [1, 2], [0, 16]], 0, 0)
-    iota(v("K37"), [[37, 16], [0, 16]], 0, 0)
+    iota(v("K37"), [[37, 16], [0, 16]], 2048 - 8192, 0)
     iota(pI, [[0, 16]], 0, 1)
     iota(lI, [[16, 16]], 0, 0)
     iota(v("IO3"), [[0, 16], [1, 16]], 0, 0)
@@ -205,7 +232,7 @@ def rank_program(g, core, T, topo):
     ts(v("PBG"), v("PRM"), -8388608.0, Op.mult)
 
     def residue(out, q, src):
-        ts(q, src, 1.0 / 8192, Op.add)
+        lin(q, src, 1.0, 1.0 / 8192, eng=PLAN["Q"])
         tt(out, src, q, Op.subtract)
     u4 = lane("u_0", "LI", 64)
     mms([(v("pb1", 0, 128, p=16), v("ONE", 0, 16), v("HLF"), True, False)] +
@@ -216,29 +243,29 @@ def rank_program(g, core, T, topo):
 
     NB, NK = v("pb7", 0, 256), v("pb7", 256, 512)
     ts(v("NMF"), v("NMI"), -2048.0, Op.add)
-    turn(v("NMT"), v("NMF"))
-    mms([(v("pb2", 2 * b + lhp, 256, 16), smx(gp, lhp), v("NMT", 32 * b + 16 * gp, 32 * b + 16 * gp + 16), gp == 0, gp == 1)
-         for b in range(8) for lhp in range(2) for gp in range(2)])
+    for b in range(8):
+        turn(v("NMT", b, 256, 8), v("NMF", 32 * b, 32 * b + 32))
+    mms([(v("pb2", lhp, 256, 2), smx(gp, lhp), v("NMT", 128 * gp, 128 * gp + 128), gp == 0, gp == 1) for lhp in range(2) for gp in range(2)])
+    tt(v("T3"), v("pb2", 0, 256), v("K37"), Op.add)
     ts(NB, v("pb2", 0, 256), 2048.0, Op.add)
-    tt(v("T3"), NB, v("K37"), Op.add)
-    ts(v("T2"), v("T3"), 4095, Op.bitwise_and)
-    ts(NK, v("T2"), 32.0, Op.mult, -131072.0, Op.add)
-    RTP, CAN = v("pb0", 0, 256), v("pb0", 256, 512)
+    ts(NK, v("T3"), 32.0, Op.mult)
+    CAN = v("pb0", 256, 512)
     for src, tr, bk, to in (("RTI", "RTT", "pb5", "RTB"), ("CAI", "CAT", "pb6", "CAB")):
         turn(v(tr), v(src))
         mms([(v(bk, 128 * lhp, 128 * lhp + 128), smx(gp, lhp), v(tr, 16 * gp, 16 * gp + 16), gp == 0, gp == 1) for lhp in range(2) for gp in range(2)])
         for lhp in range(2):
             act(w(to, lhp, 16, 0, 16, 2), v(bk, 128 * lhp, 128 * lhp + 128), Act.Copy)
-    mms([(RTP, v("IDN"), v("RTB"), True, True), (CAN, v("IDN"), v("CAB"), True, True)])
+    mms([(CAN, v("IDN"), v("CAB"), True, True)])
+    tt(v("CR"), CAN, v("RTB"), Op.add)
+    cp(v("RL0"), v("RTB"))
     ts(v("CAC"), v("CAB"), -1.0, Op.mult, 31.0, Op.add)
     ts(v("KS"), v("CAB"), -64.0, Op.mult)
     fill(v("CB", 0, 1), 4096.0)
     fill(v("CM", 0, 1), 0.0)
     tt(v("CB", 1, 9), v("KS"), v("KC"), Op.add)
     for h in range(2):
-        fill(v("AL%d" % h), 8388608.0)
-        fill(v("AL%d" % h, 1, 144, 9), 0.0)
-    fill(v("LEV0"), 0.0)
+        act(v("CK", h, 288, 2), w("CB", h, 32, 0, 9, 2), Act.Copy)
+    fill(v("AL"), 8388608.0)
     pm, lc, dmp = lane("pm", "LI"), lane("lc", "LI"), lane("dmp", "LF")
     pf, thf = lane("pf", "LF", 1), lane("thf", "LF", 1)
     ts(pm, pI, 15, Op.bitwise_and)
@@ -270,27 +297,27 @@ def rank_program(g, core, T, topo):
     fill(v("HD"), 0.0)
     fill(v("HD", 0, 1), 0.5)
     fill(v("HC"), 0.0)
-    A = None
+    popc = sub(lane("pop", "LB", 24), 0, 17)
+    fill(sub(popc, 16, 17), -15.75 / 128)
+    A = ct = None
     flip = [0]
 
     def minus(src, a, b, other):
         flip[0] ^= 1
         bank = "pb3" if flip[0] else "pb2"
-        lst = [(v(bank, 0, b - a), v("IDN"), v(src, a, b), True, False)]
-        c = 0
-        for i, o in enumerate(other):
-            lst.append((v(bank, c, c + width(o)), v("NEG"), o, False, i == len(other) - 1))
-            c += width(o)
-        mms(lst)
+        mms([(v(bank, 0, b - a), v("NEG"), other, True, False)])
+        mms([(v(bank, 0, b - a), v("IDN"), v(src, a, b), False, True)])
         return v(bank, 0, b - a)
 
-    def sums(out, src, h, rhs, first=None):
+    def sums(out, src, h, rhs, first=None, cuts=(0, 8)):
         lst = [(out, first[0], first[1], True, False)] if first else []
-        mms(lst + [((out[0], out[1] + lp, out[2], 16, None, 128), v(src, 2048 * h + lp, 2048 * h + 2048, 16), rhs, not first, not first or lp == 15)
-                   for lp in range(16)])
+        for k0, k1 in zip(cuts, cuts[1:]):
+            mms(lst + [((out[0], out[1] + lp, out[2], 16, None, (16 * k0, 16 * k1)), v(src, 2048 * h + 256 * k0 + lp, 2048 * h + 256 * k1, 16), rhs,
+                        not first, not first or lp == 15) for lp in range(16)])
+            lst = []
 
-    for s in range(STEPS):
-        par, nxp, last = "_%d" % (s % 2), "_%d" % ((s + 1) % 2), s == STEPS - 1
+    for s in range(steps):
+        par, nxp, last = "_%d" % (s % 2), "_%d" % ((s + 1) % 2), s == steps - 1
 
         def L(name, buf, wd=16):
             return lane(name, buf, wd)
@@ -306,7 +333,7 @@ def rank_program(g, core, T, topo):
                 def fn():
                     g.remote_dma(out_ap=ap(dst), in_ap=ap(src), remote_sem=T.sem[sem], local_sem=T.sem.loc, pid=pid, routing_id=rid, dma_engine_mask=mask)
                     return []
-                add("gpsimd", fn, [src], [], 1.0, done=("none", 0))
+                add("gpsimd", fn, [src], [], 0.5, done=("none", 0))
             zin, win, wo = v("ZIN", 256 * s, 256 * s + 256), v("WIN", 16 * s, 16 * s + 16), v("WO", 16 * s, 16 * s + 16)
             send(zin, z, "az%d" % s)
         for q in range(4):
@@ -316,22 +343,29 @@ def rank_program(g, core, T, topo):
             tt(t1, sub(NB, c0, c1), u, Op.mult)
             tt(t2, sub(NK, c0, c1), t1, Op.add)
             ts(t3, t2, 5, Op.arith_shift_right, 4095, Op.bitwise_and)
-            lin(xo, t3, 1.0, 0.0 if A is None else A, eng=PLAN["X"][q] if PLAN["SMALL"] == "S" else "V")
+            if A is None:
+                lin(xo, t3, eng=PLAN["XO"][q])
+            elif PLAN["XO"][q] == "V":
+                ts(xo, t3, ct, Op.add, A, Op.subtract)
+            else:
+                if PLAN["XO"][:q].count("S") == 0:
+                    act(L("A1", "LF", 1), A, Act.Identity, scale=-1.0, bias=ct)
+                lin(xo, t3, 1.0, L("A1", "LF", 1))
         tag[0] = "sh"
         dd, d2, d3, dp, dt = L("dd", "LB"), L("d2", "LB"), L("d3", "LB"), L("dp", "LF"), L("dt", "LF", 64)
         act(dd, f, Act.Identity, bias=-0.5)
         act(d2, f, Act.Identity, scale=2.0)
-        act(d3, f, Act.Identity, bias=1.0)
         act(dp, f, Act.Sign, bias=-0.5)
         for a, b, src in ((0, 16, f), (16, 32, f)):
             act(sub(dt, a, b), src, Act.Identity, scale=19616.0, bias=9808.0 + 42752)
         act(sub(dt, 32, 64), sub(dt, 0, 32), Act.Copy)
+        tag[0] = "st"
         fa, fb = L("fa", "LI"), L("fb", "LI")
         lin(fa, u1, -1.0, s63)
         ts(fb, fa, 4095, Op.bitwise_and)
         tc, tf, tca, pt = L("tc", "LI"), L("tf", "LF"), L("tca", "LF"), L("pt", "LB")
         if s:
-            ne = 4 if s < 4 else 8
+            ne = 4 if s < steps // 2 else 8
             lin(v("HC", 0, 1), fb)
             dr = v("pb6", 256, 256 + 16 * ne)
             mms([(v("pb6", 256 + e, 256 + 16 * ne, ne // 4), v("IDN"), f4, True, True) for e in range(ne // 4)])
@@ -339,7 +373,7 @@ def rank_program(g, core, T, topo):
             tt(v("DC", 0, 16 * ne), dr, v("HC", 0, ne), Op.mult)
             scan(v("TS", 0, 16 * ne), v("RS%d" % ne), v("DC", 0, 16 * ne), Op.mult, Op.max)
             top = v("TS", ne - 1, 16 * ne, ne)
-            cp(tc, top)
+            lin(tc, top)
             tt(tf, top, tc, Op.subtract)
             act(tca, tf, Act.Identity, scale=64.0)
             act(pt, tf, Act.Identity, scale=-64.0, bias=32.0)
@@ -347,14 +381,15 @@ def rank_program(g, core, T, topo):
             tc = fb
             fill(tca, 0.0)
             fill(pt, 0.0)
-        scan(v("KS"), v("RSA"), RTP, Op.max, Op.min)
+        tag[0] = "cm"
         act(v("CM", 1, 9), CAN, Act.Relu, scale=-1.0)
+        tag[0] = "kk"
+        scan(v("KH"), v("RSA"), v("RL%d" % (s % 2)), Op.max, Op.min)
         kk, kth, kp = L("kk", "LF"), L("kth", "LF"), L("kp", "LF")
-        act(kk, v("KS", 15, 256, 16), Act.Identity, scale=-131072.0, bias=31.0 * 131072 + 65536)
-        act(kth, v("KS", 15, 256, 16), Act.Identity, scale=-131072.0, bias=32.0 * 131072)
+        act(kk, v("KH", 15, 256, 16), Act.Identity, scale=-131072.0, bias=31.0 * 131072 + 65536)
+        act(kth, v("KH", 15, 256, 16), Act.Identity, scale=-131072.0, bias=32.0 * 131072)
         tt(kp, kth, dp, Op.mult)
-        alt = L("alt", "LF")
-        tt(alt, tc, kk, Op.add)
+        tt(v("AL", 2, 288, 18), tc, kk, Op.add)
         act(v("ZW", FL, FL + 256), z, Act.Identity, scale=-1.0, bias=63.0)
         tag[0] = "pl"
         if s:
@@ -369,30 +404,51 @@ def rank_program(g, core, T, topo):
             tt(pd, pb, pc, Op.add)
             ts(pe, pd, 5, Op.arith_shift_right, 4095, Op.bitwise_and)
             lin(ps, pe, 1.0, -2048.0)
+            p1 = L("p1", "LF")
+            lin(p1, pe, 1.0, 1.0)
             tt(ad, pe, dmp, Op.subtract)
             mms([(v("pb6", lp, 256, 16), v("BSEL", 128 * lp, 128 * lp + 128), ps, True, True) for lp in range(16)])
             lin(v("PR"), v("pb6", 0, 256))
         keys = []
+        tag[0] = "nz"
+        z2 = v("ZW", ZS + 256 * s, ZS + 256 * s + 512)
+        asel(sub(z2, 256, 512), z, [[0, 256]], Op.is_ge, 0, 0)
+        if set(PLAN["X"]) & set("DW"):
+            tag[0] = "nz"
+            for i in range(4):
+                dma("sync", T.Z4[:, 256 * i:256 * i + 256], ap(z), [z], [v("Z4", 256 * i, 256 * i + 256)], "n%d_%d" % (s, i), 2.5)
         for h in range(2):
             for q in (2 * h, 2 * h + 1):
                 a, b = 1024 * q, 1024 * q + 1024
                 part("gx", q)
-                if PLAN["X"][q] == "V":
-                    for k in range(4 * q, 4 * q + 4):
-                        gather("V", v("D", 256 * k, 256 * k + 256), v("XT"), v("XO", 16 * k, 16 * k + 16), z)
-                    parts = [(a, a + 512, v("D", a, a + 512)), (a + 512, b, v("D", a + 512, b))]
-                else:
+                who = (PLAN if s else FIRST)["X"][2 * q:2 * q + 2]
+                if who == "SS":
                     gather("S", v("D", a, b), v("XT"), v("XO", 64 * q, 64 * q + 64))
-                    parts = [(a, a + 512, None), (a + 512, b, None)]
-                for a1, b1, d in parts:
-                    d = d or minus("D", a1, b1, [z, z])
+                if who == "DD":
+                    gather("S", v("D", a, b), v("XT"), v("XO", 64 * q, 64 * q + 64), scale=-1.0)
+                    add("gpsimd", lambda a=a, b=b: [g.dma_start(T.D[:, a:b], T.Z4[:], accum_op=Op.add)], [v("Z4"), v("D", a, b)], [v("D", a, b)], DMA,
+                        done=("x%d_%d" % (s, q), 16))
+                if who == "WW":
+                    gather("V", v("D", a, b), v("XT"), v("XO", 64 * q, 64 * q + 64), v("Z4"))
+                for i, a1 in enumerate((a, a + 512)):
+                    b1 = a1 + 512
+                    part("gx", q)
+                    if who[i] in "DW":
+                        d = v("D", a1, b1)
+                    elif who[i] == "V":
+                        d = v("D", a1, b1)
+                        gather("V", d, v("XT"), v("XO", a1 // 16, b1 // 16), z2)
+                    else:
+                        if who != "SS":
+                            gather("S", v("D", a1, b1), v("XT"), v("XO", a1 // 16, b1 // 16))
+                        d = minus("D", a1, b1, z2)
                     part("ab", q)
                     act(v("ZW", a1, b1), d, Act.Abs)
                     part("bb", q)
-                    if PLAN["SIGN"][q] == "S":
-                        act(v("BB", a1, b1), d, Act.Sign, bias=0.5)
+                    if (PLAN if s else FIRST)["SIGN"][2 * q + i] == "S":
+                        act(v("BB", a1, b1), d, Act.Sign, bias=0.5, scale=-1.0 if who[i] == "D" else 1.0)
                     else:
-                        ts(v("BB", a1, b1), d, 0.0, Op.is_ge, -0.5, Op.add)
+                        ts(v("BB", a1, b1), d, 0.0, Op.is_le if who[i] == "D" else Op.is_ge, -0.5, Op.add)
             c0, c1 = 128 * h, 128 * h + 128
             part("vi", h)
             bk = ("pb1", "pb4")[h]
@@ -404,54 +460,59 @@ def rank_program(g, core, T, topo):
             for c in (0, 64):
                 tt(v("V4", c0 + c, c0 + c + 64), sub(ub, c, c + 64), dt, Op.add)
             ts(v("V5", c0, c1), v("V4", c0, c1), 5, Op.arith_shift_right, 4095, Op.bitwise_and)
-            lin(v("HO", c0, c1), v("V5", c0, c1))
+            lin(v("HO", c0, c1), v("V5", c0, c1), eng=PLAN["HO"])
             part("row", h)
             sums(rw, "BB", h, grp)
             act(v("G1", c0, c1), rw, Act.Relu, scale=-1.0)
             part("pk", h)
-            key = v(("pb1", "pb5")[h], 0, 144)
-            keys.append([(key, v("I2K"), w("CB", h, 32, 0, 9, 2), True, False), (key, v("NBG"), w("CM", h, 32, 0, 9, 2), False, False),
-                         (key, fr, v("P4K"), False, False), (key, v("G1", c0, c1), v("PBG"), False, False)])
-        mms(keys[1])
+            key = v("pb5", h, 288, 2)
+            keys.append(key)
+            mms(([] if h else [(v("pb5", 0, 288), v("I2K"), v("CK"), True, False)]) + [(key, fr, v("P4K"), False, False)])
+            mms([(key, v("G1", c0, c1), v("PBG"), False, False)])
         for h in range(2):
             for q in (2 * h, 2 * h + 1):
                 a = 1024 * q
                 part("vg", q)
-                if PLAN["V"][q] == "S":
+                who = PLAN["V"][2 * q:2 * q + 2]
+                if who == "SS":
                     gather("S", v("EE", a, a + 1024), v("VT", 0, 4096), v("HO", 64 * q, 64 * q + 64))
-                for wd in (PLAN["TAIL"] if q == 3 else (1024,)) if PLAN["V"][q] == "V" else (512, 512):
+                for i, wd in enumerate((1024,) if who == "VV" and q < 3 else (512, 512)):
                     b = a + wd
-                    if PLAN["V"][q] == "V":
+                    if who[i] == "V":
                         e = v("EE", a, b)
                         gather("V", e, v("VT", 0, 4096), v("HO", a // 16, b // 16), v("ZW", a, b))
                     else:
-                        e = minus("EE", a, b, [v("ZW", a, b)])
+                        if who != "SS":
+                            gather("S", v("EE", a, b), v("VT", 0, 4096), v("HO", a // 16, b // 16))
+                        e = minus("EE", a, b, v("ZW", a, b))
                     act(v("AB", a, b), e, Act.Abs)
                     a = b
             part("far", h)
             c0, c1 = 128 * h, 128 * h + 128
             fc = v(("pb1", "pb4")[h], 384, 512)
-            sums(fc, "AB", h, grp, (v("IDN"), v("THC", c0, c1)))
+            sums(fc, "AB", h, grp, (v("IDN"), v("THC", c0, c1)), PLAN["FAR"][h])
             act(v("FF", c0, c1), fc, Act.Relu, scale=-1.0, bias=1.0)
-            key = keys[h][0][0]
-            mms(([] if h else keys[0]) + [(key, v("FF", c0, c1), v("PBG"), False, True)])
-            scan(v(("W0", "WK")[h]), v("AL%d" % h), key, Op.min, Op.max)
-            if not h:
-                tt(v("AL1", 1, 144, 9), v("W0", 8, 144, 9), alt, Op.max)
-        W = v("WK", 8, 144, 9)
+            key = keys[h]
+            mms([(key, v("NBG"), w("CM", h, 32, 0, 9, 2), False, False)])
+            mms([(key, v("FF", c0, c1), v("PBG"), False, h == 1)])
+        scan(v("WK"), v("AL"), v("pb5", 0, 288), Op.min, Op.max)
+        W = v("WK", 17, 288, 18)
         tag[0] = "mv"
-        pop, m = L("pop", "LB"), L("m", "LB")
+        pop, m = sub(popc, 0, 16), L("m", "LB")
         tt(pop, W, kp, Op.is_lt)
         if s and not last:
-            cn, ct, am, A = v("pb1", 0, 16), L("ct", "LF", 1), L("am", "LI", 1), L("A", "LF", 1)
-            mms([(cn, one, pop, True, True)])
-            add("vector", lambda ct=ct, cn=cn: [g.vector.tensor_reduce(ap(ct), ap(cn), AxisListType.X, Op.add)], [cn], [ct], 64 * CYC)
-            ts(am, ct, 1.0 / 32, Op.mult, -0.484375, Op.add)
-            ts(A, am, -32.0, Op.mult, ct, Op.add)
+            cn, ct, cm, A = v("pb1", 0, 17), L("ct", "LF", 1), L("cm", "LF", 1), L("A", "LF", 1)
+            mms([(cn, one, popc, True, True)])
+            for out, src in ((cm, cn), (ct, sub(cn, 0, 16))):
+                add("vector", lambda out=out, src=src: [g.vector.tensor_reduce(ap(out), ap(src), AxisListType.X, Op.add)], [src], [out], 64 * CYC)
+            ts(A, cm, 402653184.0, Op.add, -402653184.0, Op.add)
         tag[0] = "u"
         if not last:
-            for i in range(4):
-                ts(sub(lane("u" + nxp, "LI", 64), 16 * i, 16 * i + 16), W, 4095, Op.bitwise_and)
+            un = lane("u" + nxp, "LI", 64)
+            for i in range(4 if PLAN["U"] == "V" else 2):
+                ts(sub(un, 16 * i, 16 * i + 16), W, 4095, Op.bitwise_and)
+            if PLAN["U"] != "V":
+                lin(sub(un, 32, 64), sub(un, 0, 32))
         tag[0] = "z"
         za, zb, zo = L("za", "LI"), L("zb", "LI"), v("ZO", 16 * (s % 2), 16 * (s % 2) + 16)
         ts(za, W, 4, Op.arith_shift_right, 0x1F00, Op.bitwise_and)
@@ -473,28 +534,31 @@ def rank_program(g, core, T, topo):
         tt(pn, pop, pt, Op.mult)
         act(f, dl, Act.Abs, bias=0.5)
         for i in range(4):
-            act(v("L4", i, 256, 4), L3, Act.Copy)
-        tp, dlp = v("pb5", 256, 512), v("pb5", 0, 256)
-        mms([(v("pb5", 256 + i, 512, 4), v("IDN"), tau4, True, True) for i in range(4)] + [(v("pb5", i, 256, 4), v("IDN"), dl4, True, True) for i in range(4)])
-        lv = v("LEV%d" % ((s + 1) % 2))
+            if PLAN["L4"] == "S":
+                act(v("L4", i, 256, 4), L3, Act.Copy)
+            else:
+                asel(v("L4", i, 256, 4), L3, [[0, 64]], Op.is_ge, 0, 0)
+        tag[0] = "lv"
+        tp, dlp = v("pb0", 256, 512), v("pb0", 0, 256)
+        mms([(v("pb0", 256 + i, 512, 4), v("IDN"), tau4, True, True) for i in range(4)] + [(v("pb0", i, 256, 4), v("I64"), dl4, True, True) for i in range(4)])
+        lv = v("RL%d" % ((s + 1) % 2))
         tt(v("HIT"), v("CAC"), tp, Op.is_equal)
         tt(dlp, v("HIT"), dlp, Op.mult)
-        tt(lv, v("LEV%d" % (s % 2)), dlp, Op.add)
+        tt(lv, v("RL%d" % (s % 2)), dlp, Op.add)
         if not last:
-            mms([(RTP, v("IDN"), v("RTB"), True, False), (RTP, v("I64"), lv, False, True),
-                 (CAN, v("IDN"), v("CAB"), True, False), (CAN, v("N64"), lv, False, False)] +
+            mms([(CAN, v("IDN"), v("CR"), True, False), (CAN, v("NEG"), lv, False, False)] +
                 [(v("pb0", 256 + i, 512, 4), v("NEG"), pn4, False, i == 3) for i in range(4)])
+            tag[0] = "hs"
             ca_ = L("ca_", "LF")
-            tt(v("HD", s + 1, s + 2), m, d3, Op.mult)
+            tt(v("HD", s + 1, s + 2), m, f, Op.mult)
             lin(ca_, hi, 1.0 / 64, (s + 1) * 4096.0)
             tt(v("HC", s + 1, s + 2), ca_, u1, Op.add)
         tag[0] = "dd"
         if s:
-            sx, sc = L("sx", "LF"), L("sc", "LF")
-            act(sx, pop, Act.Identity, scale=-9999.0, bias=9999.0)
-            tt(sc, sx, ps, Op.add)
+            sc = L("sc", "LF")
+            tt(sc, pop, p1, Op.mult)
             for lh in range(16):
-                ts(w("CMP", lh, lh + 1, 0, 256 - 16 * lh), v("PR", 16 * lh, 256), sub(sc, lh, lh + 1), Op.is_equal)
+                ts(w("CMP", lh, lh + 1, 0, 256 - 16 * lh), v("PR", 16 * lh, 256), 2049.0, Op.add, sub(sc, lh, lh + 1), Op.is_equal)
             cnt = v("pb6", 0, 256)
             mms([(cnt, v("IDN"), v("OFFD"), True, False)])
             for lh in range(15):
@@ -505,7 +569,7 @@ def rank_program(g, core, T, topo):
             tt(wn, v("CS", 15, 256, 16), pop, Op.is_lt)
             tt(wa, wn, ad, Op.mult)
             tt(wb, wa, dmp, Op.add)
-            lin(wo, wb, eng="V")
+            lin(wo, wb, eng=PLAN["WO"])
             send(win, wo, "aw%d" % s)
             tag[0] = "sc"
 
@@ -514,7 +578,7 @@ def rank_program(g, core, T, topo):
             snd = len(ops) - 1
             scat(wo, z)
             ne = len(topo.engines(prv, core)[:8])
-            add("net", None, [], [win, zin], 3.0, [("az%d" % s, ne), ("aw%d" % s, ne)], [snd])
+            add("net", None, [], [win, zin], NET, [("az%d" % s, ne), ("aw%d" % s, ne)], [snd])
             scat(win, zin)
     tag[0] = "out"
     dma("sync", T.yv[:], T.VT[:, 0:4096], [v("VT")], [], "ov", 8.0)
@@ -522,24 +586,27 @@ def rank_program(g, core, T, topo):
         [v("BSEL"), pn], [v("pb1", 0, 256)], 1.0)
     add("vector", lambda: [g.vector.tensor_scalar(T.YP[0:8, :], T.pb1[0:8, 0:256], -1.0, None, Op.add)], [v("pb1", 0, 256)], [v("YP")], 0.22)
     dma("sync", T.yp[:], T.YP[0:8, :], [v("YP")], [], "op", 2.5)
-    cp(v("LV3"), lv)
+    mms([(CAN, v("IDN"), lv, True, False), (CAN, v("NEG"), v("RTB"), False, True)])
+    act(v("LV3"), CAN, Act.Copy, scale=1.0 / 64)
     mms([(v("pb0", 128 * gp, 128 * gp + 128), smx(lhp, gp), w("LV3", lhp, 16, 0, 16, 2), lhp == 0, lhp == 1) for gp in range(2) for lhp in range(2)])
     for gp in range(2):
         act(v("CAT", 16 * gp, 16 * gp + 16), v("pb0", 128 * gp, 128 * gp + 128), Act.Copy)
     turn(v("YLB"), v("CAT"))
     dma("scalar", T.yl[:], T.YLB[:], [v("YLB")], [], "ol", 2.5)
-    queues = {"vector": g.vector, "scalar": g.scalar, "tensor": g.tensor, "gpsimd": g, "sync": g.sync}
-    schedule(g, T, ops, queues)
-    g.wait_ge(T.sem.loc, 2 * (STEPS - 1) * len(topo.engines(core, nxt)[:8]))
+    nth = {}
+    for o in ops:
+        k = (o["step"], o["tag"])
+        o["nth"] = nth[k] = nth.get(k, 0) + 1
+    return ops
 
 
-def schedule(g, T, ops, queues):
+def dependences(ops):
     N = len(ops)
     preds = [dict() for _ in range(N)]
     hist, bank = {}, {}
     for i, o in enumerate(ops):
         for p in o["pre"]:
-            preds[i][p] = o["q"] != "net"
+            preds[i][p] = o["q"] not in ("net", "sync")
         o["banks"] = sorted(set(x[0][:3] for x in o["rd"] + o["wr"] if SCRATCH[x[0]][0] == "psum"))
         for kind, regs in (("r", o["rd"]), ("w", o["wr"])):
             for x in regs:
@@ -550,7 +617,7 @@ def schedule(g, T, ops, queues):
                         need = not same or (k2 == "w" and not (o["q"] == "tensor" and SCRATCH[x[0]][0] == "psum"))
                         preds[i][j] = preds[i].get(j, False) or need
         if o["q"] == "tensor":
-            for b in set(o["banks"]) & {"pb5", "pb6"}:
+            for b in set(o["banks"]) & {"pb2", "pb3", "pb4", "pb5", "pb6"}:
                 if b in bank:
                     preds[i].setdefault(bank[b], False)
                 bank[b] = i
@@ -561,7 +628,12 @@ def schedule(g, T, ops, queues):
                 if kind == "w" and x[3] == 1 and sa == 1 and x[5] == 128:
                     h[:] = [y for y in h if not (x[1] <= y[2] and y[3] <= x[2] and a0 <= y[4] and y[5] <= a1 and y[0] != i)]
                 h.append((i, kind, x[1], x[2], a0, a1, x[3]))
-    occ = [0.0 if o["q"] == "net" else 0.1 if o["done"] and o["done"][1] else o["cost"] for o in ops]
+    return preds
+
+
+def arrange(ops, preds, key, rounds, more=0):
+    N = len(ops)
+    occ = [0.0 if o["q"] == "net" else (1.0 if o["q"] == "gpsimd" else 0.1) if o["done"] and o["done"][1] else o["cost"] for o in ops]
     fw = [[(j, ops[j]["cost"] + LAT if c or ops[j]["q"] != ops[i]["q"] else occ[j]) for j, c in preds[i].items()] for i in range(N)]
     bw = [[] for _ in range(N)]
     for i in range(N):
@@ -570,82 +642,115 @@ def schedule(g, T, ops, queues):
 
     lines = [[(o["q"], 0.0)] + [(b + e, LAT) for b in o["banks"] for e in ("vector", "scalar", "tensor") if e != o["q"]] for o in ops]
     holds = [[o["q"]] + [b + o["q"] for b in o["banks"]] for o in ops]
-
-    def after(lst, t):
-        a, b = 0, len(lst)
-        while a < b:
-            c = (a + b) // 2
-            a, b = (c + 1, b) if lst[c][1] <= t else (a, c)
-        return a
+    every = set(r for l in lines for r, _ in l) | set(r for l in holds for r in l)
 
     def place(edges, key):
-        at, busy, done = [0.0] * N, {}, [False] * N
-        stack = sorted(range(N), key=key, reverse=True)
+        at, busy = [-1.0] * N, {r: [(-9.0, -9.0)] for r in every}
+        stack = sorted(range(N), key=key.get, reverse=True)
         while stack:
-            i = stack[-1]
-            late = [j for j, _ in edges[i] if not done[j]]
+            i = stack.pop()
+            if at[i] >= 0:
+                continue
+            t, late = 0.0, []
+            for j, dly in edges[i]:
+                a = at[j]
+                if a < 0:
+                    late.append(j)
+                elif a + dly > t:
+                    t = a + dly
             if late:
-                stack += sorted(late, key=key, reverse=True)
+                stack.append(i)
+                stack += sorted(late, key=key.get, reverse=True)
                 continue
-            stack.pop()
-            if done[i]:
-                continue
-            t, d = max([at[j] + dly for j, dly in edges[i]] + [0.0]), occ[i]
+            d = occ[i]
             moved = d > 0
             while moved:
                 moved = False
                 for r, pad in lines[i]:
-                    lst = busy.get(r)
-                    if lst and lst[-1][1] + pad > t:
-                        c = after(lst, t - pad + 1e-9)
-                        while c < len(lst) and lst[c][0] < t + d + pad - 1e-9:
-                            t, moved, c = lst[c][1] + pad, len(lines[i]) > 1, c + 1
+                    lst = busy[r]
+                    c = len(lst) - 1
+                    if lst[c][1] + pad > t + 1e-9:
+                        while lst[c - 1][1] + pad > t + 1e-9:
+                            c -= 1
+                        for a, b in lst[c:]:
+                            if a >= t + d + pad - 1e-9:
+                                break
+                            t, moved = b + pad, True
             for r in holds[i]:
-                lst = busy.setdefault(r, [])
-                if not lst or lst[-1][1] <= t + 1e-9:
-                    lst.append((t, t + d))
-                else:
-                    lst.insert(after(lst, t + 1e-9), (t, t + d))
-            at[i], done[i] = t, True
+                lst = busy[r]
+                c = len(lst)
+                while lst[c - 1][1] > t + 1e-9:
+                    c -= 1
+                lst.insert(c, (t, t + d))
+            at[i] = t
         return at
 
-    def arrange():
-        prio = [0.0] * N
-        for i in range(N - 1, -1, -1):
-            prio[i] = max([prio[x] + dly + occ[i] - occ[x] for x, dly in bw[i]] + [ops[i]["cost"]])
-        top = max(prio) - 12
-        key = [20.0 * o["step"] + WHEN[o["tag"]] if o["tag"] in WHEN else top - prio[i] for i, o in enumerate(ops)]
-        twins, nth = {}, {}
-        for i, o in enumerate(ops):
-            k = (o["step"], o["tag"])
-            nth[k] = nth.get(k, 0) + 1
-            twins.setdefault((o["tag"], nth[k]), []).append(i)
-        names, seed, cur, best = list(twins), [SEED], None, None
+    prio = [0.0] * N
+    for i in range(N - 1, -1, -1):
+        prio[i] = max([prio[x] + dly + occ[i] - occ[x] for x, dly in bw[i]] + [ops[i]["cost"]])
+    top = max(prio)
+    key = key or [20.0 * o["step"] + WHEN[o["tag"]] if o["tag"] in WHEN else top - 12 - prio[i] for i, o in enumerate(ops)]
+    twins = {}
+    for i, o in enumerate(ops):
+        twins.setdefault((o["tag"], o["nth"]), []).append(i)
+    names, seed, cur, best, marks = list(twins), [SEED], None, None, twins["u", 1]
 
-        def rnd():
-            seed[0] = (seed[0] * 1103515245 + 12345) % 2147483648
-            return seed[0] / 2147483648.0
-        for n in range(ROUNDS + 1):
-            at = place(fw, lambda i: (key[i], i))
-            span = max(at[i] + ops[i]["cost"] for i in range(N))
-            if cur is None or span <= cur[0] - HEAT * (1.001 - n / ROUNDS) * math.log(rnd() + 1e-9):
-                cur = (span, at)
-                best = cur if best is None or span < best[0] else best
-            key = list(cur[1])
-            if rnd() < 0.15:
-                back = place(bw, lambda i: (-key[i] - occ[i], -i))
-                key = [-back[i] - occ[i] for i in range(N)]
-                continue
-            for _ in range(1 << int(4 * rnd())):
-                name, k = names[int(rnd() * len(names))]
-                shift = (rnd() + rnd() - 1) * (0.7, 2.5, 7.0)[int(3 * rnd())]
-                for j in range((1, 1, 2, 4)[int(4 * rnd())]):
-                    for i in twins.get((name, k + j), ()):
-                        key[i] += shift
-        return best + (max(prio),)
-    if N not in ORDER:
-        ORDER[N] = arrange()
-    at = ORDER[N][1]
+    def blocked(at):
+        ends = {}
+        for i in range(N):
+            for r in holds[i]:
+                ends[r, round(at[i] + occ[i], 4)] = i
+        i, out = max(range(N), key=lambda x: at[x] + ops[x]["cost"]), []
+        while at[i] > 1e-6:
+            j = next((j for j, dly in fw[i] if abs(at[j] + dly - at[i]) < 1e-6), None)
+            if j is None:
+                j = next((ends[r, round(at[i] - pad, 4)] for r, pad in lines[i] if (r, round(at[i] - pad, 4)) in ends), None)
+                if j is None or j == i:
+                    break
+                out.append((i, j))
+            i = j
+        return out
+
+    def rnd():
+        seed[0] = (seed[0] * 1103515245 + 12345) % 2147483648
+        return seed[0] / 2147483648.0
+    for n in range(rounds + 1):
+        at = place(fw, {i: k + 1e-7 * i for i, k in enumerate(key)})
+        span = max(at[i] + ops[i]["cost"] for i in range(N)) + more * (at[marks[2]] - at[marks[1]])
+        if cur is None or span <= cur[0] - HEAT * (1.001 - n / rounds) * math.log(rnd() + 1e-9):
+            cur = (span, at)
+            best = cur if best is None or span < best[0] else best
+            swaps = blocked(at)
+        key = list(cur[1])
+        if swaps and rnd() < 0.5:
+            i, j = swaps[int(rnd() * len(swaps))]
+            shift = key[i] - key[j] + 0.01
+            move, sign = (i, -1) if rnd() < 0.6 else (j, 1)
+            for x in twins[ops[move]["tag"], ops[move]["nth"]]:
+                key[x] += sign * shift
+            continue
+        if rnd() < 0.15:
+            back = place(bw, {i: -k - occ[i] - 1e-7 * i for i, k in enumerate(key)})
+            key = [-back[i] - occ[i] for i in range(N)]
+            continue
+        if rnd() < 0.2:
+            name, shift = names[int(rnd() * len(names))][0], (rnd() + rnd() - 1) * 8
+            for i, o in enumerate(ops):
+                if o["tag"] == name:
+                    key[i] += shift
+            continue
+        for _ in range(1 << int(4 * rnd())):
+            name, k = names[int(rnd() * len(names))]
+            shift = (rnd() + rnd() - 1) * (0.7, 2.5, 7.0)[int(3 * rnd())]
+            for j in range((1, 1, 2, 4)[int(4 * rnd())]):
+                for i in twins.get((name, k + j), ()):
+                    key[i] += shift
+    return best + (top,)
+
+
+def emit(g, T, ops, preds, at):
+    N = len(ops)
+    queues = {"vector": g.vector, "scalar": g.scalar, "tensor": g.tensor, "gpsimd": g, "sync": g.sync}
     seq, users = sorted(range(N), key=lambda i: (at[i], i)), {}
     for i in seq:
         for b in ops[i]["banks"]:

@@ -3,19 +3,19 @@ from concourse.mybir import AluOpType as Op, AxisListType, ActivationFunctionTyp
 
 STEPS = 8
 FL, ZS = 4096, 4352
-LAT, CYC, GAT, GAV, SCA = 0.17, 0.00087, 1.56, 1.85, 3.8
-PLAN = {"X": "VVSSVVSS", "SIGN": "VVSSVSSS", "V": "SSVVVVVV", "SMALL": "S", "Q": "S", "A": "V", "U": "V", "WO": "V", "HO": "S", "XO": "VVSS", "L4": "G", "FAR": ((0, 8), (0, 6, 8))}
-FIRST = {"X": "VVSSVVVV", "SIGN": "VVSSVVVV"}
+LAT, CYC, GAT, GAV, SCA = 0.21, 0.00084, 1.56, 1.62, 3.8
+PLAN = {"X": "VsVsVsVs", "SIGN": "VSVSVSVS", "V": "sVsVVVVV", "SMALL": "S", "Q": "V", "A": "V", "U": "V", "WO": "T", "SC": 16, "HO": "S", "TAIL": (512, 256, 256), "XO": "VVVV", "L4": "G", "FAR": ((0, 8), (0, 6, 8))}
+FIRST = {"X": "VsVsVsVV", "SIGN": "VSVSVSVV"}
 MORE = 2
-ORDER, ROUNDS, POLISH, HEAT, SEED = {}, 9000, 60, 0.3, 4
+ORDER, ROUNDS, POLISH, HEAT, SEED = {}, 11000, 60, 0.35, 21
 WHEN = dict(x0=0, x1=0.1, x2=2, x3=0.2, gx0=1, gx1=1, gx3=1.1, ab0=2, ab1=3, bb1=3.1, gx2=2.5, ab2=6, ab3=6.1, bb3=6.2, vi0=4, vi1=7, bb0=8.5, bb2=11,
             row0=9, row1=11.5, pk0=13, pk1=13, vg0=8, vg1=8, vg2=9.5, vg3=10, far0=12, far1=15, sh=3, pl=16.5, mv=19, u=19.1, z=19.05, ln=23,
             dd=20.5, sc=23, out=40, nz=0, st=16, kk=16, cm=12.5, lv=28, hs=34)
 _B = {
     "bfloat16": "XT 4128 VT 4352 ZW 6656 D 4096 BB 4096 EE 4096 AB 4096 ZIN 2048 Z4 1024 CAI 256 RTI 256 CAC 256 "
-                "G1 256 FF 256 HIT 256 CR 256 BSEL 2048 TRI 128 ONE 2048 BLK 128 IDN 128 NEG 128 "
+                "G1 256 FF 256 HIT 256 CR 256 B4 512 TRI 128 TR8 128 BL8 128 ONE 144 BLK 128 IDN 128 NEG 128 "
                 "I64 128 N64 128 I2K 128 I4K 128 NBG 128 HLF 128 PRM 144 P4K 144 PBG 144 PAR 128 NPAR 128 SM 512 UPQ 256 OFFD 256 YLB 256 LB 1024 L4 256",
-    "float16": "PR 256 NMF 256 NMT 256 SEL 256 THB 128 THC 256 WG 16 FR 256 CK 288 LH 64 RL0 256 RL1 256 KH 256 RSA 256",
+    "float16": "PR 256 NMF 256 NMT 256 SEL 256 THB 128 THC 256 WG 16 FR 256 CK 288 PS4 64 LH 64 RL0 256 RL1 256 KH 256 RSA 256",
     "uint16": "WIN 128 WO 128 XO 256 HO 256 ZO 32",
     "int32": "NMI 256 WTI 1 THI 1 K37 256 T1 256 T2 256 T3 256 QQ 256 V4 256 V5 256 WK 288 LI 1024",
     "float32": "KC 256 KS 256 CS 256 DC 128 TS 128 RS4 64 RS8 128 AL 288 RSM 256 IO3 256 IO4 256 LVT 256 YL 256 YP 256 LF 1024",
@@ -195,8 +195,7 @@ def operations(g, core, T, topo, steps):
     dma("sync", T.VT[:, 0:4096], T.vt[:], [v("XT", 0, 16)], [v("VT", 0, 4096)], "lv", 6.0)
 
     one, grp = v("ONE", 0, 128), v("BLK", 0, 128, 16)
-    fill(v("ONE", 0, 144), 1.0)
-    fill(v("ONE", 144, 2048), 1.0)
+    fill(v("ONE"), 1.0)
     fill(v("HLF"), -1.0 / 256)
     pI, lI = lane("pI", "LI"), lane("lI", "LI")
     asel(v("IDN"), one, [[-1, 128]], Op.is_equal, 0, 1)
@@ -213,7 +212,6 @@ def operations(g, core, T, topo, steps):
     iota(v("KC"), [[0, 16], [2, 16]], 1985, 0)
     asel(v("PRM"), v("ONE", 0, 144), [[-1, 16], [-16, 9]], Op.is_equal, 16, 1)
     asel(v("TRI"), v("BLK"), [[1, 128]], Op.is_ge, -1, -1)
-    asel(v("BSEL"), v("ONE"), [[-1, 16], [-16, 8], [0, 16]], Op.is_equal, 0, 1)
     ts(v("NPAR"), v("PAR"), -1.0, Op.mult, 1.0, Op.add)
 
     def smx(gp, lhp):
@@ -273,11 +271,27 @@ def operations(g, core, T, topo, steps):
     ts(dmp, lc, 4096.0, Op.add)
     cp(pf, sub(pm, 0, 1))
     cp(thf, v("THI"))
+    lo, up, mlo, mup = lane("lo", "LI", 1), lane("up", "LI", 1), lane("mlo", "LF", 4), lane("mup", "LF", 4)
+    ts(lo, sub(pm, 0, 1), 3, Op.bitwise_and)
+    ts(up, sub(pm, 0, 1), 2, Op.arith_shift_right)
+    for a in range(4):
+        ts(sub(mlo, a, a + 1), lo, float(a), Op.is_equal)
+        ts(sub(mup, a, a + 1), up, float(a), Op.is_equal)
+        ts(v("B4", 128 * a, 128 * a + 128), v("BLK"), sub(mlo, a, a + 1), Op.mult)
+
+    def quarters(out, x):
+        for j in range(4):
+            o, c = (out[0], j, 64, 4, None, 128), sub(mup, j, j + 1)
+            add("scalar", lambda o=o, c=c: [g.scalar.activation(ap(o), ap(x), Act.Copy, scale=ap(c))], [x, c], [o], 64 * CYC)
     ts(v("SEL"), v("IO4"), pf, Op.is_equal)
     ts(v("THB"), v("BLK"), thf, Op.mult)
     mms([(v("pb4", 128 * h, 128 * h + 128), v("SEL", 128 * h, 128 * h + 128), v("THB"), True, True) for h in range(2)])
-    ts(v("THC"), v("pb4", 0, 256), -1.0, Op.mult)
-    ts(v("OFFD"), v("IO3"), pf, Op.not_equal, -1000.0, Op.mult)
+    act(v("THC"), v("pb4", 0, 256), Act.Copy)
+    ts(v("CS"), v("IO3"), pf, Op.not_equal, -4194304.0 - 10240, Op.mult)
+    ts(v("OFFD"), v("CS"), 10240.0, Op.add)
+    tt(v("UPQ", 0, 128), v("TRI"), v("IDN"), Op.subtract)
+    ts(v("TR8"), v("UPQ", 0, 128), 8192.0, Op.mult)
+    ts(v("BL8"), v("BLK"), 8192.0, Op.mult)
     ts(v("RSM"), v("IO3"), 0.0, Op.is_gt)
     ts(v("RSA"), v("RSM"), -1001.0, Op.mult, 1000.0, Op.add)
     for ne in (4, 8):
@@ -394,7 +408,7 @@ def operations(g, core, T, topo, steps):
         tag[0] = "pl"
         if s:
             pb, pc, pd, pe = L("pb", "LF"), L("pc", "LF"), L("pd", "LI"), L("pe", "LI")
-            ps, ad = L("ps", "LH"), L("ad", "LF")
+            ps = L("ps", "LH")
             if PLAN["SMALL"] == "S":
                 act(pb, u1, Act.Square, bias=592.0)
             else:
@@ -405,10 +419,12 @@ def operations(g, core, T, topo, steps):
             ts(pe, pd, 5, Op.arith_shift_right, 4095, Op.bitwise_and)
             lin(ps, pe, 1.0, -2048.0)
             p1 = L("p1", "LF")
-            lin(p1, pe, 1.0, 1.0)
-            tt(ad, pe, dmp, Op.subtract)
-            mms([(v("pb6", lp, 256, 16), v("BSEL", 128 * lp, 128 * lp + 128), ps, True, True) for lp in range(16)])
-            lin(v("PR"), v("pb6", 0, 256))
+            lin(p1, pe, 1.0, 1.0, eng=PLAN["Q"])
+            quarters(v("PS4"), ps)
+            mms([(v("pb6", 256 + a, 512, 4), v("B4", 128 * a, 128 * a + 128), v("PS4"), True, True) for a in range(4)])
+            lin(v("PR"), v("pb6", 256, 512))
+            mms([(v("pb6", 0, 256), v("IDN"), v("OFFD"), True, False)] + [(v("pb6", i, 256, 4), v("IDN"), v("PS4"), False, False) for i in range(4)])
+            ops[-1]["rd"].append(v("PR"))
         keys = []
         tag[0] = "nz"
         z2 = v("ZW", ZS + 256 * s, ZS + 256 * s + 512)
@@ -445,7 +461,7 @@ def operations(g, core, T, topo, steps):
                     part("ab", q)
                     act(v("ZW", a1, b1), d, Act.Abs)
                     part("bb", q)
-                    if (PLAN if s else FIRST)["SIGN"][2 * q + i] == "S":
+                    if (PLAN if s else FIRST)["SIGN"][2 * q + i] in "Ss":
                         act(v("BB", a1, b1), d, Act.Sign, bias=0.5, scale=-1.0 if who[i] == "D" else 1.0)
                     else:
                         ts(v("BB", a1, b1), d, 0.0, Op.is_le if who[i] == "D" else Op.is_ge, -0.5, Op.add)
@@ -476,9 +492,9 @@ def operations(g, core, T, topo, steps):
                 who = PLAN["V"][2 * q:2 * q + 2]
                 if who == "SS":
                     gather("S", v("EE", a, a + 1024), v("VT", 0, 4096), v("HO", 64 * q, 64 * q + 64))
-                for i, wd in enumerate((1024,) if who == "VV" and q < 3 else (512, 512)):
+                for i, wd in enumerate((1024,) if who == "VV" and q < 3 else PLAN["TAIL"] if who == "VV" else (512, 512)):
                     b = a + wd
-                    if who[i] == "V":
+                    if who == "VV" or who[i] in "Vv":
                         e = v("EE", a, b)
                         gather("V", e, v("VT", 0, 4096), v("HO", a // 16, b // 16), v("ZW", a, b))
                     else:
@@ -490,8 +506,8 @@ def operations(g, core, T, topo, steps):
             part("far", h)
             c0, c1 = 128 * h, 128 * h + 128
             fc = v(("pb1", "pb4")[h], 384, 512)
-            sums(fc, "AB", h, grp, (v("IDN"), v("THC", c0, c1)), PLAN["FAR"][h])
-            act(v("FF", c0, c1), fc, Act.Relu, scale=-1.0, bias=1.0)
+            sums(fc, "AB", h, grp, None, PLAN["FAR"][h])
+            tt(v("FF", c0, c1), fc, v("THC", c0, c1), Op.is_le)
             key = keys[h]
             mms([(key, v("NBG"), w("CM", h, 32, 0, 9, 2), False, False)])
             mms([(key, v("FF", c0, c1), v("PBG"), False, h == 1)])
@@ -516,8 +532,11 @@ def operations(g, core, T, topo, steps):
         tag[0] = "z"
         za, zb, zo = L("za", "LI"), L("zb", "LI"), v("ZO", 16 * (s % 2), 16 * (s % 2) + 16)
         ts(za, W, 4, Op.arith_shift_right, 0x1F00, Op.bitwise_and)
-        tt(zb, za, lc, Op.add)
-        lin(zo, zb)
+        if PLAN["WO"] == "T":
+            tt(zo, za, lc, Op.add)
+        else:
+            tt(zb, za, lc, Op.add)
+            lin(zo, zb)
         zn = v("ZW", ZS + 256 * (s + 1), ZS + 256 * (s + 2))
         gather("S", zn, v("ZW", 0, ZS + 256 * (s + 1)), zo)
         if last:
@@ -560,21 +579,23 @@ def operations(g, core, T, topo, steps):
             for lh in range(16):
                 ts(w("CMP", lh, lh + 1, 0, 256 - 16 * lh), v("PR", 16 * lh, 256), 2049.0, Op.add, sub(sc, lh, lh + 1), Op.is_equal)
             cnt = v("pb6", 0, 256)
-            mms([(cnt, v("IDN"), v("OFFD"), True, False)])
             for lh in range(15):
-                mms([(v("pb6", 16 * lh + 16, 256), v("BLK"), w("CMP", lh, lh + 1, 16, 256 - 16 * lh), False, False)])
-            mms([(cnt, v("TRI"), v("CMP", 0, 16), False, True)])
+                mms([(v("pb6", 16 * lh + 16, 256), v("BL8"), w("CMP", lh, lh + 1, 16, 256 - 16 * lh), False, False)])
+            mms([(cnt, v("TR8"), v("CMP", 0, 16), False, True)])
             scan(v("CS"), v("RSM"), cnt, Op.mult, Op.max)
-            wn, wa, wb = L("wn", "LF"), L("wa", "LF"), L("wb", "LF")
-            tt(wn, v("CS", 15, 256, 16), pop, Op.is_lt)
-            tt(wa, wn, ad, Op.mult)
-            tt(wb, wa, dmp, Op.add)
-            lin(wo, wb, eng=PLAN["WO"])
+            if PLAN["WO"] == "T":
+                tt(wo, v("CS", 15, 256, 16), dmp, Op.min)
+            else:
+                tt(L("wb", "LF"), v("CS", 15, 256, 16), dmp, Op.min)
+                lin(wo, L("wb", "LF"), eng=PLAN["WO"])
             send(win, wo, "aw%d" % s)
             tag[0] = "sc"
 
             def scat(lst, src):
-                add("vector", lambda: [g.vector.tensor_copy(T.VT[:, 0:4352].indirect(ap(lst)), ap(src))], [lst, src], [v("VT")], 0.05 + SCA * 256 * CYC)
+                n = PLAN["SC"]
+                for c in range(0, 16, n):
+                    add("vector", lambda c=c: [g.vector.tensor_copy(T.VT[:, 0:4352].indirect(ap(sub(lst, c, c + n))), ap(sub(src, 16 * c, 16 * (c + n))))],
+                        [lst, src], [v("VT")], 0.05 + SCA * 16 * n * CYC)
             snd = len(ops) - 1
             scat(wo, z)
             ne = len(topo.engines(prv, core)[:8])
@@ -582,8 +603,8 @@ def operations(g, core, T, topo, steps):
             scat(win, zin)
     tag[0] = "out"
     dma("sync", T.yv[:], T.VT[:, 0:4096], [v("VT")], [], "ov", 8.0)
-    add("tensor", lambda: [g.tensor.matmul(T.pb1[0:8, lp:256:16], T.BSEL[:, lp * 128:lp * 128 + 128:16], ap(pn), True, True) for lp in range(16)],
-        [v("BSEL"), pn], [v("pb1", 0, 256)], 1.0)
+    quarters(v("PS4"), pn)
+    mms([(v("pb1", a, 256, 4, p=8), v("B4", 128 * a, 128 * a + 128, 16), v("PS4"), True, True) for a in range(4)])
     add("vector", lambda: [g.vector.tensor_scalar(T.YP[0:8, :], T.pb1[0:8, 0:256], -1.0, None, Op.add)], [v("pb1", 0, 256)], [v("YP")], 0.22)
     dma("sync", T.yp[:], T.YP[0:8, :], [v("YP")], [], "op", 2.5)
     mms([(CAN, v("IDN"), lv, True, False), (CAN, v("NEG"), v("RTB"), False, True)])
@@ -617,7 +638,7 @@ def dependences(ops):
                         need = not same or (k2 == "w" and not (o["q"] == "tensor" and SCRATCH[x[0]][0] == "psum"))
                         preds[i][j] = preds[i].get(j, False) or need
         if o["q"] == "tensor":
-            for b in set(o["banks"]) & {"pb2", "pb3", "pb4", "pb5", "pb6"}:
+            for b in set(o["banks"]) & {"pb2", "pb3", "pb5", "pb6"}:
                 if b in bank:
                     preds[i].setdefault(bank[b], False)
                 bank[b] = i

import math
from concourse.mybir import AluOpType as Op, AxisListType, ActivationFunctionType as Act

STEPS = 8
FL, ZS = 4096, 4352
LAT, CYC, GAT, GAV, SCA = 0.21, 0.00084, 1.56, 1.62, 3.8
PLAN = {"X": "VsVsVsVs", "SIGN": "VSVSVSVS", "V": "sVsVVVVV", "SMALL": "S", "Q": "V", "A": "V", "U": "V", "WO": "T", "SC": 16, "HO": "S", "TAIL": (512, 256, 256), "XO": "VVVV", "L4": "G", "FAR": ((0, 8), (0, 6, 8))}
FIRST = {"X": "VsVsVsVV", "SIGN": "VSVSVSVV"}
MORE = 2
ORDER, ROUNDS, POLISH, HEAT, SEED = {}, 11000, 60, 0.35, 21
WHEN = dict(x0=0, x1=0.1, x2=2, x3=0.2, gx0=1, gx1=1, gx3=1.1, ab0=2, ab1=3, bb1=3.1, gx2=2.5, ab2=6, ab3=6.1, bb3=6.2, vi0=4, vi1=7, bb0=8.5, bb2=11,
            row0=9, row1=11.5, pk0=13, pk1=13, vg0=8, vg1=8, vg2=9.5, vg3=10, far0=12, far1=15, sh=3, pl=16.5, mv=19, u=19.1, z=19.05, ln=23,
            dd=20.5, sc=23, out=40, nz=0, st=16, kk=16, cm=12.5, lv=28, hs=34)
_B = {
    "bfloat16": "XT 4128 VT 4352 ZW 6656 D 4096 BB 4096 EE 4096 AB 4096 ZIN 2048 Z4 1024 CAI 256 RTI 256 CAC 256 "
                "G1 256 FF 256 HIT 256 CR 256 B4 512 TRI 128 TR8 128 BL8 128 ONE 144 BLK 128 IDN 128 NEG 128 "
                "I64 128 N64 128 I2K 128 I4K 128 NBG 128 HLF 128 PRM 144 P4K 144 PBG 144 PAR 128 NPAR 128 SM 512 UPQ 256 OFFD 256 YLB 256 LB 1024 L4 256",
    "float16": "PR 256 NMF 256 NMT 256 SEL 256 THB 128 THC 256 WG 16 FR 256 CK 288 PS4 64 LH 64 RL0 256 RL1 256 KH 256 RSA 256",
    "uint16": "WIN 128 WO 128 XO 256 HO 256 ZO 32",
    "int32": "NMI 256 WTI 1 THI 1 K37 256 T1 256 T2 256 T3 256 QQ 256 V4 256 V5 256 WK 288 LI 1024",
    "float32": "KC 256 KS 256 CS 256 DC 128 TS 128 RS4 64 RS8 128 AL 288 RSM 256 IO3 256 IO4 256 LVT 256 YL 256 YP 256 LF 1024",
}
SCRATCH = {}
for _t in _B:
    _w = _B[_t].split()
    for _i in range(0, len(_w), 2):
        SCRATCH[_w[_i]] = ("sbuf", [128, int(_w[_i + 1])], _t)
for _n, _a, _b, _t in (("CMP", 16, 256, "bfloat16"), ("CAT", 8, 32, "bfloat16"), ("RTT", 8, 32, "bfloat16"), ("LV3", 16, 16, "bfloat16"), ("HD", 16, 8, "bfloat16"),
                       ("HC", 16, 8, "float32"), ("CM", 32, 9, "bfloat16"), ("CB", 32, 9, "float16"), ("CAB", 16, 16, "bfloat16"), ("RTB", 16, 16, "bfloat16")):
    SCRATCH[_n] = ("sbuf", [128, _a, _b], _t)
for _i in range(8):
    SCRATCH["pb%d" % _i] = ("psum", [128, 512], "float32")
LOADS = ["lnm", "lwt", "lca", "lx", "lxw", "lz", "lrt", "lth", "lv"]
OUTS = ["ov", "oz", "ol", "op"]
SEMAPHORES = ["sv", "ss", "st", "sg", "loc"] + LOADS + OUTS + ["az%d" % s for s in range(1, STEPS)] + ["aw%d" % s for s in range(1, STEPS)]
SEMAPHORES += [p + "%d_%d" % (s, q) for s in range(STEPS) for q in range(4) for p in "xn"]
DMA, NET = 3.0, 2.8
QSEM = {"vector": "sv", "scalar": "ss", "tensor": "st", "gpsimd": "sg"}
SIZE = {"bfloat16": 2, "float16": 2, "uint16": 2, "float32": 4, "int32": 4}


def rank_program(g, core, T, topo):
    rank = T.rank_of(core)
    if rank is None:
        return
    ops = operations(g, core, T, topo, STEPS)
    preds = dependences(ops)
    if not ORDER:
        short = operations(g, core, T, topo, 4)
        at = arrange(short, dependences(short), None, ROUNDS, MORE)[1]
        when = {(o["step"], o["tag"], o["nth"]): t for o, t in zip(short, at)}
        period = when[2, "u", 1] - when[1, "u", 1]
        like = [0, 1] + [2] * (STEPS - 3) + [3]
        key = [when[like[o["step"]], o["tag"], o["nth"]] + period * (o["step"] - like[o["step"]]) for o in ops]
        ORDER[0] = arrange(ops, preds, key, POLISH)
    emit(g, T, ops, preds, ORDER[0][1])
    g.wait_ge(T.sem.loc, 2 * (STEPS - 1) * len(topo.engines(core, T.cores[(rank + 1) % len(T.cores)])[:8]))


def operations(g, core, T, topo, steps):
    rank = T.rank_of(core)
    n = len(T.cores)
    nxt, prv = T.cores[(rank + 1) % n], T.cores[(rank - 1) % n]
    ops = []
    tag = ["init", 0]
    slots, used = {}, {"LF": 0, "LI": 0, "LB": 0, "LH": 0}

    def v(name, c0=0, c1=None, st=1, p=128):
        sh = SCRATCH[name][1]
        if len(sh) == 3:
            return (name, c0, sh[2] if c1 is None else c1, st, (0, sh[1], 1), p)
        return (name, c0, sh[1] if c1 is None else c1, st, None, p)

    def w(name, a0, a1, c0, c1, sa=1):
        return (name, c0, c1, 1, (a0, a1, sa), 128)

    def ap(x):
        if isinstance(x[5], tuple):
            return T[x[0]][x[5][0]:x[5][1], x[1]:x[2]:x[3]]
        if x[4] is None:
            return T[x[0]][0:x[5], x[1]:x[2]:x[3]]
        if x[2] - x[1] == 1:
            return T[x[0]][0:x[5], x[4][0]:x[4][1]:x[4][2], x[1]]
        if x[4][1] - x[4][0] == 1:
            return T[x[0]][0:x[5], x[4][0], x[1]:x[2]]
        return T[x[0]][0:x[5], x[4][0]:x[4][1]:x[4][2], x[1]:x[2]]

    def width(x):
        return (x[2] - x[1] + x[3] - 1) // x[3] * (1 if x[4] is None else (x[4][1] - x[4][0] + x[4][2] - 1) // x[4][2])

    def psum(x):
        return SCRATCH[x[0]][0] == "psum"

    def size(x):
        return SIZE[SCRATCH[x[0]][2]]

    def sub(x, a, b):
        return (x[0], x[1] + a, x[1] + b, 1, x[4], x[5])

    def lane(name, buf, wd=16):
        if name not in slots:
            slots[name] = v(buf, used[buf], used[buf] + wd)
            used[buf] += max(wd, 8)
        return slots[name]

    def add(q, fn, rd, wr, cost, done=None, pre=()):
        ops.append({"q": q, "fn": fn, "rd": list(rd), "wr": list(wr), "cost": cost, "done": done, "pre": list(pre), "tag": tag[0], "step": tag[1]})

    def part(name, i):
        tag[0] = name + str(i)

    def vcost(cyc):
        return max(64, cyc) * CYC

    def half(a, b):
        return 0.5 if size(a) == 2 and size(b) == 2 else 1

    def val(s):
        return ap(s) if isinstance(s, tuple) else s

    def tt(out, a, b, op):
        add("vector", lambda: [g.vector.tensor_tensor(ap(out), ap(a), ap(b), op)], [a, b], [out],
            vcost(width(out) * (1 if psum(a) or psum(b) else 2)))

    def ts(out, a, s1, op0, s2=None, op1=None):
        def fn():
            if op1 is None:
                return [g.vector.tensor_scalar(ap(out), ap(a), val(s1), None, op0)]
            return [g.vector.tensor_scalar(ap(out), ap(a), val(s1), val(s2), op0, op1)]
        add("vector", fn, [a] + [s for s in (s1, s2) if isinstance(s, tuple)], [out], vcost(width(out) * half(out, a)))

    def cp(out, a):
        add("vector", lambda: [g.vector.tensor_copy(ap(out), ap(a))], [a], [out], vcost(width(out) * half(out, a)))

    def fill(out, c):
        add("vector", lambda: [g.vector.memset(ap(out), c)], [], [out], vcost(width(out) * half(out, out)))

    def scan(out, d0, d1, op0, op1):
        add("vector", lambda: [g.vector.tensor_tensor_scan(ap(out), ap(d0), ap(d1), 0.0, op0, op1)], [d0, d1], [out],
            vcost(width(out) * max(half(out, d0), half(out, d1))))

    def turn(out, a):
        add("vector", lambda: [g.vector.transpose(ap(out), ap(a))], [a], [out], vcost(width(out)))

    def act(out, a, func, scale=1.0, bias=0.0):
        add("scalar", lambda: [g.scalar.activation(ap(out), ap(a), func, bias=val(bias), scale=scale)],
            [a] + ([bias] if isinstance(bias, tuple) else []), [out], max(64, width(out)) * CYC)

    def lin(out, a, scale=1.0, bias=0.0, eng=None):
        if eng == "G":
            asel(out, a, [[0, width(out)]], Op.is_ge, 0, 0)
        elif (eng or PLAN["SMALL"]) == "S":
            act(out, a, Act.Identity, scale, bias)
        else:
            ts(out, a, scale, Op.mult, bias, Op.add)

    def mms(lst):
        rd, wr, c = [], [], 0
        for o, l, r, a, b in lst:
            rd += [l, r]
            wr.append(o)
            c += max(min(64, width(l)), width(r))
        add("tensor", lambda: [g.tensor.matmul(ap(o), ap(l), ap(r), a, b) for o, l, r, a, b in lst], rd, wr, c * CYC)

    def iota(out, pattern, base, cm):
        if SCRATCH[out[0]][2] == "int32":
            fn = lambda: [g.iota(ap(out), pattern, base, cm)]
        else:
            fn = lambda: [g.iota(ap(out), pattern, base, cm, allow_small_or_imprecise_dtypes=True)]
        add("gpsimd", fn, [], [out], 0.13 + 2 * width(out) * CYC)

    def asel(out, a, pattern, cmp, base, cm):
        add("gpsimd", lambda: [g.affine_select(ap(out), ap(a), pattern, cmp, 0.0, base, cm)], [a], [out], 0.17 + 2 * width(out) * CYC)

    def dma(q, out, src, rd, wr, sem, cost):
        eng = g.sync if q == "sync" else g.scalar
        add(q, lambda: [eng.dma_start(out, src)], rd, wr, cost, done=(sem, 16))

    def gather(eng, out, win, lst, minus=None, scale=1.0):
        if eng == "V":
            add("vector", lambda: [g.vector.tensor_tensor(ap(out), ap(win).indirect(ap(lst)), ap(minus), Op.subtract)], [win, lst, minus], [out],
                0.05 + GAV * width(out) * CYC)
        else:
            add("scalar", lambda: [g.scalar.activation(ap(out), ap(win).indirect(ap(lst)), Act.Copy, scale=scale)], [win, lst], [out], 0.065 + GAT * width(out) * CYC)

    dma("scalar", T.NMI[:], T.nm[:], [], [v("NMI")], "lnm", 2.5)
    dma("scalar", T.ZW[:, ZS:ZS + 256], T.z0[:], [], [v("ZW", ZS, ZS + 256)], "lz", 2.5)
    dma("sync", T.WTI[:], T.wt[:], [], [v("WTI")], "lwt", 2.5)
    dma("sync", T.CAI[:], T.ca[:], [], [v("CAI")], "lca", 2.5)
    dma("sync", T.XT[:, 0:4096], T.xt[:], [], [v("XT", 0, 4096)], "lx", 6.0)
    ops[-1]["pre"] = [len(ops) - 3, len(ops) - 2]
    dma("scalar", T.XT[:, 4096:4128], T.xt[:, 0:32], [], [v("XT", 4096, 4128)], "lxw", 3.0)
    dma("scalar", T.RTI[:], T.rt[:], [], [v("RTI")], "lrt", 2.5)
    dma("scalar", T.THI[:], T.th[:], [], [v("THI")], "lth", 2.5)
    dma("sync", T.VT[:, 0:4096], T.vt[:], [v("XT", 0, 16)], [v("VT", 0, 4096)], "lv", 6.0)

    one, grp = v("ONE", 0, 128), v("BLK", 0, 128, 16)
    fill(v("ONE"), 1.0)
    fill(v("HLF"), -1.0 / 256)
    pI, lI = lane("pI", "LI"), lane("lI", "LI")
    asel(v("IDN"), one, [[-1, 128]], Op.is_equal, 0, 1)
    asel(v("BLK"), one, [[-16, 8], [0, 16]], Op.is_ge, 0, 1)
    asel(v("BLK"), v("BLK"), [[16, 8], [0, 16]], Op.is_ge, 15, -1)
    asel(v("UPQ", 0, 128), one, [[-1, 128]], Op.is_equal, -16, 1)
    asel(v("UPQ", 128, 256), one, [[-1, 128]], Op.is_equal, 16, 1)
    iota(v("PAR"), [[0, 4], [1, 2], [0, 16]], 0, 0)
    iota(v("K37"), [[37, 16], [0, 16]], 2048 - 8192, 0)
    iota(pI, [[0, 16]], 0, 1)
    iota(lI, [[16, 16]], 0, 0)
    iota(v("IO3"), [[0, 16], [1, 16]], 0, 0)
    iota(v("IO4"), [[1, 16], [0, 16]], 0, 0)
    iota(v("KC"), [[0, 16], [2, 16]], 1985, 0)
    asel(v("PRM"), v("ONE", 0, 144), [[-1, 16], [-16, 9]], Op.is_equal, 16, 1)
    asel(v("TRI"), v("BLK"), [[1, 128]], Op.is_ge, -1, -1)
    ts(v("NPAR"), v("PAR"), -1.0, Op.mult, 1.0, Op.add)

    def smx(gp, lhp):
        return v("SM", 128 * (2 * gp + lhp), 128 * (2 * gp + lhp) + 128)
    for gp in range(2):
        for lhp in range(2):
            src = v("IDN") if gp == lhp else v("UPQ", 0, 128) if lhp == 1 else v("UPQ", 128, 256)
            tt(smx(gp, lhp), src, v("PAR") if gp else v("NPAR"), Op.mult)
    wh, wf, wg = lane("wh", "LF", 1), lane("wf", "LF", 1), v("WG", 0, 8)
    ts(wh, v("WTI"), 2048.0, Op.is_ge, -4096.0, Op.mult)
    tt(wf, wh, v("WTI"), Op.add)
    ts(wg, grp, wf, Op.mult, 1.0 / 4096, Op.mult)
    for nm, c in (("I4K", 4096.0), ("NEG", -1.0), ("I64", 64.0), ("N64", -64.0), ("I2K", 2048.0), ("NBG", -8388608.0)):
        ts(v(nm), v("IDN"), c, Op.mult)
    ts(v("P4K"), v("PRM"), 4096.0, Op.mult)
    ts(v("PBG"), v("PRM"), -8388608.0, Op.mult)

    def residue(out, q, src):
        lin(q, src, 1.0, 1.0 / 8192, eng=PLAN["Q"])
        tt(out, src, q, Op.subtract)
    u4 = lane("u_0", "LI", 64)
    mms([(v("pb1", 0, 128, p=16), v("ONE", 0, 16), v("HLF"), True, False)] +
        [(v("pb1", lp, 128, 16, p=16), v("ZW", ZS + lp, ZS + 256, 16), wg, False, lp == 15) for lp in range(16)])
    residue(v("FR", 0, 128, p=16), v("QQ", 0, 128, p=16), v("pb1", 0, 128, p=16))
    mms([(v("pb1", 256 + 16 * i, 272 + 16 * i), v("FR", 0, 128, p=16), v("I4K", 0, 16, p=16), True, True) for i in range(4)])
    ts(u4, v("pb1", 256, 320), 2048.0, Op.add)

    NB, NK = v("pb7", 0, 256), v("pb7", 256, 512)
    ts(v("NMF"), v("NMI"), -2048.0, Op.add)
    for b in range(8):
        turn(v("NMT", b, 256, 8), v("NMF", 32 * b, 32 * b + 32))
    mms([(v("pb2", lhp, 256, 2), smx(gp, lhp), v("NMT", 128 * gp, 128 * gp + 128), gp == 0, gp == 1) for lhp in range(2) for gp in range(2)])
    tt(v("T3"), v("pb2", 0, 256), v("K37"), Op.add)
    ts(NB, v("pb2", 0, 256), 2048.0, Op.add)
    ts(NK, v("T3"), 32.0, Op.mult)
    CAN = v("pb0", 256, 512)
    for src, tr, bk, to in (("RTI", "RTT", "pb5", "RTB"), ("CAI", "CAT", "pb6", "CAB")):
        turn(v(tr), v(src))
        mms([(v(bk, 128 * lhp, 128 * lhp + 128), smx(gp, lhp), v(tr, 16 * gp, 16 * gp + 16), gp == 0, gp == 1) for lhp in range(2) for gp in range(2)])
        for lhp in range(2):
            act(w(to, lhp, 16, 0, 16, 2), v(bk, 128 * lhp, 128 * lhp + 128), Act.Copy)
    mms([(CAN, v("IDN"), v("CAB"), True, True)])
    tt(v("CR"), CAN, v("RTB"), Op.add)
    cp(v("RL0"), v("RTB"))
    ts(v("CAC"), v("CAB"), -1.0, Op.mult, 31.0, Op.add)
    ts(v("KS"), v("CAB"), -64.0, Op.mult)
    fill(v("CB", 0, 1), 4096.0)
    fill(v("CM", 0, 1), 0.0)
    tt(v("CB", 1, 9), v("KS"), v("KC"), Op.add)
    for h in range(2):
        act(v("CK", h, 288, 2), w("CB", h, 32, 0, 9, 2), Act.Copy)
    fill(v("AL"), 8388608.0)
    pm, lc, dmp = lane("pm", "LI"), lane("lc", "LI"), lane("dmp", "LF")
    pf, thf = lane("pf", "LF", 1), lane("thf", "LF", 1)
    ts(pm, pI, 15, Op.bitwise_and)
    tt(lc, pm, lI, Op.add)
    ts(dmp, lc, 4096.0, Op.add)
    cp(pf, sub(pm, 0, 1))
    cp(thf, v("THI"))
    lo, up, mlo, mup = lane("lo", "LI", 1), lane("up", "LI", 1), lane("mlo", "LF", 4), lane("mup", "LF", 4)
    ts(lo, sub(pm, 0, 1), 3, Op.bitwise_and)
    ts(up, sub(pm, 0, 1), 2, Op.arith_shift_right)
    for a in range(4):
        ts(sub(mlo, a, a + 1), lo, float(a), Op.is_equal)
        ts(sub(mup, a, a + 1), up, float(a), Op.is_equal)
        ts(v("B4", 128 * a, 128 * a + 128), v("BLK"), sub(mlo, a, a + 1), Op.mult)

    def quarters(out, x):
        for j in range(4):
            o, c = (out[0], j, 64, 4, None, 128), sub(mup, j, j + 1)
            add("scalar", lambda o=o, c=c: [g.scalar.activation(ap(o), ap(x), Act.Copy, scale=ap(c))], [x, c], [o], 64 * CYC)
    ts(v("SEL"), v("IO4"), pf, Op.is_equal)
    ts(v("THB"), v("BLK"), thf, Op.mult)
    mms([(v("pb4", 128 * h, 128 * h + 128), v("SEL", 128 * h, 128 * h + 128), v("THB"), True, True) for h in range(2)])
    act(v("THC"), v("pb4", 0, 256), Act.Copy)
    ts(v("CS"), v("IO3"), pf, Op.not_equal, -4194304.0 - 10240, Op.mult)
    ts(v("OFFD"), v("CS"), 10240.0, Op.add)
    tt(v("UPQ", 0, 128), v("TRI"), v("IDN"), Op.subtract)
    ts(v("TR8"), v("UPQ", 0, 128), 8192.0, Op.mult)
    ts(v("BL8"), v("BLK"), 8192.0, Op.mult)
    ts(v("RSM"), v("IO3"), 0.0, Op.is_gt)
    ts(v("RSA"), v("RSM"), -1001.0, Op.mult, 1000.0, Op.add)
    for ne in (4, 8):
        fill(v("RS%d" % ne), 1.0)
        fill(v("RS%d" % ne, 0, 16 * ne, ne), 0.0)
    wq, si, si2, s63 = lane("wq", "LH", 2), lane("si", "LI", 1), lane("si2", "LI", 1), lane("s63", "LF", 1)
    cp(sub(wq, 0, 1), wf)
    mms([(v("pb3", 0, 1), v("BLK"), sub(wq, 0, 1), True, True)])
    ts(si, v("pb3", 0, 1), 63.0, Op.mult)
    ts(si2, si, 4095, Op.bitwise_and)
    cp(s63, si2)
    L3 = lane("L3", "LB", 64)
    tau, dl, pn, f = [sub(L3, 16 * i, 16 * i + 16) for i in range(4)]
    tau4, dl4, pn4, f4 = [v("L4", 64 * i, 64 * i + 64) for i in range(4)]
    fill(f, 0.5)
    fill(f4, 0.5)
    fill(v("HD"), 0.0)
    fill(v("HD", 0, 1), 0.5)
    fill(v("HC"), 0.0)
    popc = sub(lane("pop", "LB", 24), 0, 17)
    fill(sub(popc, 16, 17), -15.75 / 128)
    A = ct = None
    flip = [0]

    def minus(src, a, b, other):
        flip[0] ^= 1
        bank = "pb3" if flip[0] else "pb2"
        mms([(v(bank, 0, b - a), v("NEG"), other, True, False)])
        mms([(v(bank, 0, b - a), v("IDN"), v(src, a, b), False, True)])
        return v(bank, 0, b - a)

    def sums(out, src, h, rhs, first=None, cuts=(0, 8)):
        lst = [(out, first[0], first[1], True, False)] if first else []
        for k0, k1 in zip(cuts, cuts[1:]):
            mms(lst + [((out[0], out[1] + lp, out[2], 16, None, (16 * k0, 16 * k1)), v(src, 2048 * h + 256 * k0 + lp, 2048 * h + 256 * k1, 16), rhs,
                        not first, not first or lp == 15) for lp in range(16)])
            lst = []

    for s in range(steps):
        par, nxp, last = "_%d" % (s % 2), "_%d" % ((s + 1) % 2), s == steps - 1

        def L(name, buf, wd=16):
            return lane(name, buf, wd)
        u = lane("u" + par, "LI", 64)
        u1 = sub(u, 0, 16)
        z = v("ZW", ZS + 256 * s, ZS + 256 * s + 256)
        tag[:] = ["x0", s]
        if s:
            en = topo.engines(core, nxt)[:8]
            rid, pid = topo.addr(nxt)[:2]

            def send(dst, src, sem, mask=sum(1 << e for e in en), rid=rid, pid=pid):
                def fn():
                    g.remote_dma(out_ap=ap(dst), in_ap=ap(src), remote_sem=T.sem[sem], local_sem=T.sem.loc, pid=pid, routing_id=rid, dma_engine_mask=mask)
                    return []
                add("gpsimd", fn, [src], [], 0.5, done=("none", 0))
            zin, win, wo = v("ZIN", 256 * s, 256 * s + 256), v("WIN", 16 * s, 16 * s + 16), v("WO", 16 * s, 16 * s + 16)
            send(zin, z, "az%d" % s)
        for q in range(4):
            part("x", q)
            c0, c1 = 64 * q, 64 * q + 64
            t1, t2, t3, xo = v("T1", c0, c1), v("T2", c0, c1), v("T3", c0, c1), v("XO", c0, c1)
            tt(t1, sub(NB, c0, c1), u, Op.mult)
            tt(t2, sub(NK, c0, c1), t1, Op.add)
            ts(t3, t2, 5, Op.arith_shift_right, 4095, Op.bitwise_and)
            if A is None:
                lin(xo, t3, eng=PLAN["XO"][q])
            elif PLAN["XO"][q] == "V":
                ts(xo, t3, ct, Op.add, A, Op.subtract)
            else:
                if PLAN["XO"][:q].count("S") == 0:
                    act(L("A1", "LF", 1), A, Act.Identity, scale=-1.0, bias=ct)
                lin(xo, t3, 1.0, L("A1", "LF", 1))
        tag[0] = "sh"
        dd, d2, d3, dp, dt = L("dd", "LB"), L("d2", "LB"), L("d3", "LB"), L("dp", "LF"), L("dt", "LF", 64)
        act(dd, f, Act.Identity, bias=-0.5)
        act(d2, f, Act.Identity, scale=2.0)
        act(dp, f, Act.Sign, bias=-0.5)
        for a, b, src in ((0, 16, f), (16, 32, f)):
            act(sub(dt, a, b), src, Act.Identity, scale=19616.0, bias=9808.0 + 42752)
        act(sub(dt, 32, 64), sub(dt, 0, 32), Act.Copy)
        tag[0] = "st"
        fa, fb = L("fa", "LI"), L("fb", "LI")
        lin(fa, u1, -1.0, s63)
        ts(fb, fa, 4095, Op.bitwise_and)
        tc, tf, tca, pt = L("tc", "LI"), L("tf", "LF"), L("tca", "LF"), L("pt", "LB")
        if s:
            ne = 4 if s < steps // 2 else 8
            lin(v("HC", 0, 1), fb)
            dr = v("pb6", 256, 256 + 16 * ne)
            mms([(v("pb6", 256 + e, 256 + 16 * ne, ne // 4), v("IDN"), f4, True, True) for e in range(ne // 4)])
            tt(dr, v("HD", 0, ne), dr, Op.is_equal)
            tt(v("DC", 0, 16 * ne), dr, v("HC", 0, ne), Op.mult)
            scan(v("TS", 0, 16 * ne), v("RS%d" % ne), v("DC", 0, 16 * ne), Op.mult, Op.max)
            top = v("TS", ne - 1, 16 * ne, ne)
            lin(tc, top)
            tt(tf, top, tc, Op.subtract)
            act(tca, tf, Act.Identity, scale=64.0)
            act(pt, tf, Act.Identity, scale=-64.0, bias=32.0)
        else:
            tc = fb
            fill(tca, 0.0)
            fill(pt, 0.0)
        tag[0] = "cm"
        act(v("CM", 1, 9), CAN, Act.Relu, scale=-1.0)
        tag[0] = "kk"
        scan(v("KH"), v("RSA"), v("RL%d" % (s % 2)), Op.max, Op.min)
        kk, kth, kp = L("kk", "LF"), L("kth", "LF"), L("kp", "LF")
        act(kk, v("KH", 15, 256, 16), Act.Identity, scale=-131072.0, bias=31.0 * 131072 + 65536)
        act(kth, v("KH", 15, 256, 16), Act.Identity, scale=-131072.0, bias=32.0 * 131072)
        tt(kp, kth, dp, Op.mult)
        tt(v("AL", 2, 288, 18), tc, kk, Op.add)
        act(v("ZW", FL, FL + 256), z, Act.Identity, scale=-1.0, bias=63.0)
        tag[0] = "pl"
        if s:
            pb, pc, pd, pe = L("pb", "LF"), L("pc", "LF"), L("pd", "LI"), L("pe", "LI")
            ps = L("ps", "LH")
            if PLAN["SMALL"] == "S":
                act(pb, u1, Act.Square, bias=592.0)
            else:
                ts(pc, u1, 592.0, Op.add)
                tt(pb, pc, pc, Op.mult)
            act(pc, f, Act.Identity, scale=19616.0, bias=42752.0 - 9808)
            tt(pd, pb, pc, Op.add)
            ts(pe, pd, 5, Op.arith_shift_right, 4095, Op.bitwise_and)
            lin(ps, pe, 1.0, -2048.0)
            p1 = L("p1", "LF")
            lin(p1, pe, 1.0, 1.0, eng=PLAN["Q"])
            quarters(v("PS4"), ps)
            mms([(v("pb6", 256 + a, 512, 4), v("B4", 128 * a, 128 * a + 128), v("PS4"), True, True) for a in range(4)])
            lin(v("PR"), v("pb6", 256, 512))
            mms([(v("pb6", 0, 256), v("IDN"), v("OFFD"), True, False)] + [(v("pb6", i, 256, 4), v("IDN"), v("PS4"), False, False) for i in range(4)])
            ops[-1]["rd"].append(v("PR"))
        keys = []
        tag[0] = "nz"
        z2 = v("ZW", ZS + 256 * s, ZS + 256 * s + 512)
        asel(sub(z2, 256, 512), z, [[0, 256]], Op.is_ge, 0, 0)
        if set(PLAN["X"]) & set("DW"):
            tag[0] = "nz"
            for i in range(4):
                dma("sync", T.Z4[:, 256 * i:256 * i + 256], ap(z), [z], [v("Z4", 256 * i, 256 * i + 256)], "n%d_%d" % (s, i), 2.5)
        for h in range(2):
            for q in (2 * h, 2 * h + 1):
                a, b = 1024 * q, 1024 * q + 1024
                part("gx", q)
                who = (PLAN if s else FIRST)["X"][2 * q:2 * q + 2]
                if who == "SS":
                    gather("S", v("D", a, b), v("XT"), v("XO", 64 * q, 64 * q + 64))
                if who == "DD":
                    gather("S", v("D", a, b), v("XT"), v("XO", 64 * q, 64 * q + 64), scale=-1.0)
                    add("gpsimd", lambda a=a, b=b: [g.dma_start(T.D[:, a:b], T.Z4[:], accum_op=Op.add)], [v("Z4"), v("D", a, b)], [v("D", a, b)], DMA,
                        done=("x%d_%d" % (s, q), 16))
                if who == "WW":
                    gather("V", v("D", a, b), v("XT"), v("XO", 64 * q, 64 * q + 64), v("Z4"))
                for i, a1 in enumerate((a, a + 512)):
                    b1 = a1 + 512
                    part("gx", q)
                    if who[i] in "DW":
                        d = v("D", a1, b1)
                    elif who[i] == "V":
                        d = v("D", a1, b1)
                        gather("V", d, v("XT"), v("XO", a1 // 16, b1 // 16), z2)
                    else:
                        if who != "SS":
                            gather("S", v("D", a1, b1), v("XT"), v("XO", a1 // 16, b1 // 16))
                        d = minus("D", a1, b1, z2)
                    part("ab", q)
                    act(v("ZW", a1, b1), d, Act.Abs)
                    part("bb", q)
                    if (PLAN if s else FIRST)["SIGN"][2 * q + i] in "Ss":
                        act(v("BB", a1, b1), d, Act.Sign, bias=0.5, scale=-1.0 if who[i] == "D" else 1.0)
                    else:
                        ts(v("BB", a1, b1), d, 0.0, Op.is_le if who[i] == "D" else Op.is_ge, -0.5, Op.add)
            c0, c1 = 128 * h, 128 * h + 128
            part("vi", h)
            bk = ("pb1", "pb4")[h]
            uc, ub, rw, fr = v(bk, 0, 128), v(bk, 128, 256), v(bk, 256, 384), v("FR", c0, c1)
            sums(uc, "ZW", h, wg, (one, v("HLF")))
            residue(fr, v("QQ", c0, c1), uc)
            mms([(ub, fr, v("I4K"), True, True)])
            act(ub, ub, Act.Square, bias=2640.0)
            for c in (0, 64):
                tt(v("V4", c0 + c, c0 + c + 64), sub(ub, c, c + 64), dt, Op.add)
            ts(v("V5", c0, c1), v("V4", c0, c1), 5, Op.arith_shift_right, 4095, Op.bitwise_and)
            lin(v("HO", c0, c1), v("V5", c0, c1), eng=PLAN["HO"])
            part("row", h)
            sums(rw, "BB", h, grp)
            act(v("G1", c0, c1), rw, Act.Relu, scale=-1.0)
            part("pk", h)
            key = v("pb5", h, 288, 2)
            keys.append(key)
            mms(([] if h else [(v("pb5", 0, 288), v("I2K"), v("CK"), True, False)]) + [(key, fr, v("P4K"), False, False)])
            mms([(key, v("G1", c0, c1), v("PBG"), False, False)])
        for h in range(2):
            for q in (2 * h, 2 * h + 1):
                a = 1024 * q
                part("vg", q)
                who = PLAN["V"][2 * q:2 * q + 2]
                if who == "SS":
                    gather("S", v("EE", a, a + 1024), v("VT", 0, 4096), v("HO", 64 * q, 64 * q + 64))
                for i, wd in enumerate((1024,) if who == "VV" and q < 3 else PLAN["TAIL"] if who == "VV" else (512, 512)):
                    b = a + wd
                    if who == "VV" or who[i] in "Vv":
                        e = v("EE", a, b)
                        gather("V", e, v("VT", 0, 4096), v("HO", a // 16, b // 16), v("ZW", a, b))
                    else:
                        if who != "SS":
                            gather("S", v("EE", a, b), v("VT", 0, 4096), v("HO", a // 16, b // 16))
                        e = minus("EE", a, b, v("ZW", a, b))
                    act(v("AB", a, b), e, Act.Abs)
                    a = b
            part("far", h)
            c0, c1 = 128 * h, 128 * h + 128
            fc = v(("pb1", "pb4")[h], 384, 512)
            sums(fc, "AB", h, grp, None, PLAN["FAR"][h])
            tt(v("FF", c0, c1), fc, v("THC", c0, c1), Op.is_le)
            key = keys[h]
            mms([(key, v("NBG"), w("CM", h, 32, 0, 9, 2), False, False)])
            mms([(key, v("FF", c0, c1), v("PBG"), False, h == 1)])
        scan(v("WK"), v("AL"), v("pb5", 0, 288), Op.min, Op.max)
        W = v("WK", 17, 288, 18)
        tag[0] = "mv"
        pop, m = sub(popc, 0, 16), L("m", "LB")
        tt(pop, W, kp, Op.is_lt)
        if s and not last:
            cn, ct, cm, A = v("pb1", 0, 17), L("ct", "LF", 1), L("cm", "LF", 1), L("A", "LF", 1)
            mms([(cn, one, popc, True, True)])
            for out, src in ((cm, cn), (ct, sub(cn, 0, 16))):
                add("vector", lambda out=out, src=src: [g.vector.tensor_reduce(ap(out), ap(src), AxisListType.X, Op.add)], [src], [out], 64 * CYC)
            ts(A, cm, 402653184.0, Op.add, -402653184.0, Op.add)
        tag[0] = "u"
        if not last:
            un = lane("u" + nxp, "LI", 64)
            for i in range(4 if PLAN["U"] == "V" else 2):
                ts(sub(un, 16 * i, 16 * i + 16), W, 4095, Op.bitwise_and)
            if PLAN["U"] != "V":
                lin(sub(un, 32, 64), sub(un, 0, 32))
        tag[0] = "z"
        za, zb, zo = L("za", "LI"), L("zb", "LI"), v("ZO", 16 * (s % 2), 16 * (s % 2) + 16)
        ts(za, W, 4, Op.arith_shift_right, 0x1F00, Op.bitwise_and)
        if PLAN["WO"] == "T":
            tt(zo, za, lc, Op.add)
        else:
            tt(zb, za, lc, Op.add)
            lin(zo, zb)
        zn = v("ZW", ZS + 256 * (s + 1), ZS + 256 * (s + 2))
        gather("S", zn, v("ZW", 0, ZS + 256 * (s + 1)), zo)
        if last:
            dma("scalar", T.yz[:], ap(zn), [zn], [], "oz", 2.5)
        tag[0] = "ln"
        hi, y1, y2, y3 = L("hi", "LI"), L("y1", "LF"), L("y2", "LF"), L("y3", "LB")
        tt(m, W, kth, Op.is_ge)
        ts(hi, W, 17, Op.arith_shift_right)
        tt(y1, hi, tca, Op.subtract)
        tt(y2, y1, m, Op.mult)
        tt(tau, y2, tca, Op.add)
        tt(y3, m, d2, Op.mult)
        tt(dl, y3, dd, Op.subtract)
        tt(pn, pop, pt, Op.mult)
        act(f, dl, Act.Abs, bias=0.5)
        for i in range(4):
            if PLAN["L4"] == "S":
                act(v("L4", i, 256, 4), L3, Act.Copy)
            else:
                asel(v("L4", i, 256, 4), L3, [[0, 64]], Op.is_ge, 0, 0)
        tag[0] = "lv"
        tp, dlp = v("pb0", 256, 512), v("pb0", 0, 256)
        mms([(v("pb0", 256 + i, 512, 4), v("IDN"), tau4, True, True) for i in range(4)] + [(v("pb0", i, 256, 4), v("I64"), dl4, True, True) for i in range(4)])
        lv = v("RL%d" % ((s + 1) % 2))
        tt(v("HIT"), v("CAC"), tp, Op.is_equal)
        tt(dlp, v("HIT"), dlp, Op.mult)
        tt(lv, v("RL%d" % (s % 2)), dlp, Op.add)
        if not last:
            mms([(CAN, v("IDN"), v("CR"), True, False), (CAN, v("NEG"), lv, False, False)] +
                [(v("pb0", 256 + i, 512, 4), v("NEG"), pn4, False, i == 3) for i in range(4)])
            tag[0] = "hs"
            ca_ = L("ca_", "LF")
            tt(v("HD", s + 1, s + 2), m, f, Op.mult)
            lin(ca_, hi, 1.0 / 64, (s + 1) * 4096.0)
            tt(v("HC", s + 1, s + 2), ca_, u1, Op.add)
        tag[0] = "dd"
        if s:
            sc = L("sc", "LF")
            tt(sc, pop, p1, Op.mult)
            for lh in range(16):
                ts(w("CMP", lh, lh + 1, 0, 256 - 16 * lh), v("PR", 16 * lh, 256), 2049.0, Op.add, sub(sc, lh, lh + 1), Op.is_equal)
            cnt = v("pb6", 0, 256)
            for lh in range(15):
                mms([(v("pb6", 16 * lh + 16, 256), v("BL8"), w("CMP", lh, lh + 1, 16, 256 - 16 * lh), False, False)])
            mms([(cnt, v("TR8"), v("CMP", 0, 16), False, True)])
            scan(v("CS"), v("RSM"), cnt, Op.mult, Op.max)
            if PLAN["WO"] == "T":
                tt(wo, v("CS", 15, 256, 16), dmp, Op.min)
            else:
                tt(L("wb", "LF"), v("CS", 15, 256, 16), dmp, Op.min)
                lin(wo, L("wb", "LF"), eng=PLAN["WO"])
            send(win, wo, "aw%d" % s)
            tag[0] = "sc"

            def scat(lst, src):
                n = PLAN["SC"]
                for c in range(0, 16, n):
                    add("vector", lambda c=c: [g.vector.tensor_copy(T.VT[:, 0:4352].indirect(ap(sub(lst, c, c + n))), ap(sub(src, 16 * c, 16 * (c + n))))],
                        [lst, src], [v("VT")], 0.05 + SCA * 16 * n * CYC)
            snd = len(ops) - 1
            scat(wo, z)
            ne = len(topo.engines(prv, core)[:8])
            add("net", None, [], [win, zin], NET, [("az%d" % s, ne), ("aw%d" % s, ne)], [snd])
            scat(win, zin)
    tag[0] = "out"
    dma("sync", T.yv[:], T.VT[:, 0:4096], [v("VT")], [], "ov", 8.0)
    quarters(v("PS4"), pn)
    mms([(v("pb1", a, 256, 4, p=8), v("B4", 128 * a, 128 * a + 128, 16), v("PS4"), True, True) for a in range(4)])
    add("vector", lambda: [g.vector.tensor_scalar(T.YP[0:8, :], T.pb1[0:8, 0:256], -1.0, None, Op.add)], [v("pb1", 0, 256)], [v("YP")], 0.22)
    dma("sync", T.yp[:], T.YP[0:8, :], [v("YP")], [], "op", 2.5)
    mms([(CAN, v("IDN"), lv, True, False), (CAN, v("NEG"), v("RTB"), False, True)])
    act(v("LV3"), CAN, Act.Copy, scale=1.0 / 64)
    mms([(v("pb0", 128 * gp, 128 * gp + 128), smx(lhp, gp), w("LV3", lhp, 16, 0, 16, 2), lhp == 0, lhp == 1) for gp in range(2) for lhp in range(2)])
    for gp in range(2):
        act(v("CAT", 16 * gp, 16 * gp + 16), v("pb0", 128 * gp, 128 * gp + 128), Act.Copy)
    turn(v("YLB"), v("CAT"))
    dma("scalar", T.yl[:], T.YLB[:], [v("YLB")], [], "ol", 2.5)
    nth = {}
    for o in ops:
        k = (o["step"], o["tag"])
        o["nth"] = nth[k] = nth.get(k, 0) + 1
    return ops


def dependences(ops):
    N = len(ops)
    preds = [dict() for _ in range(N)]
    hist, bank = {}, {}
    for i, o in enumerate(ops):
        for p in o["pre"]:
            preds[i][p] = o["q"] not in ("net", "sync")
        o["banks"] = sorted(set(x[0][:3] for x in o["rd"] + o["wr"] if SCRATCH[x[0]][0] == "psum"))
        for kind, regs in (("r", o["rd"]), ("w", o["wr"])):
            for x in regs:
                a0, a1 = x[4][:2] if x[4] else (0, 1)
                for (j, k2, b0, b1, e0, e1, st) in hist.get(x[0], ()):
                    if j != i and (st != x[3] or (b0 - x[1]) % st == 0) and b0 < x[2] and x[1] < b1 and e0 < a1 and a0 < e1 and (kind == "w" or k2 == "w"):
                        same = ops[j]["q"] == o["q"] and not ops[j]["done"]
                        need = not same or (k2 == "w" and not (o["q"] == "tensor" and SCRATCH[x[0]][0] == "psum"))
                        preds[i][j] = preds[i].get(j, False) or need
        if o["q"] == "tensor":
            for b in set(o["banks"]) & {"pb2", "pb3", "pb5", "pb6"}:
                if b in bank:
                    preds[i].setdefault(bank[b], False)
                bank[b] = i
        for kind, regs in (("r", o["rd"]), ("w", o["wr"])):
            for x in regs:
                a0, a1, sa = x[4] or (0, 1, 1)
                h = hist.setdefault(x[0], [])
                if kind == "w" and x[3] == 1 and sa == 1 and x[5] == 128:
                    h[:] = [y for y in h if not (x[1] <= y[2] and y[3] <= x[2] and a0 <= y[4] and y[5] <= a1 and y[0] != i)]
                h.append((i, kind, x[1], x[2], a0, a1, x[3]))
    return preds


def arrange(ops, preds, key, rounds, more=0):
    N = len(ops)
    occ = [0.0 if o["q"] == "net" else (1.0 if o["q"] == "gpsimd" else 0.1) if o["done"] and o["done"][1] else o["cost"] for o in ops]
    fw = [[(j, ops[j]["cost"] + LAT if c or ops[j]["q"] != ops[i]["q"] else occ[j]) for j, c in preds[i].items()] for i in range(N)]
    bw = [[] for _ in range(N)]
    for i in range(N):
        for j, dly in fw[i]:
            bw[j].append((i, dly + occ[i] - occ[j]))

    lines = [[(o["q"], 0.0)] + [(b + e, LAT) for b in o["banks"] for e in ("vector", "scalar", "tensor") if e != o["q"]] for o in ops]
    holds = [[o["q"]] + [b + o["q"] for b in o["banks"]] for o in ops]
    every = set(r for l in lines for r, _ in l) | set(r for l in holds for r in l)

    def place(edges, key):
        at, busy = [-1.0] * N, {r: [(-9.0, -9.0)] for r in every}
        stack = sorted(range(N), key=key.get, reverse=True)
        while stack:
            i = stack.pop()
            if at[i] >= 0:
                continue
            t, late = 0.0, []
            for j, dly in edges[i]:
                a = at[j]
                if a < 0:
                    late.append(j)
                elif a + dly > t:
                    t = a + dly
            if late:
                stack.append(i)
                stack += sorted(late, key=key.get, reverse=True)
                continue
            d = occ[i]
            moved = d > 0
            while moved:
                moved = False
                for r, pad in lines[i]:
                    lst = busy[r]
                    c = len(lst) - 1
                    if lst[c][1] + pad > t + 1e-9:
                        while lst[c - 1][1] + pad > t + 1e-9:
                            c -= 1
                        for a, b in lst[c:]:
                            if a >= t + d + pad - 1e-9:
                                break
                            t, moved = b + pad, True
            for r in holds[i]:
                lst = busy[r]
                c = len(lst)
                while lst[c - 1][1] > t + 1e-9:
                    c -= 1
                lst.insert(c, (t, t + d))
            at[i] = t
        return at

    prio = [0.0] * N
    for i in range(N - 1, -1, -1):
        prio[i] = max([prio[x] + dly + occ[i] - occ[x] for x, dly in bw[i]] + [ops[i]["cost"]])
    top = max(prio)
    key = key or [20.0 * o["step"] + WHEN[o["tag"]] if o["tag"] in WHEN else top - 12 - prio[i] for i, o in enumerate(ops)]
    twins = {}
    for i, o in enumerate(ops):
        twins.setdefault((o["tag"], o["nth"]), []).append(i)
    names, seed, cur, best, marks = list(twins), [SEED], None, None, twins["u", 1]

    def blocked(at):
        ends = {}
        for i in range(N):
            for r in holds[i]:
                ends[r, round(at[i] + occ[i], 4)] = i
        i, out = max(range(N), key=lambda x: at[x] + ops[x]["cost"]), []
        while at[i] > 1e-6:
            j = next((j for j, dly in fw[i] if abs(at[j] + dly - at[i]) < 1e-6), None)
            if j is None:
                j = next((ends[r, round(at[i] - pad, 4)] for r, pad in lines[i] if (r, round(at[i] - pad, 4)) in ends), None)
                if j is None or j == i:
                    break
                out.append((i, j))
            i = j
        return out

    def rnd():
        seed[0] = (seed[0] * 1103515245 + 12345) % 2147483648
        return seed[0] / 2147483648.0
    for n in range(rounds + 1):
        at = place(fw, {i: k + 1e-7 * i for i, k in enumerate(key)})
        span = max(at[i] + ops[i]["cost"] for i in range(N)) + more * (at[marks[2]] - at[marks[1]])
        if cur is None or span <= cur[0] - HEAT * (1.001 - n / rounds) * math.log(rnd() + 1e-9):
            cur = (span, at)
            best = cur if best is None or span < best[0] else best
            swaps = blocked(at)
        key = list(cur[1])
        if swaps and rnd() < 0.5:
            i, j = swaps[int(rnd() * len(swaps))]
            shift = key[i] - key[j] + 0.01
            move, sign = (i, -1) if rnd() < 0.6 else (j, 1)
            for x in twins[ops[move]["tag"], ops[move]["nth"]]:
                key[x] += sign * shift
            continue
        if rnd() < 0.15:
            back = place(bw, {i: -k - occ[i] - 1e-7 * i for i, k in enumerate(key)})
            key = [-back[i] - occ[i] for i in range(N)]
            continue
        if rnd() < 0.2:
            name, shift = names[int(rnd() * len(names))][0], (rnd() + rnd() - 1) * 8
            for i, o in enumerate(ops):
                if o["tag"] == name:
                    key[i] += shift
            continue
        for _ in range(1 << int(4 * rnd())):
            name, k = names[int(rnd() * len(names))]
            shift = (rnd() + rnd() - 1) * (0.7, 2.5, 7.0)[int(3 * rnd())]
            for j in range((1, 1, 2, 4)[int(4 * rnd())]):
                for i in twins.get((name, k + j), ()):
                    key[i] += shift
    return best + (top,)


def emit(g, T, ops, preds, at):
    N = len(ops)
    queues = {"vector": g.vector, "scalar": g.scalar, "tensor": g.tensor, "gpsimd": g, "sync": g.sync}
    seq, users = sorted(range(N), key=lambda i: (at[i], i)), {}
    for i in seq:
        for b in ops[i]["banks"]:
            for q, j in users.setdefault(b, {}).items():
                if q != ops[i]["q"]:
                    preds[i][j] = True
            users[b][ops[i]["q"]] = i
    count = {q: 0 for q in QSEM}
    known, fin = {}, [None] * N
    for i in seq:
        o = ops[i]
        q = o["q"]
        if q == "net":
            fin[i] = (list(o["done"]), {})
            continue
        kq = known.setdefault(q, {})
        pj = [j for j, c in preds[i].items() if c]
        need = {}
        for j in pj:
            for sem, val in fin[j][0]:
                if sem != "none" and kq.get(sem, 0) < val:
                    need[sem] = max(need.get(sem, 0), val)
        for j in pj:
            for sem, val in fin[j][1].items():
                if sem in need and need[sem] <= val and sem not in [x[0] for x in fin[j][0]]:
                    del need[sem]
        for sem, val in sorted(need.items()):
            queues[q].wait_ge(T.sem[sem], val)
            kq[sem] = max(kq.get(sem, 0), val)
        for j in pj:
            for sem, val in list(fin[j][1].items()) + fin[j][0]:
                kq[sem] = max(kq.get(sem, 0), val)
        ins = o["fn"]()
        if o["done"]:
            sem, val = o["done"]
            for x in ins:
                x.then_inc(T.sem[sem], val)
            fin[i] = ([(sem, val)], dict(kq))
        else:
            for x in ins:
                x.then_inc(T.sem[QSEM[q]], 1)
            count[q] += len(ins)
            fin[i] = ([(QSEM[q], count[q])], dict(kq))
    for q in QSEM:
        if count[q]:
            g.wait_ge(T.sem[QSEM[q]], count[q])
    for sem in LOADS + OUTS:
        g.wait_ge(T.sem[sem], 16)
